import numpy as np
import ml_dtypes


def mxq(x, axis, fmt="e4m3"):
    dtype, down = {"e4m3": (ml_dtypes.float8_e4m3fn, 7), "e5m2": (ml_dtypes.float8_e5m2, 14)}[fmt]
    v = np.moveaxis(np.asarray(x, np.float32).astype(ml_dtypes.bfloat16).astype(np.float64), axis, -1)
    blocks = v.reshape(v.shape[:-1] + (-1, 32))
    amax = np.abs(blocks).max(-1, keepdims=True)
    byte = np.maximum(np.where(amax > 0, np.frexp(amax)[1] - 1 + 127, 0) - down, 1)
    scale = np.exp2(byte - 127.0)
    codes = (blocks / scale).astype(np.float32).astype(dtype).astype(np.float64)
    return np.moveaxis((codes * scale).reshape(v.shape), -1, axis)


WIDE = False


def mx_kscale(k):
    if not WIDE:
        return np.ones(k)
    levels = np.array([10, -10, 5, -5, 0])
    if k % 512:
        return np.exp2(np.random.permutation(np.resize(levels, k // 32))).repeat(32)
    a = np.empty((k // 512, 16))
    for p in range(k // 512):
        a[p, :8] = np.random.permutation(np.resize(levels, 8))
        for g in range(8):
            far = levels[np.abs(levels - a[p, g]) >= 10]
            a[p, g + 8] = far[np.random.randint(len(far))]
    return np.exp2(a.ravel()).repeat(32)


def f64(x):
    return np.asarray(x).astype(np.float64)


def striped(idx):
    return np.tile(idx.reshape(-1, 16).T, (8, 1)).astype(np.uint16)


def unstriped(offs):
    return offs[:16].T.reshape(-1).astype(np.int64)


def pack_weight(w):
    k, n = w.shape
    w = f64(np.asarray(w, np.float32).astype(ml_dtypes.bfloat16)).reshape(k // 32, 32, n)
    amax = np.abs(w).max(1)
    byte = np.clip(np.where(amax > 0, np.frexp(amax)[1] - 1 + 127 - 7, 1), 1, 254)
    scaled = (w * np.exp2(127.0 - byte)[:, None, :]).reshape(k, n).astype(np.float32)
    words = np.ascontiguousarray(scaled.reshape(k // 512, 128, 4, n).transpose(0, 1, 3, 2)).astype(ml_dtypes.float8_e4m3fn).view(np.uint8)
    return words, np.ascontiguousarray(byte.astype(np.uint8).reshape(k // 512, 16, n))


def unpack_weight(words, scales):
    g, p, n, _ = words.shape
    vals = np.ascontiguousarray(words).view(ml_dtypes.float8_e4m3fn).astype(np.float64) * np.repeat(np.exp2(scales.astype(np.float64) - 127.0), 8, axis=1)[..., None]
    return vals.transpose(0, 1, 3, 2).reshape(g * 512, n)


E2M1 = np.array([0.0, 0.5, 1.0, 1.5, 2.0, 3.0, 4.0, 6.0, -0.0, -0.5, -1.0, -1.5, -2.0, -3.0, -4.0, -6.0])


def pack_fp4(w):
    k, n = w.shape
    w = f64(np.asarray(w, np.float32).astype(ml_dtypes.bfloat16)).reshape(k // 32, 32, n)
    amax = np.abs(w).max(1)
    mant, ex = np.frexp(amax / 6.0)
    byte = np.clip(np.where(amax > 0, np.where(mant > 0.5, ex, ex - 1) + 127, 1), 1, 254)
    scaled = (w * np.exp2(127.0 - byte)[:, None, :]).reshape(k, n).astype(np.float32)
    c = np.ascontiguousarray(scaled.reshape(k // 512, 128, 4, n).transpose(0, 1, 3, 2)).astype(ml_dtypes.float4_e2m1fn).view(np.uint8) & 0xF
    words = (c[..., 0::2] | (c[..., 1::2] << 4)).reshape(k // 512, 128, 2 * n)
    return np.ascontiguousarray(words), np.ascontiguousarray(byte.astype(np.uint8).reshape(k // 512, 16, n))


def unpack_fp4(words, scales):
    g, _, n = scales.shape
    words = np.ascontiguousarray(words).reshape(g, 128, n, 2)
    nib = np.empty((g, 128, n, 4), np.uint8)
    nib[..., 0::2] = words & 0xF
    nib[..., 1::2] = words >> 4
    vals = E2M1[nib] * np.repeat(np.exp2(scales.astype(np.float64) - 127.0), 8, axis=1)[..., None]
    return vals.transpose(0, 1, 3, 2).reshape(g * 512, n)


def silu(v):
    return v / (1.0 + np.exp(-np.maximum(v, -700.0)))


K, T, H, N, J, U = 1024, 512, 512, 256, 512, 1024


def setup_inputs():
    n = np.random.standard_normal
    s = mx_kscale(K)[:, None]
    u = mx_kscale(H)
    r = mx_kscale(J)[:, None]
    packed_xT = pack_weight(n((K, T)) * s)
    packed_w2 = pack_fp4(n((H, N)) / np.sqrt(2 * H) / u[:, None])
    return {
        "x_words": packed_xT[0],
        "x_scales": packed_xT[1],
        "aT": (n((J, U)) * r).astype(np.float32),
        "w1": (n((K, H)) / np.sqrt(K) / s * u).astype(np.float32),
        "w3": (n((J, H)) / np.sqrt(J) / r).astype(np.float32),
        "w2_words": packed_w2[0],
        "w2_scales": packed_w2[1],
        "pos1": striped(np.random.permutation(T)),
        "pos2": striped(np.random.permutation(T)),
    }


def reference(x_words, x_scales, aT, w1, w3, w2_words, w2_scales, pos1, pos2):
    xq = unpack_weight(x_words, x_scales)
    h = silu(mxq(f64(w1), 0, "e4m3").T @ xq)
    f = mxq(f64(w3), 0, "e4m3").T @ mxq(f64(aT), 0, "e4m3")
    z = h[:, unstriped(pos1)] * f[:, :T] + h[:, unstriped(pos2)] * f[:, T:2 * T]
    return silu(unpack_fp4(w2_words, w2_scales).T @ mxq(z, 0, "e4m3"))

@@ -1,0 +1,225 @@
+from contextlib import ExitStack
+
+import concourse.mybir as mybir
+from concourse.masks import make_identity
+
+K, T, H, N, J = 1024, 512, 512, 256, 512
+FLOPS = 2 * (K * H * T + J * H * 2 * T + H * N * T)
+
+F32 = mybir.dt.float32
+BF16 = mybir.dt.bfloat16
+I32 = mybir.dt.int32
+U32 = mybir.dt.uint32
+U16 = mybir.dt.uint16
+U8 = mybir.dt.uint8
+FP8X4 = mybir.dt.float8_e4m3fn_x4
+FP4X4 = mybir.dt.float4_e2m1fn_x4
+SILU = mybir.ActivationFunctionType.Silu
+MULT = mybir.AluOpType.mult
+
+P = 128
+PACK = 4
+K_PASS = P * PACK
+BLOCKS = H // P
+HALF = T // 2
+LISTS = 2
+
+
+def interleave(copy, grouped, raw):
+    copy(
+        out=grouped.rearrange("p s (c i) j -> p s c j i", i=PACK),
+        in_=raw.rearrange("p s j (c i) -> p s c j i", i=PACK),
+    )
+
+
+def quantize(nc, codes, scales, grouped):
+    nc.vector.quantize_mx(out=codes.bitcast(FP8X4), scales=scales, in_=grouped)
+
+
+def tile_picked_wdime_silu_l_kernel(tc, x_words, x_scales, aT, w1, w3, w2_words, w2_scales, pos1, pos2, out):
+    nc = tc.nc
+    with ExitStack() as ctx:
+        keep = ctx.enter_context(tc.tile_pool(name="keep", bufs=1))
+        psum = ctx.enter_context(tc.psum_pool(name="psum", bufs=1))
+
+        lists = [keep.tile([P, T // 16], U16, name="pos%d" % d) for d in range(LISTS)]
+        x_codes = [keep.tile([P, T], U32, name="x_codes%d" % g, align_bytes=64) for g in range(2)]
+        x_sc = keep.tile([P, 2, T], U8, align_bytes=64)
+        w2_codes = keep.tile([P, 2 * N], U8, align_bytes=64)
+        w2_sc = keep.tile([P, N], U8, align_bytes=64)
+        ident = keep.tile([P, P], F32)
+        nc.vector.memset(x_sc[:].bitcast(I32), 0)
+        nc.vector.memset(w2_sc[:].bitcast(I32), 0)
+        make_identity(nc, ident[:])
+
+        w1_raw = [keep.tile([P, 2, PACK, P], F32, name="w1_raw%d" % c) for c in range(BLOCKS)]
+        w3_raw = [keep.tile([P, 1, PACK, HALF], F32, name="w3_raw%d" % s) for s in range(2)]
+        a_raw = [[keep.tile([P, 1, PACK, HALF], F32, name="a_raw%d%d" % (hf, d)) for d in range(LISTS)] for hf in range(2)]
+
+        def load_w1(c):
+            for g in range(2):
+                rows = w1[g * K_PASS : (g + 1) * K_PASS, c * P : (c + 1) * P]
+                nc.sync.dma_start(out=w1_raw[c][:, g], in_=rows.rearrange("(p j) n -> p j n", j=PACK))
+
+        def load_cols(raw, src, first):
+            nc.sync.dma_start(out=raw[:, 0], in_=src[:, first : first + HALF].rearrange("(p j) n -> p j n", j=PACK))
+
+        load_w1(0)
+        for q in range(4):
+            nc.sync.dma_start(
+                out=x_sc[32 * q : 32 * q + 4].bitcast(I32),
+                in_=x_scales[:, 4 * q : 4 * q + 4, :].rearrange("g r n -> r g n").bitcast(I32),
+            )
+        for g in range(2):
+            nc.sync.dma_start(out=x_codes[g][:].bitcast(I32), in_=x_words[g].rearrange("p n j -> p (n j)").bitcast(I32))
+        nc.sync.dma_start(lists[0][:], pos1)
+        nc.sync.dma_start(lists[1][:], pos2)
+        load_w1(1)
+        load_cols(w3_raw[0], w3, 0)
+        load_cols(a_raw[0][0], aT, 0)
+        load_cols(a_raw[0][1], aT, T)
+        load_w1(2)
+        load_w1(3)
+        load_cols(w3_raw[1], w3, HALF)
+        load_cols(a_raw[1][0], aT, HALF)
+        load_cols(a_raw[1][1], aT, T + HALF)
+        nc.sync.dma_start(out=w2_codes[:].bitcast(I32), in_=w2_words[0].bitcast(I32))
+        for q in range(4):
+            nc.sync.dma_start(
+                out=w2_sc[32 * q : 32 * q + 4].bitcast(I32),
+                in_=w2_scales[0, 4 * q : 4 * q + 4, :].bitcast(I32),
+            )
+
+        h = [None] * BLOCKS
+        picked = {}
+        prods = {}
+
+        def make_h(c, copy, tag):
+            grouped = keep.tile([P, 2, P, PACK], BF16, name="w1_bf%d" % c, tag=tag, align_bytes=64)
+            interleave(copy, grouped[:], w1_raw[c][:])
+            codes = keep.tile([P, 2, P], U32, name="w1_codes%d" % c, align_bytes=64)
+            scales = keep.tile([P, 2, P], U8, name="w1_sc%d" % c, align_bytes=64)
+            quantize(nc, codes[:].rearrange("p g n -> p (g n)"), scales[:].rearrange("p g n -> p (g n)"),
+                     grouped[:].rearrange("p g n j -> p (g n j)"))
+            acc = psum.tile([P, T], F32, name="h_acc%d" % c, tag="wide", bufs=2)
+            for g in range(2):
+                nc.tensor.matmul_mx(out=acc[:], lhsT=codes[:, g].bitcast(FP8X4), lhsT_scale=scales[:, g],
+                                    rhs=x_codes[g][:].bitcast(FP8X4), rhs_scale=x_sc[:, g],
+                                    start=(g == 0), stop=(g == 1))
+            h[c] = keep.tile([P, T], F32, name="h%d" % c)
+            nc.scalar.activation(out=h[c][:], in_=acc[:], func=SILU)
+
+        def gather(c, hf, tag):
+            g = keep.tile([P, LISTS, HALF], F32, name="picked%d%d" % (c, hf), tag=tag, align_bytes=64)
+            for d in range(LISTS):
+                offsets = lists[d][:, hf * HALF // 16 : (hf + 1) * HALF // 16]
+                nc.vector.tensor_copy(g[:, d], h[c][:].indirect(offsets))
+            picked[c, hf] = g
+
+        w3_codes = [keep.tile([P, HALF], U32, name="w3_codes%d" % s, align_bytes=64) for s in range(2)]
+        w3_sc = [keep.tile([P, HALF], U8, name="w3_sc%d" % s, align_bytes=64) for s in range(2)]
+
+        def make_w3(s, tag):
+            grouped = keep.tile([P, 1, HALF, PACK], BF16, name="w3_bf%d" % s, tag=tag, align_bytes=64)
+            interleave(nc.scalar.copy, grouped[:], w3_raw[s][:])
+            quantize(nc, w3_codes[s][:], w3_sc[s][:], grouped[:].rearrange("p g n j -> p (g n j)"))
+
+        a_q = {}
+
+        def make_a(hf, d, copy, tag):
+            grouped = keep.tile([P, 1, HALF, PACK], BF16, name="a_bf%d%d" % (hf, d), tag=tag, align_bytes=64)
+            interleave(copy, grouped[:], a_raw[hf][d][:])
+            codes = keep.tile([P, HALF], U32, name="a_codes%d%d" % (hf, d), align_bytes=64)
+            scales = keep.tile([P, HALF], U8, name="a_sc%d%d" % (hf, d), align_bytes=64)
+            quantize(nc, codes[:], scales[:], grouped[:].rearrange("p g n j -> p (g n j)"))
+            a_q[hf, d] = (codes, scales)
+
+        zts = {}
+
+        def product(c, hf, tag):
+            w_cols = slice((c % 2) * P, (c % 2 + 1) * P)
+            f = psum.tile([P, LISTS, HALF], F32, name="f%d%d" % (hf, c), tag="f", bufs=2)
+            for d in range(LISTS):
+                codes, scales = a_q[hf, d]
+                nc.tensor.matmul_mx(out=f[:, d], lhsT=w3_codes[c // 2][:, w_cols].bitcast(FP8X4),
+                                    lhsT_scale=w3_sc[c // 2][:, w_cols],
+                                    rhs=codes[:].bitcast(FP8X4), rhs_scale=scales[:], start=True, stop=True)
+            prod = keep.tile([P, LISTS, HALF], F32, name="prod%d%d" % (hf, c), tag=tag, align_bytes=64)
+            nc.vector.tensor_tensor(out=prod[:], in0=picked[c, hf][:], in1=f[:], op=MULT)
+            prods[c, hf] = prod
+            for b in range(2):
+                if c % 2 == 0:
+                    zts[hf, c // 2, b] = psum.tile([P, 2 * P], F32, name="zt%d%d%d" % (hf, c // 2, b), tag="zt%d%d" % (c // 2, b))
+                for d in range(LISTS):
+                    nc.tensor.matmul(out=zts[hf, c // 2, b][:, w_cols], lhsT=prod[:, d, b * P : (b + 1) * P], rhs=ident[:],
+                                     start=(d == 0), stop=(d == LISTS - 1), is_transpose=True)
+
+        zbs = [[keep.tile([P, 2, P, 2], BF16, name="zb%d%d" % (hf, b)) for b in range(2)] for hf in range(2)]
+
+        def round_z(hf, pair, b, copy):
+            src = zts[hf, pair, b][:].rearrange("v (p u e) -> v u p e", u=2, e=2)
+            copy(out=zbs[hf][b][:, :, pair * 64 : (pair + 1) * 64, :], in_=src)
+
+        def finish(hf, blocks, copy, tag, back_tag, back_bufs):
+            nb = len(blocks)
+            key = "%d%d" % (hf, blocks[0])
+            width = nb * P
+            back = psum.tile([P, nb, 2, P], F32, name="back" + key, tag=back_tag, bufs=back_bufs)
+            for i, b in enumerate(blocks):
+                words = zbs[hf][b][:].rearrange("v u p e -> v u (p e)").bitcast(F32)
+                for u in range(2):
+                    nc.tensor.transpose(back[:, i, u], words[:, u], ident[:])
+            grouped = keep.tile([P, width * PACK], BF16, name="z_bf" + key, tag=tag, align_bytes=64)
+            copy(out=grouped[:].bitcast(F32).rearrange("p (b v u) -> p b v u", b=nb, u=2),
+                 in_=back[:].rearrange("p b u v -> p b v u"))
+            codes = keep.tile([P, width], U32, name="z_codes" + key, align_bytes=64)
+            scales = keep.tile([P, width], U8, name="z_sc" + key, align_bytes=64)
+            quantize(nc, codes[:], scales[:], grouped[:])
+            acc = psum.tile([P, N // P, width], F32, name="o_acc" + key, tag="wide", bufs=2)
+            for m in range(N // P):
+                nc.tensor.matmul_mx(out=acc[:, m], lhsT=w2_codes[:, 2 * m * P : 2 * (m + 1) * P].bitcast(FP4X4),
+                                    lhsT_scale=w2_sc[:, m * P : (m + 1) * P],
+                                    rhs=codes[:].bitcast(FP8X4), rhs_scale=scales[:], start=True, stop=True)
+            res = keep.tile([P, N // P, width], F32, name="res" + key)
+            nc.scalar.activation(out=res[:], in_=acc[:], func=SILU)
+            first = hf * HALF + blocks[0] * P
+            nc.sync.dma_start(out=out[:, first : first + width].rearrange("(m p) v -> p m v", p=P), in_=res[:])
+
+        on_vector, on_scalar = nc.vector.tensor_copy, nc.scalar.copy
+        make_h(0, on_vector, "s0")
+        gather(0, 0, "g00")
+        make_h(1, on_scalar, "s1")
+        gather(0, 1, "s1")
+        make_w3(0, "s4")
+        gather(1, 0, "g10")
+        make_a(0, 0, on_scalar, "s6")
+        make_a(0, 1, on_vector, "s7")
+        make_h(2, on_scalar, "s2")
+        gather(1, 1, "s2")
+        make_h(3, on_scalar, "s3")
+        product(0, 0, "s3")
+        product(1, 0, "p10")
+        gather(2, 0, "g20")
+        make_w3(1, "s5")
+        gather(3, 0, "g30")
+        make_a(1, 0, on_scalar, "s8")
+        product(2, 0, "s8")
+        make_a(1, 1, on_scalar, "s9")
+        round_z(0, 0, 0, on_scalar)
+        round_z(0, 0, 1, on_scalar)
+        product(3, 0, "s9")
+        round_z(0, 1, 0, on_scalar)
+        round_z(0, 1, 1, on_scalar)
+        gather(2, 1, "g30")
+        gather(3, 1, "g20")
+        product(0, 1, "p01")
+        product(1, 1, "p11")
+        finish(0, [0, 1], on_scalar, "z0", "wide", 2)
+        round_z(1, 0, 0, on_scalar)
+        round_z(1, 0, 1, on_scalar)
+        product(2, 1, "z0")
+        product(3, 1, "p31")
+        round_z(1, 1, 0, on_scalar)
+        round_z(1, 1, 1, on_vector)
+        finish(1, [0], on_scalar, "z10", "zt00", 1)
+        finish(1, [1], on_vector, "z11", "zt01", 1)

@@ -1,7 +1,6 @@
 from contextlib import ExitStack
 
 import concourse.mybir as mybir
-from concourse.masks import make_identity
 
 K, T, H, N, J = 1024, 512, 512, 256, 512
 FLOPS = 2 * (K * H * T + J * H * 2 * T + H * N * T)
@@ -15,6 +14,7 @@ U8 = mybir.dt.uint8
 FP8X4 = mybir.dt.float8_e4m3fn_x4
 FP4X4 = mybir.dt.float4_e2m1fn_x4
 SILU = mybir.ActivationFunctionType.Silu
+ADD = mybir.AluOpType.add
 MULT = mybir.AluOpType.mult
 
 P = 128
@@ -47,42 +47,35 @@ def tile_picked_wdime_silu_l_kernel(tc, x_words, x_scales, aT, w1, w3, w2_words,
         x_sc = keep.tile([P, 2, T], U8, align_bytes=64)
         w2_codes = keep.tile([P, 2 * N], U8, align_bytes=64)
         w2_sc = keep.tile([P, N], U8, align_bytes=64)
-        ident = keep.tile([P, P], F32)
         nc.vector.memset(x_sc[:].bitcast(I32), 0)
         nc.vector.memset(w2_sc[:].bitcast(I32), 0)
-        make_identity(nc, ident[:])
 
-        w1_raw = [keep.tile([P, 2, PACK, P], F32, name="w1_raw%d" % c) for c in range(BLOCKS)]
-        w3_raw = [keep.tile([P, 1, PACK, HALF], F32, name="w3_raw%d" % s) for s in range(2)]
-        a_raw = [[keep.tile([P, 1, PACK, HALF], F32, name="a_raw%d%d" % (hf, d)) for d in range(LISTS)] for hf in range(2)]
+        def load_cols(name, src, first):
+            raw = keep.tile([P, PACK, HALF], F32, name=name)
+            nc.sync.dma_start(out=raw[:], in_=src[:, first : first + HALF].rearrange("(p j) n -> p j n", j=PACK))
+            return raw
 
-        def load_w1(c):
-            for g in range(2):
-                rows = w1[g * K_PASS : (g + 1) * K_PASS, c * P : (c + 1) * P]
-                nc.sync.dma_start(out=w1_raw[c][:, g], in_=rows.rearrange("(p j) n -> p j n", j=PACK))
-
-        def load_cols(raw, src, first):
-            nc.sync.dma_start(out=raw[:, 0], in_=src[:, first : first + HALF].rearrange("(p j) n -> p j n", j=PACK))
-
-        load_w1(0)
-        for q in range(4):
-            nc.sync.dma_start(
-                out=x_sc[32 * q : 32 * q + 4].bitcast(I32),
-                in_=x_scales[:, 4 * q : 4 * q + 4, :].rearrange("g r n -> r g n").bitcast(I32),
-            )
-        for g in range(2):
+        def load_x(g):
             nc.sync.dma_start(out=x_codes[g][:].bitcast(I32), in_=x_words[g].rearrange("p n j -> p (n j)").bitcast(I32))
+
+        w1_raw = {}
+        for g in range(2):
+            for s in range(2):
+                w1_raw[g, s] = load_cols("w1_raw%d%d" % (g, s), w1[g * K_PASS : (g + 1) * K_PASS], s * HALF)
+            if g == 0:
+                for q in range(4):
+                    nc.sync.dma_start(
+                        out=x_sc[32 * q : 32 * q + 4].bitcast(I32),
+                        in_=x_scales[:, 4 * q : 4 * q + 4, :].rearrange("g r n -> r g n").bitcast(I32),
+                    )
+            load_x(g)
         nc.sync.dma_start(lists[0][:], pos1)
         nc.sync.dma_start(lists[1][:], pos2)
-        load_w1(1)
-        load_cols(w3_raw[0], w3, 0)
-        load_cols(a_raw[0][0], aT, 0)
-        load_cols(a_raw[0][1], aT, T)
-        load_w1(2)
-        load_w1(3)
-        load_cols(w3_raw[1], w3, HALF)
-        load_cols(a_raw[1][0], aT, HALF)
-        load_cols(a_raw[1][1], aT, T + HALF)
+        w3_raw = [load_cols("w3_raw%d" % s, w3, s * HALF) for s in range(2)]
+        a_raw = {}
+        for hf in range(2):
+            for d in range(LISTS):
+                a_raw[hf, d] = load_cols("a_raw%d%d" % (hf, d), aT, d * T + hf * HALF)
         nc.sync.dma_start(out=w2_codes[:].bitcast(I32), in_=w2_words[0].bitcast(I32))
         for q in range(4):
             nc.sync.dma_start(
@@ -90,136 +83,107 @@ def tile_picked_wdime_silu_l_kernel(tc, x_words, x_scales, aT, w1, w3, w2_words,
                 in_=w2_scales[0, 4 * q : 4 * q + 4, :].bitcast(I32),
             )
 
-        h = [None] * BLOCKS
-        picked = {}
-        prods = {}
+        on_vector, on_scalar = nc.vector.tensor_copy, nc.scalar.copy
 
-        def make_h(c, copy, tag):
-            grouped = keep.tile([P, 2, P, PACK], BF16, name="w1_bf%d" % c, tag=tag, align_bytes=64)
-            interleave(copy, grouped[:], w1_raw[c][:])
-            codes = keep.tile([P, 2, P], U32, name="w1_codes%d" % c, align_bytes=64)
-            scales = keep.tile([P, 2, P], U8, name="w1_sc%d" % c, align_bytes=64)
-            quantize(nc, codes[:].rearrange("p g n -> p (g n)"), scales[:].rearrange("p g n -> p (g n)"),
-                     grouped[:].rearrange("p g n j -> p (g n j)"))
-            acc = psum.tile([P, T], F32, name="h_acc%d" % c, tag="wide", bufs=2)
-            for g in range(2):
-                nc.tensor.matmul_mx(out=acc[:], lhsT=codes[:, g].bitcast(FP8X4), lhsT_scale=scales[:, g],
-                                    rhs=x_codes[g][:].bitcast(FP8X4), rhs_scale=x_sc[:, g],
-                                    start=(g == 0), stop=(g == 1))
-            h[c] = keep.tile([P, T], F32, name="h%d" % c)
-            nc.scalar.activation(out=h[c][:], in_=acc[:], func=SILU)
+        def deal(name, raws, copies, tag):
+            grouped = keep.tile([P, PACK, P, PACK], BF16, name=name + "_bf", tag=tag, align_bytes=64)
+            for s in range(2):
+                copies[s](out=grouped[:, :, s * 64 : (s + 1) * 64, :].rearrange("p t m j -> p m j t"),
+                          in_=raws[s][:].rearrange("p j (m t) -> p m j t", t=PACK))
+            codes = keep.tile([P, H], U32, name=name + "_codes", align_bytes=64)
+            scales = keep.tile([P, H], U8, name=name + "_sc", align_bytes=64)
+            for s in range(2):
+                cols = slice(s * HALF, (s + 1) * HALF)
+                quantize(nc, codes[:, cols], scales[:, cols], grouped[:, 2 * s : 2 * s + 2].rearrange("p t m j -> p (t m j)"))
+            return codes, scales
 
-        def gather(c, hf, tag):
-            g = keep.tile([P, LISTS, HALF], F32, name="picked%d%d" % (c, hf), tag=tag, align_bytes=64)
+        accs = [psum.tile([P, T], F32, name="h_acc%d" % t, tag="bank%d" % t) for t in range(PACK)]
+        h = [keep.tile([P, T], F32, name="h%d" % t) for t in range(PACK)]
+        for g in range(2):
+            codes, scales = deal("w1%d" % g, [w1_raw[g, 0], w1_raw[g, 1]], [on_scalar, on_vector], "w1b%d" % g)
+            for t in range(PACK):
+                cols = slice(t * P, (t + 1) * P)
+                nc.tensor.matmul_mx(out=accs[t][:], lhsT=codes[:, cols].bitcast(FP8X4), lhsT_scale=scales[:, cols],
+                                    rhs=x_codes[g][:].bitcast(FP8X4), rhs_scale=x_sc[:, g], start=(g == 0), stop=(g == 1))
+        for t in range(PACK):
+            nc.scalar.activation(out=h[t][:], in_=accs[t][:], func=SILU)
+
+        picked, a_q, w3_q = {}, {}, []
+        prods = [keep.tile([P, PACK, LISTS, HALF], F32, name="prod%d" % hf) for hf in range(2)]
+
+        def gather(t, hf, tag):
+            g = keep.tile([P, LISTS, HALF], F32, name="picked%d%d" % (t, hf), tag=tag, align_bytes=64)
             for d in range(LISTS):
                 offsets = lists[d][:, hf * HALF // 16 : (hf + 1) * HALF // 16]
-                nc.vector.tensor_copy(g[:, d], h[c][:].indirect(offsets))
-            picked[c, hf] = g
-
-        w3_codes = [keep.tile([P, HALF], U32, name="w3_codes%d" % s, align_bytes=64) for s in range(2)]
-        w3_sc = [keep.tile([P, HALF], U8, name="w3_sc%d" % s, align_bytes=64) for s in range(2)]
-
-        def make_w3(s, tag):
-            grouped = keep.tile([P, 1, HALF, PACK], BF16, name="w3_bf%d" % s, tag=tag, align_bytes=64)
-            interleave(nc.scalar.copy, grouped[:], w3_raw[s][:])
-            quantize(nc, w3_codes[s][:], w3_sc[s][:], grouped[:].rearrange("p g n j -> p (g n j)"))
-
-        a_q = {}
+                nc.vector.tensor_copy(g[:, d], h[t][:].indirect(offsets))
+            picked[t, hf] = g
 
         def make_a(hf, d, copy, tag):
             grouped = keep.tile([P, 1, HALF, PACK], BF16, name="a_bf%d%d" % (hf, d), tag=tag, align_bytes=64)
-            interleave(copy, grouped[:], a_raw[hf][d][:])
+            interleave(copy, grouped[:], a_raw[hf, d][:].unsqueeze(1))
             codes = keep.tile([P, HALF], U32, name="a_codes%d%d" % (hf, d), align_bytes=64)
             scales = keep.tile([P, HALF], U8, name="a_sc%d%d" % (hf, d), align_bytes=64)
             quantize(nc, codes[:], scales[:], grouped[:].rearrange("p g n j -> p (g n j)"))
             a_q[hf, d] = (codes, scales)
 
-        zts = {}
+        def product(t, d):
+            cols = slice(t * P, (t + 1) * P)
+            f = psum.tile([P, HALF], F32, name="f%d0%d" % (t, d), tag=("f%d" if d == 0 else "bank%d") % t)
+            codes, scales = a_q[0, d]
+            nc.tensor.matmul_mx(out=f[:], lhsT=w3_q[0][:, cols].bitcast(FP8X4), lhsT_scale=w3_q[1][:, cols],
+                                rhs=codes[:].bitcast(FP8X4), rhs_scale=scales[:], start=True, stop=True)
+            nc.vector.tensor_tensor(out=prods[0][:, t, d], in0=picked[t, 0][:, d], in1=f[:], op=MULT)
 
-        def product(c, hf, tag):
-            w_cols = slice((c % 2) * P, (c % 2 + 1) * P)
-            f = psum.tile([P, LISTS, HALF], F32, name="f%d%d" % (hf, c), tag="f", bufs=2)
+        def filters(t, hf):
+            cols = slice(t * P, (t + 1) * P)
+            f = psum.tile([P, LISTS, HALF], F32, name="f%d%d" % (t, hf), tag="f%d" % t)
             for d in range(LISTS):
                 codes, scales = a_q[hf, d]
-                nc.tensor.matmul_mx(out=f[:, d], lhsT=w3_codes[c // 2][:, w_cols].bitcast(FP8X4),
-                                    lhsT_scale=w3_sc[c // 2][:, w_cols],
+                nc.tensor.matmul_mx(out=f[:, d], lhsT=w3_q[0][:, cols].bitcast(FP8X4), lhsT_scale=w3_q[1][:, cols],
                                     rhs=codes[:].bitcast(FP8X4), rhs_scale=scales[:], start=True, stop=True)
-            prod = keep.tile([P, LISTS, HALF], F32, name="prod%d%d" % (hf, c), tag=tag, align_bytes=64)
-            nc.vector.tensor_tensor(out=prod[:], in0=picked[c, hf][:], in1=f[:], op=MULT)
-            prods[c, hf] = prod
-            for b in range(2):
-                if c % 2 == 0:
-                    zts[hf, c // 2, b] = psum.tile([P, 2 * P], F32, name="zt%d%d%d" % (hf, c // 2, b), tag="zt%d%d" % (c // 2, b))
-                for d in range(LISTS):
-                    nc.tensor.matmul(out=zts[hf, c // 2, b][:, w_cols], lhsT=prod[:, d, b * P : (b + 1) * P], rhs=ident[:],
-                                     start=(d == 0), stop=(d == LISTS - 1), is_transpose=True)
+            f_sb = keep.tile([P, LISTS, HALF], F32, name="f_sb%d" % t)
+            nc.scalar.copy(out=f_sb[:], in_=f[:])
+            return f_sb
 
-        zbs = [[keep.tile([P, 2, P, 2], BF16, name="zb%d%d" % (hf, b)) for b in range(2)] for hf in range(2)]
+        def fused(t, hf, f_sb):
+            for d in range(LISTS):
+                offsets = lists[d][:, hf * HALF // 16 : (hf + 1) * HALF // 16]
+                nc.vector.tensor_tensor(out=prods[hf][:, t, d], in0=h[t][:].indirect(offsets), in1=f_sb[:, d], op=MULT)
 
-        def round_z(hf, pair, b, copy):
-            src = zts[hf, pair, b][:].rearrange("v (p u e) -> v u p e", u=2, e=2)
-            copy(out=zbs[hf][b][:, :, pair * 64 : (pair + 1) * 64, :], in_=src)
-
-        def finish(hf, blocks, copy, tag, back_tag, back_bufs):
-            nb = len(blocks)
-            key = "%d%d" % (hf, blocks[0])
-            width = nb * P
-            back = psum.tile([P, nb, 2, P], F32, name="back" + key, tag=back_tag, bufs=back_bufs)
-            for i, b in enumerate(blocks):
-                words = zbs[hf][b][:].rearrange("v u p e -> v u (p e)").bitcast(F32)
-                for u in range(2):
-                    nc.tensor.transpose(back[:, i, u], words[:, u], ident[:])
-            grouped = keep.tile([P, width * PACK], BF16, name="z_bf" + key, tag=tag, align_bytes=64)
-            copy(out=grouped[:].bitcast(F32).rearrange("p (b v u) -> p b v u", b=nb, u=2),
-                 in_=back[:].rearrange("p b u v -> p b v u"))
+        def finish(hf, first, width, bank, tag):
+            key = "%d%d" % (hf, first // P)
+            cols = slice(first, first + width)
+            grouped = keep.tile([P, width, PACK], BF16, name="z_bf" + key, tag=tag, align_bytes=64)
+            nc.vector.tensor_tensor(out=grouped[:].rearrange("p (c i) t -> p c t i", i=PACK),
+                                    in0=prods[hf][:, :, 0, cols].rearrange("p t (c i) -> p c t i", i=PACK),
+                                    in1=prods[hf][:, :, 1, cols].rearrange("p t (c i) -> p c t i", i=PACK), op=ADD)
             codes = keep.tile([P, width], U32, name="z_codes" + key, align_bytes=64)
             scales = keep.tile([P, width], U8, name="z_sc" + key, align_bytes=64)
-            quantize(nc, codes[:], scales[:], grouped[:])
-            acc = psum.tile([P, N // P, width], F32, name="o_acc" + key, tag="wide", bufs=2)
+            quantize(nc, codes[:], scales[:], grouped[:].rearrange("p v t -> p (v t)"))
+            acc = psum.tile([P, N // P, width], F32, name="o_acc" + key, tag=bank)
             for m in range(N // P):
                 nc.tensor.matmul_mx(out=acc[:, m], lhsT=w2_codes[:, 2 * m * P : 2 * (m + 1) * P].bitcast(FP4X4),
                                     lhsT_scale=w2_sc[:, m * P : (m + 1) * P],
                                     rhs=codes[:].bitcast(FP8X4), rhs_scale=scales[:], start=True, stop=True)
             res = keep.tile([P, N // P, width], F32, name="res" + key)
             nc.scalar.activation(out=res[:], in_=acc[:], func=SILU)
-            first = hf * HALF + blocks[0] * P
-            nc.sync.dma_start(out=out[:, first : first + width].rearrange("(m p) v -> p m v", p=P), in_=res[:])
+            at = hf * HALF + first
+            nc.sync.dma_start(out=out[:, at : at + width].rearrange("(m p) v -> p m v", p=P), in_=res[:])
 
-        on_vector, on_scalar = nc.vector.tensor_copy, nc.scalar.copy
-        make_h(0, on_vector, "s0")
-        gather(0, 0, "g00")
-        make_h(1, on_scalar, "s1")
-        gather(0, 1, "s1")
-        make_w3(0, "s4")
-        gather(1, 0, "g10")
-        make_a(0, 0, on_scalar, "s6")
-        make_a(0, 1, on_vector, "s7")
-        make_h(2, on_scalar, "s2")
-        gather(1, 1, "s2")
-        make_h(3, on_scalar, "s3")
-        product(0, 0, "s3")
-        product(1, 0, "p10")
-        gather(2, 0, "g20")
-        make_w3(1, "s5")
-        gather(3, 0, "g30")
-        make_a(1, 0, on_scalar, "s8")
-        product(2, 0, "s8")
-        make_a(1, 1, on_scalar, "s9")
-        round_z(0, 0, 0, on_scalar)
-        round_z(0, 0, 1, on_scalar)
-        product(3, 0, "s9")
-        round_z(0, 1, 0, on_scalar)
-        round_z(0, 1, 1, on_scalar)
-        gather(2, 1, "g30")
-        gather(3, 1, "g20")
-        product(0, 1, "p01")
-        product(1, 1, "p11")
-        finish(0, [0, 1], on_scalar, "z0", "wide", 2)
-        round_z(1, 0, 0, on_scalar)
-        round_z(1, 0, 1, on_scalar)
-        product(2, 1, "z0")
-        product(3, 1, "p31")
-        round_z(1, 1, 0, on_scalar)
-        round_z(1, 1, 1, on_vector)
-        finish(1, [0], on_scalar, "z10", "zt00", 1)
-        finish(1, [1], on_vector, "z11", "zt01", 1)
+        w3_q.extend(deal("w3", w3_raw, [on_vector, on_scalar], "w3b"))
+        for t in range(PACK - 1):
+            gather(t, 0, "g%d0" % t)
+        make_a(0, 0, on_scalar, "a00")
+        gather(3, 0, "a00")
+        make_a(0, 1, on_scalar, "a01")
+        make_a(1, 0, on_scalar, "a10")
+        make_a(1, 1, on_scalar, "a11")
+        for d in range(LISTS):
+            for t in range(PACK):
+                product(t, d)
+        f_late = [filters(t, 1) for t in range(PACK)]
+        finish(0, 0, HALF, "bank0", "z0")
+        for t in range(PACK):
+            fused(t, 1, f_late[t])
+        finish(1, 0, P, "bank1", "z10")
+        finish(1, P, P, "bank2", "z11")

@@ -23,6 +23,7 @@ K_PASS = P * PACK
 BLOCKS = H // P
 HALF = T // 2
 LISTS = 2
+WINDOW = 704
 
 
 def interleave(copy, grouped, raw):
@@ -44,7 +45,7 @@ def tile_picked_wdime_silu_l_kernel(tc, x_words, x_scales, aT, w1, w3, w2_words,
 
         lists = [keep.tile([P, T // 16], U16, name="pos%d" % d) for d in range(LISTS)]
         x_codes = [keep.tile([P, T], U32, name="x_codes%d" % g, align_bytes=64) for g in range(2)]
-        x_sc = keep.tile([P, 2, T], U8, align_bytes=64)
+        x_sc = keep.tile([P, T], U8, align_bytes=64)
         w2_codes = keep.tile([P, 2 * N], U8, align_bytes=64)
         w2_sc = keep.tile([P, N], U8, align_bytes=64)
         nc.vector.memset(x_sc[:].bitcast(I32), 0)
@@ -65,8 +66,8 @@ def tile_picked_wdime_silu_l_kernel(tc, x_words, x_scales, aT, w1, w3, w2_words,
             if g == 0:
                 for q in range(4):
                     nc.sync.dma_start(
-                        out=x_sc[32 * q : 32 * q + 4].bitcast(I32),
-                        in_=x_scales[:, 4 * q : 4 * q + 4, :].rearrange("g r n -> r g n").bitcast(I32),
+                        out=x_sc[32 * q : 32 * q + 8].bitcast(I32),
+                        in_=x_scales[:, 4 * q : 4 * q + 4, :].bitcast(I32),
                     )
             load_x(g)
         nc.sync.dma_start(lists[0][:], pos1)
@@ -85,38 +86,46 @@ def tile_picked_wdime_silu_l_kernel(tc, x_words, x_scales, aT, w1, w3, w2_words,
 
         on_vector, on_scalar = nc.vector.tensor_copy, nc.scalar.copy
 
-        def deal(name, raws, copies, tag):
+        def deal(name, raws, shares, calls, tag):
             grouped = keep.tile([P, PACK, P, PACK], BF16, name=name + "_bf", tag=tag, align_bytes=64)
             for s in range(2):
-                copies[s](out=grouped[:, :, s * 64 : (s + 1) * 64, :].rearrange("p t m j -> p m j t"),
-                          in_=raws[s][:].rearrange("p j (m t) -> p m j t", t=PACK))
+                src = raws[s][:].rearrange("p j (m t) -> p m j t", t=PACK)
+                first = 0
+                for copy, count in shares[s]:
+                    dst = grouped[:, :, s * 64 + first : s * 64 + first + count, :]
+                    copy(out=dst.rearrange("p t m j -> p m j t"), in_=src[:, first : first + count])
+                    first = first + count
             codes = keep.tile([P, H], U32, name=name + "_codes", align_bytes=64)
             scales = keep.tile([P, H], U8, name=name + "_sc", align_bytes=64)
-            for s in range(2):
-                cols = slice(s * HALF, (s + 1) * HALF)
-                quantize(nc, codes[:, cols], scales[:, cols], grouped[:, 2 * s : 2 * s + 2].rearrange("p t m j -> p (t m j)"))
+            tiles = PACK // calls
+            for s in range(calls):
+                cols = slice(s * tiles * P, (s + 1) * tiles * P)
+                quantize(nc, codes[:, cols], scales[:, cols],
+                         grouped[:, s * tiles : (s + 1) * tiles].rearrange("p t m j -> p (t m j)"))
             return codes, scales
 
         accs = [psum.tile([P, T], F32, name="h_acc%d" % t, tag="bank%d" % t) for t in range(PACK)]
-        h = [keep.tile([P, T], F32, name="h%d" % t) for t in range(PACK)]
+        h = [keep.tile([P, WINDOW], F32, name="h%d" % t) for t in range(PACK)]
+        for t in range(PACK):
+            nc.vector.memset(h[t][:, T:], 0.0)
         for g in range(2):
-            codes, scales = deal("w1%d" % g, [w1_raw[g, 0], w1_raw[g, 1]], [on_scalar, on_vector], "w1b%d" % g)
+            codes, scales = deal("w1%d" % g, [w1_raw[g, 0], w1_raw[g, 1]],
+                                 [[(on_scalar, 64)], [(on_vector, 40), (on_scalar, 24)]], PACK if g == 1 else 1, "w1b%d" % g)
             for t in range(PACK):
                 cols = slice(t * P, (t + 1) * P)
                 nc.tensor.matmul_mx(out=accs[t][:], lhsT=codes[:, cols].bitcast(FP8X4), lhsT_scale=scales[:, cols],
-                                    rhs=x_codes[g][:].bitcast(FP8X4), rhs_scale=x_sc[:, g], start=(g == 0), stop=(g == 1))
+                                    rhs=x_codes[g][:].bitcast(FP8X4), rhs_scale=x_sc[4 * g :, :], start=(g == 0), stop=(g == 1))
         for t in range(PACK):
-            nc.scalar.activation(out=h[t][:], in_=accs[t][:], func=SILU)
+            nc.scalar.activation(out=h[t][:, :T], in_=accs[t][:], func=SILU)
 
         picked, a_q, w3_q = {}, {}, []
-        prods = [keep.tile([P, PACK, LISTS, HALF], F32, name="prod%d" % hf) for hf in range(2)]
+        prods = []
 
-        def gather(t, hf, tag):
-            g = keep.tile([P, LISTS, HALF], F32, name="picked%d%d" % (t, hf), tag=tag, align_bytes=64)
+        def gather(t, tag):
+            g = keep.tile([P, LISTS, T], F32, name="picked%d" % t, tag=tag, align_bytes=64)
             for d in range(LISTS):
-                offsets = lists[d][:, hf * HALF // 16 : (hf + 1) * HALF // 16]
-                nc.vector.tensor_copy(g[:, d], h[t][:].indirect(offsets))
-            picked[t, hf] = g
+                nc.vector.tensor_copy(g[:, d], h[t][:].indirect(lists[d][:]))
+            picked[t] = g
 
         def make_a(hf, d, copy, tag):
             grouped = keep.tile([P, 1, HALF, PACK], BF16, name="a_bf%d%d" % (hf, d), tag=tag, align_bytes=64)
@@ -126,37 +135,29 @@ def tile_picked_wdime_silu_l_kernel(tc, x_words, x_scales, aT, w1, w3, w2_words,
             quantize(nc, codes[:], scales[:], grouped[:].rearrange("p g n j -> p (g n j)"))
             a_q[hf, d] = (codes, scales)
 
-        def product(t, d):
+        def product(t, hf, pieces):
             cols = slice(t * P, (t + 1) * P)
-            f = psum.tile([P, HALF], F32, name="f%d0%d" % (t, d), tag=("f%d" if d == 0 else "bank%d") % t)
-            codes, scales = a_q[0, d]
-            nc.tensor.matmul_mx(out=f[:], lhsT=w3_q[0][:, cols].bitcast(FP8X4), lhsT_scale=w3_q[1][:, cols],
-                                rhs=codes[:].bitcast(FP8X4), rhs_scale=scales[:], start=True, stop=True)
-            nc.vector.tensor_tensor(out=prods[0][:, t, d], in0=picked[t, 0][:, d], in1=f[:], op=MULT)
-
-        def filters(t, hf):
-            cols = slice(t * P, (t + 1) * P)
-            f = psum.tile([P, LISTS, HALF], F32, name="f%d%d" % (t, hf), tag="f%d" % t)
+            f = psum.tile([P, LISTS, HALF], F32, name="f%d%d" % (t, hf), tag=("f%d" if hf == 0 else "bank%d") % t)
             for d in range(LISTS):
                 codes, scales = a_q[hf, d]
                 nc.tensor.matmul_mx(out=f[:, d], lhsT=w3_q[0][:, cols].bitcast(FP8X4), lhsT_scale=w3_q[1][:, cols],
                                     rhs=codes[:].bitcast(FP8X4), rhs_scale=scales[:], start=True, stop=True)
-            f_sb = keep.tile([P, LISTS, HALF], F32, name="f_sb%d" % t)
-            nc.scalar.copy(out=f_sb[:], in_=f[:])
-            return f_sb
+            width = HALF // pieces
+            for b in range(pieces):
+                v = slice(b * width, (b + 1) * width)
+                seen = picked[t][:, :, hf * HALF : (hf + 1) * HALF]
+                nc.vector.tensor_tensor(out=prods[hf][:, t, :, v], in0=seen[:, :, v], in1=f[:, :, v], op=MULT)
 
-        def fused(t, hf, f_sb):
-            for d in range(LISTS):
-                offsets = lists[d][:, hf * HALF // 16 : (hf + 1) * HALF // 16]
-                nc.vector.tensor_tensor(out=prods[hf][:, t, d], in0=h[t][:].indirect(offsets), in1=f_sb[:, d], op=MULT)
-
-        def finish(hf, first, width, bank, tag):
+        def finish(hf, first, width, bank, tag, sums):
             key = "%d%d" % (hf, first // P)
             cols = slice(first, first + width)
             grouped = keep.tile([P, width, PACK], BF16, name="z_bf" + key, tag=tag, align_bytes=64)
-            nc.vector.tensor_tensor(out=grouped[:].rearrange("p (c i) t -> p c t i", i=PACK),
-                                    in0=prods[hf][:, :, 0, cols].rearrange("p t (c i) -> p c t i", i=PACK),
-                                    in1=prods[hf][:, :, 1, cols].rearrange("p t (c i) -> p c t i", i=PACK), op=ADD)
+            if sums is None:
+                nc.vector.tensor_tensor(out=grouped[:].rearrange("p (c i) t -> p c t i", i=PACK),
+                                        in0=prods[hf][:, :, 0, cols].rearrange("p t (c i) -> p c t i", i=PACK),
+                                        in1=prods[hf][:, :, 1, cols].rearrange("p t (c i) -> p c t i", i=PACK), op=ADD)
+            else:
+                interleave(on_scalar, grouped[:].unsqueeze(1), sums[:].unsqueeze(1))
             codes = keep.tile([P, width], U32, name="z_codes" + key, align_bytes=64)
             scales = keep.tile([P, width], U8, name="z_sc" + key, align_bytes=64)
             quantize(nc, codes[:], scales[:], grouped[:].rearrange("p v t -> p (v t)"))
@@ -170,20 +171,22 @@ def tile_picked_wdime_silu_l_kernel(tc, x_words, x_scales, aT, w1, w3, w2_words,
             at = hf * HALF + first
             nc.sync.dma_start(out=out[:, at : at + width].rearrange("(m p) v -> p m v", p=P), in_=res[:])
 
-        w3_q.extend(deal("w3", w3_raw, [on_vector, on_scalar], "w3b"))
         for t in range(PACK - 1):
-            gather(t, 0, "g%d0" % t)
+            gather(t, "g%d" % t)
+        w3_q.extend(deal("w3", w3_raw, [[(on_scalar, 64)], [(on_scalar, 64)]], 1, "w11_codes"))
         make_a(0, 0, on_scalar, "a00")
-        gather(3, 0, "a00")
         make_a(0, 1, on_scalar, "a01")
+        gather(3, "a01")
         make_a(1, 0, on_scalar, "a10")
         make_a(1, 1, on_scalar, "a11")
-        for d in range(LISTS):
-            for t in range(PACK):
-                product(t, d)
-        f_late = [filters(t, 1) for t in range(PACK)]
-        finish(0, 0, HALF, "bank0", "z0")
+        prods.append(keep.tile([P, PACK, LISTS, HALF], F32, name="prod0", tag="a11", align_bytes=64))
+        prods.append(keep.tile([P, PACK, LISTS, HALF], F32, name="prod1"))
+        sums = keep.tile([P, PACK, HALF], F32)
         for t in range(PACK):
-            fused(t, 1, f_late[t])
-        finish(1, 0, P, "bank1", "z10")
-        finish(1, P, P, "bank2", "z11")
+            product(t, 0, 1)
+            nc.gpsimd.tensor_tensor(out=sums[:, t], in0=prods[0][:, t, 0], in1=prods[0][:, t, 1], op=ADD)
+        for t in range(PACK):
+            product(t, 1, 2 if t == PACK - 1 else 1)
+        finish(0, 0, HALF, "f0", "z0", sums)
+        finish(1, 0, P, "f1", "z10", None)
+        finish(1, P, P, "f2", "z11", None)

@@ -61,9 +61,14 @@ def tile_picked_wdime_silu_l_kernel(tc, x_words, x_scales, aT, w1, w3, w2_words,
 
         w1_raw = {}
         for g in range(2):
-            for s in range(2):
-                w1_raw[g, s] = load_cols("w1_raw%d%d" % (g, s), w1[g * K_PASS : (g + 1) * K_PASS], s * HALF)
+            if g == 1:
+                for s in range(2):
+                    w1_raw[g, s] = load_cols("w1_raw%d%d" % (g, s), w1[g * K_PASS : (g + 1) * K_PASS], s * HALF)
             if g == 0:
+                whole = keep.tile([P, PACK, H], F32, name="w1_raw0")
+                nc.sync.dma_start(out=whole[:], in_=w1[:K_PASS].rearrange("(p j) n -> p j n", j=PACK))
+                for s in range(2):
+                    w1_raw[g, s] = whole[:, :, s * HALF : (s + 1) * HALF]
                 for q in range(4):
                     nc.sync.dma_start(
                         out=x_sc[32 * q : 32 * q + 8].bitcast(I32),
@@ -74,8 +79,8 @@ def tile_picked_wdime_silu_l_kernel(tc, x_words, x_scales, aT, w1, w3, w2_words,
         nc.sync.dma_start(lists[1][:], pos2)
         w3_raw = [load_cols("w3_raw%d" % s, w3, s * HALF) for s in range(2)]
         a_raw = {}
-        for hf in range(2):
-            for d in range(LISTS):
+        for d in range(LISTS):
+            for hf in range(2):
                 a_raw[hf, d] = load_cols("a_raw%d%d" % (hf, d), aT, d * T + hf * HALF)
         nc.sync.dma_start(out=w2_codes[:].bitcast(I32), in_=w2_words[0].bitcast(I32))
         for q in range(4):
@@ -110,7 +115,7 @@ def tile_picked_wdime_silu_l_kernel(tc, x_words, x_scales, aT, w1, w3, w2_words,
             nc.vector.memset(h[t][:, T:], 0.0)
         for g in range(2):
             codes, scales = deal("w1%d" % g, [w1_raw[g, 0], w1_raw[g, 1]],
-                                 [[(on_scalar, 64)], [(on_vector, 40), (on_scalar, 24)]], PACK if g == 1 else 1, "w1b%d" % g)
+                                 [[(on_scalar, 64)], [(on_vector, 40), (on_scalar, 24)]] if g == 1 else [[(on_scalar, 44), (on_vector, 20)], [(on_vector, 64)]], PACK if g == 1 else 1, "w1b%d" % g)
             for t in range(PACK):
                 cols = slice(t * P, (t + 1) * P)
                 nc.tensor.matmul_mx(out=accs[t][:], lhsT=codes[:, cols].bitcast(FP8X4), lhsT_scale=scales[:, cols],
@@ -119,12 +124,11 @@ def tile_picked_wdime_silu_l_kernel(tc, x_words, x_scales, aT, w1, w3, w2_words,
             nc.scalar.activation(out=h[t][:, :T], in_=accs[t][:], func=SILU)
 
         picked, a_q, w3_q = {}, {}, []
-        prods = []
+        prods = [keep.tile([P, PACK, LISTS, HALF], F32, name="prod%d" % hf) for hf in range(2)]
 
         def gather(t, tag):
-            g = keep.tile([P, LISTS, T], F32, name="picked%d" % t, tag=tag, align_bytes=64)
-            for d in range(LISTS):
-                nc.vector.tensor_copy(g[:, d], h[t][:].indirect(lists[d][:]))
+            g = keep.tile([P, T], F32, name="picked%d" % t, tag=tag, align_bytes=64)
+            nc.vector.tensor_copy(g[:], h[t][:].indirect(lists[0][:]))
             picked[t] = g
 
         def make_a(hf, d, copy, tag):
@@ -135,18 +139,28 @@ def tile_picked_wdime_silu_l_kernel(tc, x_words, x_scales, aT, w1, w3, w2_words,
             quantize(nc, codes[:], scales[:], grouped[:].rearrange("p g n j -> p (g n j)"))
             a_q[hf, d] = (codes, scales)
 
-        def product(t, hf, pieces):
+        def filters(t, hf, d):
             cols = slice(t * P, (t + 1) * P)
-            f = psum.tile([P, LISTS, HALF], F32, name="f%d%d" % (t, hf), tag=("f%d" if hf == 0 else "bank%d") % t)
-            for d in range(LISTS):
-                codes, scales = a_q[hf, d]
-                nc.tensor.matmul_mx(out=f[:, d], lhsT=w3_q[0][:, cols].bitcast(FP8X4), lhsT_scale=w3_q[1][:, cols],
-                                    rhs=codes[:].bitcast(FP8X4), rhs_scale=scales[:], start=True, stop=True)
+            f = psum.tile([P, HALF], F32, name="f%d%d%d" % (t, hf, d), tag=("f%d" if hf == 0 else "bank%d") % t)
+            codes, scales = a_q[hf, d]
+            nc.tensor.matmul_mx(out=f[:], lhsT=w3_q[0][:, cols].bitcast(FP8X4), lhsT_scale=w3_q[1][:, cols],
+                                rhs=codes[:].bitcast(FP8X4), rhs_scale=scales[:], start=True, stop=True)
+            return f
+
+        def product(t, hf):
+            f = filters(t, hf, 0)
+            nc.vector.tensor_tensor(out=prods[hf][:, t, 0], in0=picked[t][:, hf * HALF : (hf + 1) * HALF], in1=f[:], op=MULT)
+
+        def fused(t, hf, pieces):
+            f = filters(t, hf, 1)
+            f_sb = keep.tile([P, HALF], F32, name="f_sb%d%d" % (t, hf))
+            nc.scalar.copy(out=f_sb[:], in_=f[:])
             width = HALF // pieces
             for b in range(pieces):
                 v = slice(b * width, (b + 1) * width)
-                seen = picked[t][:, :, hf * HALF : (hf + 1) * HALF]
-                nc.vector.tensor_tensor(out=prods[hf][:, t, :, v], in0=seen[:, :, v], in1=f[:, :, v], op=MULT)
+                first = (hf * HALF + b * width) // 16
+                offsets = lists[1][:, first : first + width // 16]
+                nc.vector.tensor_tensor(out=prods[hf][:, t, 1, v], in0=h[t][:].indirect(offsets), in1=f_sb[:, v], op=MULT)
 
         def finish(hf, first, width, bank, tag, sums):
             key = "%d%d" % (hf, first // P)
@@ -171,22 +185,21 @@ def tile_picked_wdime_silu_l_kernel(tc, x_words, x_scales, aT, w1, w3, w2_words,
             at = hf * HALF + first
             nc.sync.dma_start(out=out[:, at : at + width].rearrange("(m p) v -> p m v", p=P), in_=res[:])
 
+        w3_q.extend(deal("w3", w3_raw, [[(on_vector, 64)], [(on_scalar, 64)]], 1, "w3b"))
         for t in range(PACK - 1):
             gather(t, "g%d" % t)
-        w3_q.extend(deal("w3", w3_raw, [[(on_scalar, 64)], [(on_scalar, 64)]], 1, "w11_codes"))
         make_a(0, 0, on_scalar, "a00")
-        make_a(0, 1, on_scalar, "a01")
-        gather(3, "a01")
+        gather(3, "a00")
         make_a(1, 0, on_scalar, "a10")
+        make_a(0, 1, on_scalar, "a01")
         make_a(1, 1, on_scalar, "a11")
-        prods.append(keep.tile([P, PACK, LISTS, HALF], F32, name="prod0", tag="a11", align_bytes=64))
-        prods.append(keep.tile([P, PACK, LISTS, HALF], F32, name="prod1"))
-        sums = keep.tile([P, PACK, HALF], F32)
+        for hf in range(2):
+            for t in range(PACK):
+                product(t, hf)
         for t in range(PACK):
-            product(t, 0, 1)
-            nc.gpsimd.tensor_tensor(out=sums[:, t], in0=prods[0][:, t, 0], in1=prods[0][:, t, 1], op=ADD)
+            fused(t, 0, 1)
+        finish(0, 0, HALF, "f0", "z0", None)
         for t in range(PACK):
-            product(t, 1, 2 if t == PACK - 1 else 1)
-        finish(0, 0, HALF, "f0", "z0", sums)
+            fused(t, 1, 2 if t == PACK - 1 else 1)
         finish(1, 0, P, "f1", "z10", None)
         finish(1, P, P, "f2", "z11", None)

@@ -20,17 +20,18 @@ MULT = mybir.AluOpType.mult
 P = 128
 PACK = 4
 K_PASS = P * PACK
-BLOCKS = H // P
-HALF = T // 2
+PASSES = K // K_PASS
+QUADRANTS = 4
 LISTS = 2
+HALF = T // 2
+HALF_WORDS = HALF // PACK
+PER_COLUMN = 16
 WINDOW = 704
+VECTOR_WORDS = 36
 
 
-def interleave(copy, grouped, raw):
-    copy(
-        out=grouped.rearrange("p s (c i) j -> p s c j i", i=PACK),
-        in_=raw.rearrange("p s j (c i) -> p s c j i", i=PACK),
-    )
+def four_by_four(ap, pattern):
+    return ap.rearrange(pattern + " -> p c j i", i=PACK)
 
 
 def quantize(nc, codes, scales, grouped):
@@ -39,12 +40,13 @@ def quantize(nc, codes, scales, grouped):
 
 def tile_picked_wdime_silu_l_kernel(tc, x_words, x_scales, aT, w1, w3, w2_words, w2_scales, pos1, pos2, out):
     nc = tc.nc
+    on_vector, on_scalar = nc.vector.tensor_copy, nc.scalar.copy
     with ExitStack() as ctx:
         keep = ctx.enter_context(tc.tile_pool(name="keep", bufs=1))
         psum = ctx.enter_context(tc.psum_pool(name="psum", bufs=1))
 
-        lists = [keep.tile([P, T // 16], U16, name="pos%d" % d) for d in range(LISTS)]
-        x_codes = [keep.tile([P, T], U32, name="x_codes%d" % g, align_bytes=64) for g in range(2)]
+        lists = [keep.tile([P, T // PER_COLUMN], U16, name="pos%d" % d) for d in range(LISTS)]
+        x_codes = [keep.tile([P, T], U32, name="x_codes%d" % g, align_bytes=64) for g in range(PASSES)]
         x_sc = keep.tile([P, T], U8, align_bytes=64)
         w2_codes = keep.tile([P, 2 * N], U8, align_bytes=64)
         w2_sc = keep.tile([P, N], U8, align_bytes=64)
@@ -56,126 +58,117 @@ def tile_picked_wdime_silu_l_kernel(tc, x_words, x_scales, aT, w1, w3, w2_words,
             nc.sync.dma_start(out=raw[:], in_=src[:, first : first + HALF].rearrange("(p j) n -> p j n", j=PACK))
             return raw
 
+        def load_w1(g):
+            return [load_cols("w1_raw%d%d" % (g, s), w1[g * K_PASS : (g + 1) * K_PASS], s * HALF) for s in range(2)]
+
         def load_x(g):
             nc.sync.dma_start(out=x_codes[g][:].bitcast(I32), in_=x_words[g].rearrange("p n j -> p (n j)").bitcast(I32))
 
-        w1_raw = {}
-        for g in range(2):
-            if g == 1:
-                for s in range(2):
-                    w1_raw[g, s] = load_cols("w1_raw%d%d" % (g, s), w1[g * K_PASS : (g + 1) * K_PASS], s * HALF)
-            if g == 0:
-                whole = keep.tile([P, PACK, H], F32, name="w1_raw0")
-                nc.sync.dma_start(out=whole[:], in_=w1[:K_PASS].rearrange("(p j) n -> p j n", j=PACK))
-                for s in range(2):
-                    w1_raw[g, s] = whole[:, :, s * HALF : (s + 1) * HALF]
-                for q in range(4):
-                    nc.sync.dma_start(
-                        out=x_sc[32 * q : 32 * q + 8].bitcast(I32),
-                        in_=x_scales[:, 4 * q : 4 * q + 4, :].bitcast(I32),
-                    )
-            load_x(g)
+        w1_raw = [load_w1(0)]
+        for q in range(QUADRANTS):
+            nc.sync.dma_start(out=x_sc[32 * q : 32 * q + 4 * PASSES].bitcast(I32),
+                              in_=x_scales[:, 4 * q : 4 * q + 4, :].bitcast(I32))
+        load_x(0)
+        w1_raw.append(load_w1(1))
+        load_x(1)
+        w3_raw = [load_cols("w3_raw0", w3, 0)]
         nc.sync.dma_start(lists[0][:], pos1)
+        w3_raw.append(load_cols("w3_raw1", w3, HALF))
         nc.sync.dma_start(lists[1][:], pos2)
-        w3_raw = [load_cols("w3_raw%d" % s, w3, s * HALF) for s in range(2)]
-        a_raw = {}
-        for d in range(LISTS):
-            for hf in range(2):
-                a_raw[hf, d] = load_cols("a_raw%d%d" % (hf, d), aT, d * T + hf * HALF)
+        a_raw = {(hf, d): load_cols("a_raw%d%d" % (hf, d), aT, d * T + hf * HALF) for d in range(LISTS) for hf in range(2)}
         nc.sync.dma_start(out=w2_codes[:].bitcast(I32), in_=w2_words[0].bitcast(I32))
-        for q in range(4):
-            nc.sync.dma_start(
-                out=w2_sc[32 * q : 32 * q + 4].bitcast(I32),
-                in_=w2_scales[0, 4 * q : 4 * q + 4, :].bitcast(I32),
-            )
+        for q in range(QUADRANTS):
+            nc.sync.dma_start(out=w2_sc[32 * q : 32 * q + 4].bitcast(I32),
+                              in_=w2_scales[0, 4 * q : 4 * q + 4, :].bitcast(I32))
 
-        on_vector, on_scalar = nc.vector.tensor_copy, nc.scalar.copy
-
-        def deal(name, raws, shares, calls, tag):
-            grouped = keep.tile([P, PACK, P, PACK], BF16, name=name + "_bf", tag=tag, align_bytes=64)
-            for s in range(2):
-                src = raws[s][:].rearrange("p j (m t) -> p m j t", t=PACK)
-                first = 0
-                for copy, count in shares[s]:
-                    dst = grouped[:, :, s * 64 + first : s * 64 + first + count, :]
-                    copy(out=dst.rearrange("p t m j -> p m j t"), in_=src[:, first : first + count])
-                    first = first + count
+        def deal(name, raws, shares, calls):
+            grouped = keep.tile([P, PACK, P, PACK], BF16, name=name + "_bf", align_bytes=64)
+            for s, raw in enumerate(raws):
+                src = raw[:].rearrange("p j (m t) -> p m j t", t=PACK)
+                for copy, words, tiles in shares[s]:
+                    dst = grouped[:, tiles, s * HALF_WORDS : (s + 1) * HALF_WORDS][:, :, words]
+                    copy(out=dst.rearrange("p t m j -> p m j t"), in_=src[:, words, :, tiles])
             codes = keep.tile([P, H], U32, name=name + "_codes", align_bytes=64)
             scales = keep.tile([P, H], U8, name=name + "_sc", align_bytes=64)
-            tiles = PACK // calls
+            per_call = PACK // calls
             for s in range(calls):
-                cols = slice(s * tiles * P, (s + 1) * tiles * P)
+                cols = slice(s * per_call * P, (s + 1) * per_call * P)
                 quantize(nc, codes[:, cols], scales[:, cols],
-                         grouped[:, s * tiles : (s + 1) * tiles].rearrange("p t m j -> p (t m j)"))
+                         grouped[:, s * per_call : (s + 1) * per_call].rearrange("p t m j -> p (t m j)"))
             return codes, scales
 
-        accs = [psum.tile([P, T], F32, name="h_acc%d" % t, tag="bank%d" % t) for t in range(PACK)]
+        all_words, all_tiles = slice(0, HALF_WORDS), slice(0, PACK)
+        whole_on_vector = [(on_vector, all_words, all_tiles)]
+        whole_on_scalar = [(on_scalar, all_words, all_tiles)]
+        tile_0_first = [(on_vector, all_words, slice(0, 1)),
+                        (on_vector, slice(0, VECTOR_WORDS), slice(1, PACK)),
+                        (on_scalar, slice(VECTOR_WORDS, HALF_WORDS), slice(1, PACK))]
+        w1_shares = [[whole_on_scalar, whole_on_vector], [whole_on_scalar, tile_0_first]]
+        w1_calls = [1, PACK]
+
+        h_acc = [psum.tile([P, T], F32, name="h_acc%d" % t, tag="upper%d" % t) for t in range(PACK)]
         h = [keep.tile([P, WINDOW], F32, name="h%d" % t) for t in range(PACK)]
         for t in range(PACK):
             nc.vector.memset(h[t][:, T:], 0.0)
-        for g in range(2):
-            codes, scales = deal("w1%d" % g, [w1_raw[g, 0], w1_raw[g, 1]],
-                                 [[(on_scalar, 64)], [(on_vector, 40), (on_scalar, 24)]] if g == 1 else [[(on_scalar, 44), (on_vector, 20)], [(on_vector, 64)]], PACK if g == 1 else 1, "w1b%d" % g)
+        for g in range(PASSES):
+            codes, scales = deal("w1%d" % g, w1_raw[g], w1_shares[g], w1_calls[g])
             for t in range(PACK):
                 cols = slice(t * P, (t + 1) * P)
-                nc.tensor.matmul_mx(out=accs[t][:], lhsT=codes[:, cols].bitcast(FP8X4), lhsT_scale=scales[:, cols],
-                                    rhs=x_codes[g][:].bitcast(FP8X4), rhs_scale=x_sc[4 * g :, :], start=(g == 0), stop=(g == 1))
+                nc.tensor.matmul_mx(out=h_acc[t][:], lhsT=codes[:, cols].bitcast(FP8X4), lhsT_scale=scales[:, cols],
+                                    rhs=x_codes[g][:].bitcast(FP8X4), rhs_scale=x_sc[4 * g :, :],
+                                    start=(g == 0), stop=(g == PASSES - 1))
         for t in range(PACK):
-            nc.scalar.activation(out=h[t][:, :T], in_=accs[t][:], func=SILU)
+            nc.scalar.activation(out=h[t][:, :T], in_=h_acc[t][:], func=SILU)
 
-        picked, a_q, w3_q = {}, {}, []
-        prods = [keep.tile([P, PACK, LISTS, HALF], F32, name="prod%d" % hf) for hf in range(2)]
+        terms = [keep.tile([P, PACK, LISTS, HALF], F32, name="terms%d" % hf) for hf in range(2)]
 
-        def gather(t, tag):
-            g = keep.tile([P, T], F32, name="picked%d" % t, tag=tag, align_bytes=64)
-            nc.vector.tensor_copy(g[:], h[t][:].indirect(lists[0][:]))
-            picked[t] = g
+        def gather_first_list(t, tag):
+            columns = keep.tile([P, T], F32, name="picked%d" % t, tag=tag, align_bytes=64)
+            nc.vector.tensor_copy(columns[:], h[t][:].indirect(lists[0][:]))
+            return columns
 
-        def make_a(hf, d, copy, tag):
-            grouped = keep.tile([P, 1, HALF, PACK], BF16, name="a_bf%d%d" % (hf, d), tag=tag, align_bytes=64)
-            interleave(copy, grouped[:], a_raw[hf, d][:].unsqueeze(1))
+        def quantize_a(hf, d):
+            grouped = keep.tile([P, HALF, PACK], BF16, name="a_bf%d%d" % (hf, d), align_bytes=64)
+            on_scalar(out=four_by_four(grouped[:], "p (c i) j"), in_=four_by_four(a_raw[hf, d][:], "p j (c i)"))
             codes = keep.tile([P, HALF], U32, name="a_codes%d%d" % (hf, d), align_bytes=64)
             scales = keep.tile([P, HALF], U8, name="a_sc%d%d" % (hf, d), align_bytes=64)
-            quantize(nc, codes[:], scales[:], grouped[:].rearrange("p g n j -> p (g n j)"))
-            a_q[hf, d] = (codes, scales)
+            quantize(nc, codes[:], scales[:], grouped[:].rearrange("p n j -> p (n j)"))
+            return codes, scales
 
         def filters(t, hf, d):
             cols = slice(t * P, (t + 1) * P)
-            f = psum.tile([P, HALF], F32, name="f%d%d%d" % (t, hf, d), tag=("f%d" if hf == 0 else "bank%d") % t)
+            f = psum.tile([P, HALF], F32, name="f%d%d%d" % (t, hf, d), tag=("lower%d", "upper%d")[hf] % t)
             codes, scales = a_q[hf, d]
-            nc.tensor.matmul_mx(out=f[:], lhsT=w3_q[0][:, cols].bitcast(FP8X4), lhsT_scale=w3_q[1][:, cols],
+            nc.tensor.matmul_mx(out=f[:], lhsT=w3_codes[:, cols].bitcast(FP8X4), lhsT_scale=w3_sc[:, cols],
                                 rhs=codes[:].bitcast(FP8X4), rhs_scale=scales[:], start=True, stop=True)
             return f
 
-        def product(t, hf):
+        def first_term(t, hf):
             f = filters(t, hf, 0)
-            nc.vector.tensor_tensor(out=prods[hf][:, t, 0], in0=picked[t][:, hf * HALF : (hf + 1) * HALF], in1=f[:], op=MULT)
+            nc.vector.tensor_tensor(out=terms[hf][:, t, 0], in0=picked[t][:, hf * HALF : (hf + 1) * HALF], in1=f[:], op=MULT)
 
-        def fused(t, hf, pieces):
+        def second_term(t, hf, pieces):
             f = filters(t, hf, 1)
             f_sb = keep.tile([P, HALF], F32, name="f_sb%d%d" % (t, hf))
-            nc.scalar.copy(out=f_sb[:], in_=f[:])
+            on_scalar(out=f_sb[:], in_=f[:])
             width = HALF // pieces
             for b in range(pieces):
-                v = slice(b * width, (b + 1) * width)
-                first = (hf * HALF + b * width) // 16
-                offsets = lists[1][:, first : first + width // 16]
-                nc.vector.tensor_tensor(out=prods[hf][:, t, 1, v], in0=h[t][:].indirect(offsets), in1=f_sb[:, v], op=MULT)
+                cols = slice(b * width, (b + 1) * width)
+                first = (hf * HALF + b * width) // PER_COLUMN
+                offsets = lists[1][:, first : first + width // PER_COLUMN]
+                nc.vector.tensor_tensor(out=terms[hf][:, t, 1, cols], in0=h[t][:].indirect(offsets), in1=f_sb[:, cols], op=MULT)
 
-        def finish(hf, first, width, bank, tag, sums):
+        def finish(hf, first, width, bank):
             key = "%d%d" % (hf, first // P)
             cols = slice(first, first + width)
-            grouped = keep.tile([P, width, PACK], BF16, name="z_bf" + key, tag=tag, align_bytes=64)
-            if sums is None:
-                nc.vector.tensor_tensor(out=grouped[:].rearrange("p (c i) t -> p c t i", i=PACK),
-                                        in0=prods[hf][:, :, 0, cols].rearrange("p t (c i) -> p c t i", i=PACK),
-                                        in1=prods[hf][:, :, 1, cols].rearrange("p t (c i) -> p c t i", i=PACK), op=ADD)
-            else:
-                interleave(on_scalar, grouped[:].unsqueeze(1), sums[:].unsqueeze(1))
+            grouped = keep.tile([P, width, PACK], BF16, name="z_bf" + key, align_bytes=64)
+            nc.vector.tensor_tensor(out=four_by_four(grouped[:], "p (c i) j"),
+                                    in0=four_by_four(terms[hf][:, :, 0, cols], "p j (c i)"),
+                                    in1=four_by_four(terms[hf][:, :, 1, cols], "p j (c i)"), op=ADD)
             codes = keep.tile([P, width], U32, name="z_codes" + key, align_bytes=64)
             scales = keep.tile([P, width], U8, name="z_sc" + key, align_bytes=64)
             quantize(nc, codes[:], scales[:], grouped[:].rearrange("p v t -> p (v t)"))
-            acc = psum.tile([P, N // P, width], F32, name="o_acc" + key, tag=bank)
+            acc = psum.tile([P, N // P, width], F32, name="out_acc" + key, tag=bank)
             for m in range(N // P):
                 nc.tensor.matmul_mx(out=acc[:, m], lhsT=w2_codes[:, 2 * m * P : 2 * (m + 1) * P].bitcast(FP4X4),
                                     lhsT_scale=w2_sc[:, m * P : (m + 1) * P],
@@ -185,21 +178,22 @@ def tile_picked_wdime_silu_l_kernel(tc, x_words, x_scales, aT, w1, w3, w2_words,
             at = hf * HALF + first
             nc.sync.dma_start(out=out[:, at : at + width].rearrange("(m p) v -> p m v", p=P), in_=res[:])
 
-        w3_q.extend(deal("w3", w3_raw, [[(on_vector, 64)], [(on_scalar, 64)]], 1, "w3b"))
-        for t in range(PACK - 1):
-            gather(t, "g%d" % t)
-        make_a(0, 0, on_scalar, "a00")
-        gather(3, "a00")
-        make_a(1, 0, on_scalar, "a10")
-        make_a(0, 1, on_scalar, "a01")
-        make_a(1, 1, on_scalar, "a11")
+        w3_codes, w3_sc = deal("w3", w3_raw, [whole_on_vector, whole_on_scalar], 1)
+
+        last = PACK - 1
+        picked = [gather_first_list(t, "picked%d" % t) for t in range(last)]
+        a_q = {(0, 0): quantize_a(0, 0)}
+        picked.append(gather_first_list(last, "a_bf00"))
+        for hf, d in ((1, 0), (0, 1), (1, 1)):
+            a_q[hf, d] = quantize_a(hf, d)
+
         for hf in range(2):
             for t in range(PACK):
-                product(t, hf)
+                first_term(t, hf)
         for t in range(PACK):
-            fused(t, 0, 1)
-        finish(0, 0, HALF, "f0", "z0", None)
+            second_term(t, 0, 1)
+        finish(0, 0, HALF, "lower0")
         for t in range(PACK):
-            fused(t, 1, 2 if t == PACK - 1 else 1)
-        finish(1, 0, P, "f1", "z10", None)
-        finish(1, P, P, "f2", "z11", None)
+            second_term(t, 1, HALF // P if t == last else 1)
+        for b in range(HALF // P):
+            finish(1, b * P, P, "lower%d" % (b + 1))

@@ -53,13 +53,13 @@ def tile_picked_wdime_silu_l_kernel(tc, x_words, x_scales, aT, w1, w3, w2_words,
         nc.vector.memset(x_sc[:].bitcast(I32), 0)
         nc.vector.memset(w2_sc[:].bitcast(I32), 0)
 
-        def load_cols(name, src, first):
-            raw = keep.tile([P, PACK, HALF], F32, name=name)
-            nc.sync.dma_start(out=raw[:], in_=src[:, first : first + HALF].rearrange("(p j) n -> p j n", j=PACK))
+        def load_cols(name, src, first, width):
+            raw = keep.tile([P, PACK, width], F32, name=name)
+            nc.sync.dma_start(out=raw[:], in_=src[:, first : first + width].rearrange("(p j) n -> p j n", j=PACK))
             return raw
 
         def load_w1(g):
-            return [load_cols("w1_raw%d%d" % (g, s), w1[g * K_PASS : (g + 1) * K_PASS], s * HALF) for s in range(2)]
+            return load_cols("w1_raw%d" % g, w1[g * K_PASS : (g + 1) * K_PASS], 0, H)
 
         def load_x(g):
             nc.sync.dma_start(out=x_codes[g][:].bitcast(I32), in_=x_words[g].rearrange("p n j -> p (n j)").bitcast(I32))
@@ -71,54 +71,58 @@ def tile_picked_wdime_silu_l_kernel(tc, x_words, x_scales, aT, w1, w3, w2_words,
         load_x(0)
         w1_raw.append(load_w1(1))
         load_x(1)
-        w3_raw = [load_cols("w3_raw0", w3, 0)]
+        w3_raw = [load_cols("w3_raw0", w3, 0, HALF)]
         nc.sync.dma_start(lists[0][:], pos1)
-        w3_raw.append(load_cols("w3_raw1", w3, HALF))
+        w3_raw.append(load_cols("w3_raw1", w3, HALF, HALF))
         nc.sync.dma_start(lists[1][:], pos2)
-        a_raw = {(hf, d): load_cols("a_raw%d%d" % (hf, d), aT, d * T + hf * HALF) for d in range(LISTS) for hf in range(2)}
+        a_raw = [load_cols("a_raw%d" % d, aT, d * T, T) for d in range(LISTS)]
         nc.sync.dma_start(out=w2_codes[:].bitcast(I32), in_=w2_words[0].bitcast(I32))
         for q in range(QUADRANTS):
             nc.sync.dma_start(out=w2_sc[32 * q : 32 * q + 4].bitcast(I32),
                               in_=w2_scales[0, 4 * q : 4 * q + 4, :].bitcast(I32))
 
-        def deal(name, raws, shares, calls):
+        def deal(name, steps):
             grouped = keep.tile([P, PACK, P, PACK], BF16, name=name + "_bf", align_bytes=64)
-            for s, raw in enumerate(raws):
-                src = raw[:].rearrange("p j (m t) -> p m j t", t=PACK)
-                for copy, words, tiles in shares[s]:
-                    dst = grouped[:, tiles, s * HALF_WORDS : (s + 1) * HALF_WORDS][:, :, words]
-                    copy(out=dst.rearrange("p t m j -> p m j t"), in_=src[:, words, :, tiles])
             codes = keep.tile([P, H], U32, name=name + "_codes", align_bytes=64)
             scales = keep.tile([P, H], U8, name=name + "_sc", align_bytes=64)
-            per_call = PACK // calls
-            for s in range(calls):
-                cols = slice(s * per_call * P, (s + 1) * per_call * P)
-                quantize(nc, codes[:, cols], scales[:, cols],
-                         grouped[:, s * per_call : (s + 1) * per_call].rearrange("p t m j -> p (t m j)"))
+            for step in steps:
+                if isinstance(step, slice):
+                    cols = slice(step.start * P, step.stop * P)
+                    quantize(nc, codes[:, cols], scales[:, cols], grouped[:, step].rearrange("p t m j -> p (t m j)"))
+                else:
+                    copy, raw, first, words, tiles = step
+                    src = raw[:].rearrange("p j (m t) -> p m j t", t=PACK)
+                    copy(out=grouped[:, tiles, words].rearrange("p t m j -> p m j t"),
+                         in_=src[:, words.start - first : words.stop - first, :, tiles])
             return codes, scales
 
-        all_words, all_tiles = slice(0, HALF_WORDS), slice(0, PACK)
-        whole_on_vector = [(on_vector, all_words, all_tiles)]
-        whole_on_scalar = [(on_scalar, all_words, all_tiles)]
-        tile_0_first = [(on_vector, all_words, slice(0, 1)),
-                        (on_vector, slice(0, VECTOR_WORDS), slice(1, PACK)),
-                        (on_scalar, slice(VECTOR_WORDS, HALF_WORDS), slice(1, PACK))]
-        w1_shares = [[whole_on_scalar, whole_on_vector], [whole_on_scalar, tile_0_first]]
-        w1_calls = [1, PACK]
+        all_tiles, rest = slice(0, PACK), slice(1, PACK)
+        w1_steps = [
+            [(on_vector, w1_raw[0], 0, slice(0, 84), all_tiles), (on_scalar, w1_raw[0], 0, slice(84, P), all_tiles),
+             slice(0, 2), slice(2, PACK)],
+            [(on_vector, w1_raw[1], 0, slice(0, 84), slice(0, 1)), (on_scalar, w1_raw[1], 0, slice(84, P), slice(0, 1)),
+             slice(0, 1),
+             (on_vector, w1_raw[1], 0, slice(0, 36), rest), (on_vector, w1_raw[1], 0, slice(36, 72), rest),
+             (on_scalar, w1_raw[1], 0, slice(72, P), rest), slice(1, 2), slice(2, 3), slice(3, 4)],
+        ]
 
-        h_acc = [psum.tile([P, T], F32, name="h_acc%d" % t, tag="upper%d" % t) for t in range(PACK)]
+        h_parts = [(0, slice(0, HALF), "upper0"), (0, slice(HALF, T), "lower0")]
+        h_parts.extend((t, slice(0, T), "upper%d" % t) for t in range(1, PACK))
+        h_acc = [psum.tile([P, edges.stop - edges.start], F32, name="h_acc%d" % n, tag=bank)
+                 for n, (t, edges, bank) in enumerate(h_parts)]
         h = [keep.tile([P, WINDOW], F32, name="h%d" % t) for t in range(PACK)]
-        for t in range(PACK):
+        for t in (0, 2, 3):
             nc.vector.memset(h[t][:, T:], 0.0)
+        nc.scalar.activation(out=h[1][:, T:], in_=h[0][:, T:], func=SILU)
         for g in range(PASSES):
-            codes, scales = deal("w1%d" % g, w1_raw[g], w1_shares[g], w1_calls[g])
-            for t in range(PACK):
+            codes, scales = deal("w1%d" % g, w1_steps[g])
+            for acc, (t, edges, bank) in zip(h_acc, h_parts):
                 cols = slice(t * P, (t + 1) * P)
-                nc.tensor.matmul_mx(out=h_acc[t][:], lhsT=codes[:, cols].bitcast(FP8X4), lhsT_scale=scales[:, cols],
-                                    rhs=x_codes[g][:].bitcast(FP8X4), rhs_scale=x_sc[4 * g :, :],
+                nc.tensor.matmul_mx(out=acc[:], lhsT=codes[:, cols].bitcast(FP8X4), lhsT_scale=scales[:, cols],
+                                    rhs=x_codes[g][:, edges].bitcast(FP8X4), rhs_scale=x_sc[4 * g :, edges],
                                     start=(g == 0), stop=(g == PASSES - 1))
-        for t in range(PACK):
-            nc.scalar.activation(out=h[t][:, :T], in_=h_acc[t][:], func=SILU)
+        for acc, (t, edges, bank) in zip(h_acc, h_parts):
+            nc.scalar.activation(out=h[t][:, edges], in_=acc[:], func=SILU)
 
         terms = [keep.tile([P, PACK, LISTS, HALF], F32, name="terms%d" % hf) for hf in range(2)]
 
@@ -129,7 +133,7 @@ def tile_picked_wdime_silu_l_kernel(tc, x_words, x_scales, aT, w1, w3, w2_words,
 
         def quantize_a(hf, d):
             grouped = keep.tile([P, HALF, PACK], BF16, name="a_bf%d%d" % (hf, d), align_bytes=64)
-            on_scalar(out=four_by_four(grouped[:], "p (c i) j"), in_=four_by_four(a_raw[hf, d][:], "p j (c i)"))
+            on_scalar(out=four_by_four(grouped[:], "p (c i) j"), in_=four_by_four(a_raw[d][:, :, hf * HALF : (hf + 1) * HALF], "p j (c i)"))
             codes = keep.tile([P, HALF], U32, name="a_codes%d%d" % (hf, d), align_bytes=64)
             scales = keep.tile([P, HALF], U8, name="a_sc%d%d" % (hf, d), align_bytes=64)
             quantize(nc, codes[:], scales[:], grouped[:].rearrange("p n j -> p (n j)"))
@@ -178,7 +182,8 @@ def tile_picked_wdime_silu_l_kernel(tc, x_words, x_scales, aT, w1, w3, w2_words,
             at = hf * HALF + first
             nc.sync.dma_start(out=out[:, at : at + width].rearrange("(m p) v -> p m v", p=P), in_=res[:])
 
-        w3_codes, w3_sc = deal("w3", w3_raw, [whole_on_vector, whole_on_scalar], 1)
+        w3_codes, w3_sc = deal("w3", [(on_vector, w3_raw[0], 0, slice(0, HALF_WORDS), all_tiles),
+                                       (on_scalar, w3_raw[1], HALF_WORDS, slice(HALF_WORDS, P), all_tiles), all_tiles])
 
         last = PACK - 1
         picked = [gather_first_list(t, "picked%d" % t) for t in range(last)]

@@ -1,6 +1,7 @@
 from contextlib import ExitStack
 
 import concourse.mybir as mybir
+from concourse.masks import make_identity
 
 K, T, H, N, J = 1024, 512, 512, 256, 512
 FLOPS = 2 * (K * H * T + J * H * 2 * T + H * N * T)
@@ -53,6 +54,9 @@ def tile_picked_wdime_silu_l_kernel(tc, x_words, x_scales, aT, w1, w3, w2_words,
         nc.vector.memset(x_sc[:].bitcast(I32), 0)
         nc.vector.memset(w2_sc[:].bitcast(I32), 0)
 
+        identity = keep.tile([P, P], F32)
+        make_identity(nc, identity[:])
+
         def load_cols(name, src, first, width):
             raw = keep.tile([P, PACK, width], F32, name=name)
             nc.sync.dma_start(out=raw[:], in_=src[:, first : first + width].rearrange("(p j) n -> p j n", j=PACK))
@@ -75,7 +79,10 @@ def tile_picked_wdime_silu_l_kernel(tc, x_words, x_scales, aT, w1, w3, w2_words,
         nc.sync.dma_start(lists[0][:], pos1)
         w3_raw.append(load_cols("w3_raw1", w3, HALF, HALF))
         nc.sync.dma_start(lists[1][:], pos2)
-        a_raw = [load_cols("a_raw%d" % d, aT, d * T, T) for d in range(LISTS)]
+        a_first = load_cols("a_raw0", aT, 0, T)
+        a_raw = {(hf, 0): a_first[:, :, hf * HALF : (hf + 1) * HALF] for hf in range(2)}
+        for hf in range(2):
+            a_raw[hf, 1] = load_cols("a_raw1%d" % hf, aT, T + hf * HALF, HALF)[:]
         nc.sync.dma_start(out=w2_codes[:].bitcast(I32), in_=w2_words[0].bitcast(I32))
         for q in range(QUADRANTS):
             nc.sync.dma_start(out=w2_sc[32 * q : 32 * q + 4].bitcast(I32),
@@ -124,7 +131,10 @@ def tile_picked_wdime_silu_l_kernel(tc, x_words, x_scales, aT, w1, w3, w2_words,
         for acc, (t, edges, bank) in zip(h_acc, h_parts):
             nc.scalar.activation(out=h[t][:, edges], in_=acc[:], func=SILU)
 
-        terms = [keep.tile([P, PACK, LISTS, HALF], F32, name="terms%d" % hf) for hf in range(2)]
+        terms = {}
+
+        def term_tile(d, hf, tag):
+            terms[d, hf] = keep.tile([P, PACK, HALF], F32, name="terms%d%d" % (d, hf), tag=tag, align_bytes=64)
 
         def gather_first_list(t, tag):
             columns = keep.tile([P, T], F32, name="picked%d" % t, tag=tag, align_bytes=64)
@@ -133,45 +143,67 @@ def tile_picked_wdime_silu_l_kernel(tc, x_words, x_scales, aT, w1, w3, w2_words,
 
         def quantize_a(hf, d):
             grouped = keep.tile([P, HALF, PACK], BF16, name="a_bf%d%d" % (hf, d), align_bytes=64)
-            on_scalar(out=four_by_four(grouped[:], "p (c i) j"), in_=four_by_four(a_raw[d][:, :, hf * HALF : (hf + 1) * HALF], "p j (c i)"))
+            on_scalar(out=four_by_four(grouped[:], "p (c i) j"), in_=four_by_four(a_raw[hf, d], "p j (c i)"))
             codes = keep.tile([P, HALF], U32, name="a_codes%d%d" % (hf, d), align_bytes=64)
             scales = keep.tile([P, HALF], U8, name="a_sc%d%d" % (hf, d), align_bytes=64)
             quantize(nc, codes[:], scales[:], grouped[:].rearrange("p n j -> p (n j)"))
             return codes, scales
 
-        def filters(t, hf, d):
+        def filters(f, t, hf, d):
             cols = slice(t * P, (t + 1) * P)
-            f = psum.tile([P, HALF], F32, name="f%d%d%d" % (t, hf, d), tag=("lower%d", "upper%d")[hf] % t)
             codes, scales = a_q[hf, d]
-            nc.tensor.matmul_mx(out=f[:], lhsT=w3_codes[:, cols].bitcast(FP8X4), lhsT_scale=w3_sc[:, cols],
+            nc.tensor.matmul_mx(out=f, lhsT=w3_codes[:, cols].bitcast(FP8X4), lhsT_scale=w3_sc[:, cols],
                                 rhs=codes[:].bitcast(FP8X4), rhs_scale=scales[:], start=True, stop=True)
-            return f
 
-        def first_term(t, hf):
-            f = filters(t, hf, 0)
-            nc.vector.tensor_tensor(out=terms[hf][:, t, 0], in0=picked[t][:, hf * HALF : (hf + 1) * HALF], in1=f[:], op=MULT)
+        def first_term(f, t, hf):
+            nc.vector.tensor_tensor(out=terms[0, hf][:, t], in0=picked[t][:, hf * HALF : (hf + 1) * HALF], in1=f, op=MULT)
 
-        def second_term(t, hf, pieces):
-            f = filters(t, hf, 1)
-            f_sb = keep.tile([P, HALF], F32, name="f_sb%d%d" % (t, hf))
+        def second_filters(pair, hf, bank):
+            f = psum.tile([P, 2, HALF], F32, name="f1_%d%d" % (pair, hf), tag=bank)
+            for e in range(2):
+                filters(f[:, e], 2 * pair + e, hf, 1)
+            f_sb = keep.tile([P, 2, HALF], F32, name="f_sb%d%d" % (pair, hf), align_bytes=64)
             on_scalar(out=f_sb[:], in_=f[:])
-            width = HALF // pieces
-            for b in range(pieces):
-                cols = slice(b * width, (b + 1) * width)
-                first = (hf * HALF + b * width) // PER_COLUMN
-                offsets = lists[1][:, first : first + width // PER_COLUMN]
-                nc.vector.tensor_tensor(out=terms[hf][:, t, 1, cols], in0=h[t][:].indirect(offsets), in1=f_sb[:, cols], op=MULT)
+            return f_sb
 
-        def finish(hf, first, width, bank):
-            key = "%d%d" % (hf, first // P)
+        def second_term(t, hf, first, width):
             cols = slice(first, first + width)
-            grouped = keep.tile([P, width, PACK], BF16, name="z_bf" + key, align_bytes=64)
+            at = (hf * HALF + first) // PER_COLUMN
+            offsets = lists[1][:, at : at + width // PER_COLUMN]
+            nc.vector.tensor_tensor(out=(early[t] if hf == 0 else terms[1, 1][:, t])[:, cols], in0=h[t][:].indirect(offsets),
+                                    in1=f1[hf][t // 2][:, t % 2, cols], op=MULT)
+
+        def turn(t, d):
+            for b, acc in enumerate(sums):
+                nc.tensor.matmul(acc[:, t], lhsT=(early[t] if d else terms[0, 0][:, t])[:, b * P : (b + 1) * P], rhs=identity[:],
+                                 is_transpose=True, start=(t == 0 and d == 0), stop=(t == last and d == LISTS - 1))
+
+        def turn_back(key, sums, bank):
+            blocks = len(sums)
+            back = psum.tile([P, blocks, 2, P], F32, name="back" + key, tag=bank)
+            for b, acc in enumerate(sums):
+                rounded = keep.tile([P, 2, P, 2], BF16, name="zt_bf%s%d" % (key, b))
+                on_scalar(out=rounded[:], in_=acc[:].rearrange("v (u e) p -> v u p e", e=2))
+                words = rounded[:].rearrange("v u p e -> v (u p e)").bitcast(F32)
+                for u in range(2):
+                    nc.tensor.transpose(back[:, b, u], words[:, u * P : (u + 1) * P], identity[:])
+            grouped = keep.tile([P, blocks * P * PACK], BF16, name="z_bf" + key, align_bytes=64)
+            on_scalar(out=grouped[:].bitcast(F32).rearrange("p (b v u) -> p b v u", b=blocks, u=2),
+                      in_=back[:].rearrange("p b u v -> p b v u"))
+            return grouped[:]
+
+        def add_on_vector(key, hf, first, width, tag):
+            cols = slice(first, first + width)
+            grouped = keep.tile([P, width, PACK], BF16, name="z_bf" + key, tag=tag, align_bytes=64)
             nc.vector.tensor_tensor(out=four_by_four(grouped[:], "p (c i) j"),
-                                    in0=four_by_four(terms[hf][:, :, 0, cols], "p j (c i)"),
-                                    in1=four_by_four(terms[hf][:, :, 1, cols], "p j (c i)"), op=ADD)
+                                    in0=four_by_four(terms[0, hf][:, :, cols], "p j (c i)"),
+                                    in1=four_by_four(terms[1, hf][:, :, cols], "p j (c i)"), op=ADD)
+            return grouped[:].rearrange("p v t -> p (v t)")
+
+        def finish(key, grouped, at, width, bank):
             codes = keep.tile([P, width], U32, name="z_codes" + key, align_bytes=64)
             scales = keep.tile([P, width], U8, name="z_sc" + key, align_bytes=64)
-            quantize(nc, codes[:], scales[:], grouped[:].rearrange("p v t -> p (v t)"))
+            quantize(nc, codes[:], scales[:], grouped)
             acc = psum.tile([P, N // P, width], F32, name="out_acc" + key, tag=bank)
             for m in range(N // P):
                 nc.tensor.matmul_mx(out=acc[:, m], lhsT=w2_codes[:, 2 * m * P : 2 * (m + 1) * P].bitcast(FP4X4),
@@ -179,7 +211,6 @@ def tile_picked_wdime_silu_l_kernel(tc, x_words, x_scales, aT, w1, w3, w2_words,
                                     rhs=codes[:].bitcast(FP8X4), rhs_scale=scales[:], start=True, stop=True)
             res = keep.tile([P, N // P, width], F32, name="res" + key)
             nc.scalar.activation(out=res[:], in_=acc[:], func=SILU)
-            at = hf * HALF + first
             nc.sync.dma_start(out=out[:, at : at + width].rearrange("(m p) v -> p m v", p=P), in_=res[:])
 
         w3_codes, w3_sc = deal("w3", [(on_vector, w3_raw[0], 0, slice(0, HALF_WORDS), all_tiles),
@@ -189,16 +220,39 @@ def tile_picked_wdime_silu_l_kernel(tc, x_words, x_scales, aT, w1, w3, w2_words,
         picked = [gather_first_list(t, "picked%d" % t) for t in range(last)]
         a_q = {(0, 0): quantize_a(0, 0)}
         picked.append(gather_first_list(last, "a_bf00"))
-        for hf, d in ((1, 0), (0, 1), (1, 1)):
+        for hf, d in ((0, 1), (1, 0), (1, 1)):
             a_q[hf, d] = quantize_a(hf, d)
 
-        for hf in range(2):
-            for t in range(PACK):
-                first_term(t, hf)
+        term_tile(0, 0, "a_bf01")
+        early = [keep.tile([P, HALF], F32, name="early%d" % t, tag="a_bf11" if t == last else "early%d" % t, align_bytes=64)
+                 for t in range(PACK)]
+        term_tile(1, 1, "terms11")
+        f0_early = [psum.tile([P, HALF], F32, name="f0_early%d" % t, tag="lower%d" % t) for t in range(PACK)]
+        f0_late = [psum.tile([P, 2, HALF], F32, name="f0_late%d" % pair, tag="upper%d" % pair) for pair in range(2)]
         for t in range(PACK):
-            second_term(t, 0, 1)
-        finish(0, 0, HALF, "lower0")
+            filters(f0_early[t][:], t, 0, 0)
+        f1 = [[second_filters(pair, 0, "upper%d" % (2 + pair)) for pair in range(2)]]
         for t in range(PACK):
-            second_term(t, 1, HALF // P if t == last else 1)
-        for b in range(HALF // P):
-            finish(1, b * P, P, "lower%d" % (b + 1))
+            filters(f0_late[t // 2][:, t % 2], t, 1, 0)
+        for t in range(PACK):
+            first_term(f0_early[t][:], t, 0)
+        f1.append([second_filters(pair, 1, "lower%d" % (2 + pair)) for pair in range(2)])
+        sums = [psum.tile([P, PACK, P], F32, name="zt%d" % b, tag="lower%d" % b) for b in range(2)]
+        for t in range(PACK):
+            turn(t, 0)
+        for t in range(PACK):
+            second_term(t, 0, 0, HALF)
+            turn(t, 1)
+        z_first = turn_back("0", sums, "upper2")
+        term_tile(0, 1, "f_sb00")
+        for t in range(PACK):
+            first_term(f0_late[t // 2][:, t % 2], t, 1)
+        for t in range(last):
+            second_term(t, 1, 0, HALF)
+        for b in range(2):
+            second_term(last, 1, b * P, P)
+        finish("0", z_first, 0, HALF, "upper3")
+        z_third = add_on_vector("2", 1, 0, P, "z_bf0")
+        z_last = add_on_vector("3", 1, P, P, "z_bf3")
+        finish("2", z_third, HALF, P, "lower2")
+        finish("3", z_last, HALF + P, P, "lower3")

@@ -58,7 +58,7 @@ def tile_picked_wdime_silu_l_kernel(tc, x_words, x_scales, aT, w1, w3, w2_words,
         make_identity(nc, identity[:])
 
         def load_cols(name, src, first, width):
-            raw = keep.tile([P, PACK, width], F32, name=name)
+            raw = keep.tile([P, PACK, width], F32, name=name, align_bytes=64)
             nc.sync.dma_start(out=raw[:], in_=src[:, first : first + width].rearrange("(p j) n -> p j n", j=PACK))
             return raw
 
@@ -142,7 +142,8 @@ def tile_picked_wdime_silu_l_kernel(tc, x_words, x_scales, aT, w1, w3, w2_words,
             return columns
 
         def quantize_a(hf, d):
-            grouped = keep.tile([P, HALF, PACK], BF16, name="a_bf%d%d" % (hf, d), align_bytes=64)
+            name = "a_bf%d%d" % (hf, d)
+            grouped = keep.tile([P, HALF, PACK], BF16, name=name, tag="a_raw10" if (hf, d) == (1, 0) else name, align_bytes=64)
             on_scalar(out=four_by_four(grouped[:], "p (c i) j"), in_=four_by_four(a_raw[hf, d], "p j (c i)"))
             codes = keep.tile([P, HALF], U32, name="a_codes%d%d" % (hf, d), align_bytes=64)
             scales = keep.tile([P, HALF], U8, name="a_sc%d%d" % (hf, d), align_bytes=64)
@@ -166,17 +167,16 @@ def tile_picked_wdime_silu_l_kernel(tc, x_words, x_scales, aT, w1, w3, w2_words,
             on_scalar(out=f_sb[:], in_=f[:])
             return f_sb
 
-        def second_term(t, hf, first, width):
+        def second_term(dst, t, hf, first, width):
             cols = slice(first, first + width)
             at = (hf * HALF + first) // PER_COLUMN
             offsets = lists[1][:, at : at + width // PER_COLUMN]
-            nc.vector.tensor_tensor(out=(early[t] if hf == 0 else terms[1, 1][:, t])[:, cols], in0=h[t][:].indirect(offsets),
+            nc.vector.tensor_tensor(out=dst, in0=h[t][:].indirect(offsets),
                                     in1=f1[hf][t // 2][:, t % 2, cols], op=MULT)
 
-        def turn(t, d):
-            for b, acc in enumerate(sums):
-                nc.tensor.matmul(acc[:, t], lhsT=(early[t] if d else terms[0, 0][:, t])[:, b * P : (b + 1) * P], rhs=identity[:],
-                                 is_transpose=True, start=(t == 0 and d == 0), stop=(t == last and d == LISTS - 1))
+        def turn(acc, src, t, d):
+            nc.tensor.matmul(acc[:, t], lhsT=src, rhs=identity[:], is_transpose=True,
+                             start=(t == 0 and d == 0), stop=(t == last and d == LISTS - 1))
 
         def turn_back(key, sums, bank):
             blocks = len(sums)
@@ -197,7 +197,7 @@ def tile_picked_wdime_silu_l_kernel(tc, x_words, x_scales, aT, w1, w3, w2_words,
             grouped = keep.tile([P, width, PACK], BF16, name="z_bf" + key, tag=tag, align_bytes=64)
             nc.vector.tensor_tensor(out=four_by_four(grouped[:], "p (c i) j"),
                                     in0=four_by_four(terms[0, hf][:, :, cols], "p j (c i)"),
-                                    in1=four_by_four(terms[1, hf][:, :, cols], "p j (c i)"), op=ADD)
+                                    in1=four_by_four(fourth[:], "p j (c i)"), op=ADD)
             return grouped[:].rearrange("p v t -> p (v t)")
 
         def finish(key, grouped, at, width, bank):
@@ -226,7 +226,6 @@ def tile_picked_wdime_silu_l_kernel(tc, x_words, x_scales, aT, w1, w3, w2_words,
         term_tile(0, 0, "a_bf01")
         early = [keep.tile([P, HALF], F32, name="early%d" % t, tag="a_bf11" if t == last else "early%d" % t, align_bytes=64)
                  for t in range(PACK)]
-        term_tile(1, 1, "terms11")
         f0_early = [psum.tile([P, HALF], F32, name="f0_early%d" % t, tag="lower%d" % t) for t in range(PACK)]
         f0_late = [psum.tile([P, 2, HALF], F32, name="f0_late%d" % pair, tag="upper%d" % pair) for pair in range(2)]
         for t in range(PACK):
@@ -239,20 +238,28 @@ def tile_picked_wdime_silu_l_kernel(tc, x_words, x_scales, aT, w1, w3, w2_words,
         f1.append([second_filters(pair, 1, "lower%d" % (2 + pair)) for pair in range(2)])
         sums = [psum.tile([P, PACK, P], F32, name="zt%d" % b, tag="lower%d" % b) for b in range(2)]
         for t in range(PACK):
-            turn(t, 0)
+            for b in range(2):
+                turn(sums[b], terms[0, 0][:, t, b * P : (b + 1) * P], t, 0)
         for t in range(PACK):
-            second_term(t, 0, 0, HALF)
-            turn(t, 1)
-        z_first = turn_back("0", sums, "upper2")
+            second_term(early[t][:], t, 0, 0, HALF)
+            for b in range(2):
+                turn(sums[b], early[t][:, b * P : (b + 1) * P], t, 1)
+        z = [turn_back("%d" % b, [sums[b]], "upper%d" % (2 + b)) for b in range(2)]
         term_tile(0, 1, "f_sb00")
+        sums.append(psum.tile([P, PACK, P], F32, name="zt2", tag="lower1"))
         for t in range(PACK):
             first_term(f0_late[t // 2][:, t % 2], t, 1)
-        for t in range(last):
-            second_term(t, 1, 0, HALF)
-        for b in range(2):
-            second_term(last, 1, b * P, P)
-        finish("0", z_first, 0, HALF, "upper3")
-        z_third = add_on_vector("2", 1, 0, P, "z_bf0")
-        z_last = add_on_vector("3", 1, P, P, "z_bf3")
-        finish("2", z_third, HALF, P, "lower2")
-        finish("3", z_last, HALF + P, P, "lower3")
+            turn(sums[2], terms[0, 1][:, t, :P], t, 0)
+        third = keep.tile([P, PACK, P], F32)
+        for t in range(PACK):
+            second_term(third[:, t], t, 1, 0, P)
+            turn(sums[2], third[:, t], t, 1)
+        z.append(turn_back("2", [sums[2]], "upper0"))
+        finish("0", z[0], 0, P, "lower0")
+        fourth = keep.tile([P, PACK, P], F32, tag="z_bf0", align_bytes=64)
+        for t in range(PACK):
+            second_term(fourth[:, t], t, 1, P, P)
+        finish("1", z[1], P, P, "lower1")
+        z.append(add_on_vector("3", 1, P, P, "z_bf1"))
+        finish("2", z[2], HALF, P, "lower2")
+        finish("3", z[3], HALF + P, P, "lower3")

@@ -48,7 +48,7 @@ def tile_picked_wdime_silu_l_kernel(tc, x_words, x_scales, aT, w1, w3, w2_words,
 
         lists = [keep.tile([P, T // PER_COLUMN], U16, name="pos%d" % d) for d in range(LISTS)]
         x_codes = [keep.tile([P, T], U32, name="x_codes%d" % g, align_bytes=64) for g in range(PASSES)]
-        x_sc = keep.tile([P, T], U8, align_bytes=64)
+        x_sc = keep.tile([P, PASSES * T], U8, align_bytes=64)
         w2_codes = keep.tile([P, 2 * N], U8, align_bytes=64)
         w2_sc = keep.tile([P, N], U8, align_bytes=64)
         nc.vector.memset(x_sc[:].bitcast(I32), 0)
@@ -69,20 +69,22 @@ def tile_picked_wdime_silu_l_kernel(tc, x_words, x_scales, aT, w1, w3, w2_words,
             nc.sync.dma_start(out=x_codes[g][:].bitcast(I32), in_=x_words[g].rearrange("p n j -> p (n j)").bitcast(I32))
 
         w1_raw = [load_w1(0)]
-        for q in range(QUADRANTS):
-            nc.sync.dma_start(out=x_sc[32 * q : 32 * q + 4 * PASSES].bitcast(I32),
-                              in_=x_scales[:, 4 * q : 4 * q + 4, :].bitcast(I32))
+        def load_x_scales(g):
+            for q in range(QUADRANTS):
+                nc.sync.dma_start(out=x_sc[32 * q : 32 * q + 4, g * T : (g + 1) * T].bitcast(I32),
+                                  in_=x_scales[g, 4 * q : 4 * q + 4, :].bitcast(I32))
+
+        load_x_scales(0)
         load_x(0)
         w1_raw.append(load_w1(1))
         load_x(1)
+        load_x_scales(1)
         w3_raw = [load_cols("w3_raw0", w3, 0, HALF)]
         nc.sync.dma_start(lists[0][:], pos1)
         w3_raw.append(load_cols("w3_raw1", w3, HALF, HALF))
         nc.sync.dma_start(lists[1][:], pos2)
-        a_first = load_cols("a_raw0", aT, 0, T)
-        a_raw = {(hf, 0): a_first[:, :, hf * HALF : (hf + 1) * HALF] for hf in range(2)}
-        for hf in range(2):
-            a_raw[hf, 1] = load_cols("a_raw1%d" % hf, aT, T + hf * HALF, HALF)[:]
+        a_raw = {(hf, d): load_cols("a_raw%d%d" % (hf, d), aT, d * T + hf * HALF, HALF)[:]
+                 for hf, d in ((0, 0), (0, 1), (1, 0), (1, 1))}
         nc.sync.dma_start(out=w2_codes[:].bitcast(I32), in_=w2_words[0].bitcast(I32))
         for q in range(QUADRANTS):
             nc.sync.dma_start(out=w2_sc[32 * q : 32 * q + 4].bitcast(I32),
@@ -126,7 +128,7 @@ def tile_picked_wdime_silu_l_kernel(tc, x_words, x_scales, aT, w1, w3, w2_words,
             for acc, (t, edges, bank) in zip(h_acc, h_parts):
                 cols = slice(t * P, (t + 1) * P)
                 nc.tensor.matmul_mx(out=acc[:], lhsT=codes[:, cols].bitcast(FP8X4), lhsT_scale=scales[:, cols],
-                                    rhs=x_codes[g][:, edges].bitcast(FP8X4), rhs_scale=x_sc[4 * g :, edges],
+                                    rhs=x_codes[g][:, edges].bitcast(FP8X4), rhs_scale=x_sc[:, g * T + edges.start : g * T + edges.stop],
                                     start=(g == 0), stop=(g == PASSES - 1))
         for acc, (t, edges, bank) in zip(h_acc, h_parts):
             nc.scalar.activation(out=h[t][:, edges], in_=acc[:], func=SILU)
@@ -143,7 +145,7 @@ def tile_picked_wdime_silu_l_kernel(tc, x_words, x_scales, aT, w1, w3, w2_words,
 
         def quantize_a(hf, d):
             name = "a_bf%d%d" % (hf, d)
-            grouped = keep.tile([P, HALF, PACK], BF16, name=name, tag="a_raw10" if (hf, d) == (1, 0) else name, align_bytes=64)
+            grouped = keep.tile([P, HALF, PACK], BF16, name=name, align_bytes=64)
             on_scalar(out=four_by_four(grouped[:], "p (c i) j"), in_=four_by_four(a_raw[hf, d], "p j (c i)"))
             codes = keep.tile([P, HALF], U32, name="a_codes%d%d" % (hf, d), align_bytes=64)
             scales = keep.tile([P, HALF], U8, name="a_sc%d%d" % (hf, d), align_bytes=64)
@@ -163,7 +165,8 @@ def tile_picked_wdime_silu_l_kernel(tc, x_words, x_scales, aT, w1, w3, w2_words,
             f = psum.tile([P, 2, HALF], F32, name="f1_%d%d" % (pair, hf), tag=bank)
             for e in range(2):
                 filters(f[:, e], 2 * pair + e, hf, 1)
-            f_sb = keep.tile([P, 2, HALF], F32, name="f_sb%d%d" % (pair, hf), align_bytes=64)
+            f_sb = keep.tile([P, 2, HALF], F32, name="f_sb%d%d" % (pair, hf), align_bytes=64,
+                             tag=("a_raw11", "a_bf11")[pair] if hf == 0 else "f_sb%d%d" % (pair, hf))
             on_scalar(out=f_sb[:], in_=f[:])
             return f_sb
 
@@ -224,7 +227,7 @@ def tile_picked_wdime_silu_l_kernel(tc, x_words, x_scales, aT, w1, w3, w2_words,
             a_q[hf, d] = quantize_a(hf, d)
 
         term_tile(0, 0, "a_bf01")
-        early = [keep.tile([P, HALF], F32, name="early%d" % t, tag="a_bf11" if t == last else "early%d" % t, align_bytes=64)
+        early = [keep.tile([P, HALF], F32, name="early%d" % t, align_bytes=64)
                  for t in range(PACK)]
         f0_early = [psum.tile([P, HALF], F32, name="f0_early%d" % t, tag="lower%d" % t) for t in range(PACK)]
         f0_late = [psum.tile([P, 2, HALF], F32, name="f0_late%d" % pair, tag="upper%d" % pair) for pair in range(2)]
@@ -245,7 +248,7 @@ def tile_picked_wdime_silu_l_kernel(tc, x_words, x_scales, aT, w1, w3, w2_words,
             for b in range(2):
                 turn(sums[b], early[t][:, b * P : (b + 1) * P], t, 1)
         z = [turn_back("%d" % b, [sums[b]], "upper%d" % (2 + b)) for b in range(2)]
-        term_tile(0, 1, "f_sb00")
+        term_tile(0, 1, "a_raw11")
         sums.append(psum.tile([P, PACK, P], F32, name="zt2", tag="lower1"))
         for t in range(PACK):
             first_term(f0_late[t // 2][:, t % 2], t, 1)

@@ -20,15 +20,16 @@ MULT = mybir.AluOpType.mult
 
 P = 128
 PACK = 4
+LAST = PACK - 1
 K_PASS = P * PACK
 PASSES = K // K_PASS
 QUADRANTS = 4
 LISTS = 2
 HALF = T // 2
-HALF_WORDS = HALF // PACK
 PER_COLUMN = 16
 WINDOW = 704
-VECTOR_WORDS = 36
+VECTOR_COLUMNS = 84
+VECTOR_COLUMNS_LATE = 72
 
 
 def four_by_four(ap, pattern):
@@ -45,6 +46,9 @@ def tile_picked_wdime_silu_l_kernel(tc, x_words, x_scales, aT, w1, w3, w2_words,
     with ExitStack() as ctx:
         keep = ctx.enter_context(tc.tile_pool(name="keep", bufs=1))
         psum = ctx.enter_context(tc.psum_pool(name="psum", bufs=1))
+
+        def bank(number, name, shape):
+            return psum.tile(shape, F32, name=name, tag="bank%d" % number)
 
         lists = [keep.tile([P, T // PER_COLUMN], U16, name="pos%d" % d) for d in range(LISTS)]
         x_codes = [keep.tile([P, T], U32, name="x_codes%d" % g, align_bytes=64) for g in range(PASSES)]
@@ -68,85 +72,88 @@ def tile_picked_wdime_silu_l_kernel(tc, x_words, x_scales, aT, w1, w3, w2_words,
         def load_x(g):
             nc.sync.dma_start(out=x_codes[g][:].bitcast(I32), in_=x_words[g].rearrange("p n j -> p (n j)").bitcast(I32))
 
-        w1_raw = [load_w1(0)]
-        def load_x_scales(g):
+        def load_scales(dst, rows):
             for q in range(QUADRANTS):
-                nc.sync.dma_start(out=x_sc[32 * q : 32 * q + 4, g * T : (g + 1) * T].bitcast(I32),
-                                  in_=x_scales[g, 4 * q : 4 * q + 4, :].bitcast(I32))
+                nc.sync.dma_start(out=dst[32 * q : 32 * q + 4].bitcast(I32), in_=rows[4 * q : 4 * q + 4, :].bitcast(I32))
 
-        load_x_scales(0)
+        w1_raw = [load_w1(0)]
+        load_scales(x_sc[:, :T], x_scales[0])
         load_x(0)
         w1_raw.append(load_w1(1))
         load_x(1)
-        load_x_scales(1)
+        load_scales(x_sc[:, T:], x_scales[1])
         w3_raw = [load_cols("w3_raw0", w3, 0, HALF)]
         nc.sync.dma_start(lists[0][:], pos1)
         w3_raw.append(load_cols("w3_raw1", w3, HALF, HALF))
         nc.sync.dma_start(lists[1][:], pos2)
-        a_raw = {(hf, d): load_cols("a_raw%d%d" % (hf, d), aT, d * T + hf * HALF, HALF)[:]
-                 for hf, d in ((0, 0), (0, 1), (1, 0), (1, 1))}
+        a_raw = {(hf, d): load_cols("a_raw%d%d" % (hf, d), aT, d * T + hf * HALF, HALF)
+                 for hf in range(2) for d in range(LISTS)}
         nc.sync.dma_start(out=w2_codes[:].bitcast(I32), in_=w2_words[0].bitcast(I32))
-        for q in range(QUADRANTS):
-            nc.sync.dma_start(out=w2_sc[32 * q : 32 * q + 4].bitcast(I32),
-                              in_=w2_scales[0, 4 * q : 4 * q + 4, :].bitcast(I32))
+        load_scales(w2_sc[:], w2_scales[0])
 
-        def deal(name, steps):
+        def dealer(name):
             grouped = keep.tile([P, PACK, P, PACK], BF16, name=name + "_bf", align_bytes=64)
             codes = keep.tile([P, H], U32, name=name + "_codes", align_bytes=64)
             scales = keep.tile([P, H], U8, name=name + "_sc", align_bytes=64)
-            for step in steps:
-                if isinstance(step, slice):
-                    cols = slice(step.start * P, step.stop * P)
-                    quantize(nc, codes[:, cols], scales[:, cols], grouped[:, step].rearrange("p t m j -> p (t m j)"))
-                else:
-                    copy, raw, first, words, tiles = step
-                    src = raw[:].rearrange("p j (m t) -> p m j t", t=PACK)
-                    copy(out=grouped[:, tiles, words].rearrange("p t m j -> p m j t"),
-                         in_=src[:, words.start - first : words.stop - first, :, tiles])
+
+            def deal(copy, raw, first, columns, tiles):
+                src = raw[:].rearrange("p j (m t) -> p m j t", t=PACK)
+                copy(out=grouped[:, tiles, columns].rearrange("p t m j -> p m j t"),
+                     in_=src[:, columns.start - first : columns.stop - first, :, tiles])
+
+            def codes_of(tiles):
+                cols = slice(tiles.start * P, tiles.stop * P)
+                quantize(nc, codes[:, cols], scales[:, cols], grouped[:, tiles].rearrange("p t m j -> p (t m j)"))
+
+            return deal, codes_of, codes, scales
+
+        all_tiles, tile_0, tiles_1_to_3 = slice(0, PACK), slice(0, 1), slice(1, PACK)
+
+        def quantize_w1(g):
+            deal, codes_of, codes, scales = dealer("w1%d" % g)
+            raw = w1_raw[g]
+            if g == 0:
+                deal(on_vector, raw, 0, slice(0, VECTOR_COLUMNS), all_tiles)
+                deal(on_scalar, raw, 0, slice(VECTOR_COLUMNS, P), all_tiles)
+                codes_of(slice(0, 2))
+                codes_of(slice(2, PACK))
+            else:
+                deal(on_vector, raw, 0, slice(0, VECTOR_COLUMNS), tile_0)
+                deal(on_scalar, raw, 0, slice(VECTOR_COLUMNS, P), tile_0)
+                codes_of(tile_0)
+                deal(on_vector, raw, 0, slice(0, VECTOR_COLUMNS_LATE // 2), tiles_1_to_3)
+                deal(on_vector, raw, 0, slice(VECTOR_COLUMNS_LATE // 2, VECTOR_COLUMNS_LATE), tiles_1_to_3)
+                deal(on_scalar, raw, 0, slice(VECTOR_COLUMNS_LATE, P), tiles_1_to_3)
+                for t in range(1, PACK):
+                    codes_of(slice(t, t + 1))
             return codes, scales
 
-        all_tiles, rest = slice(0, PACK), slice(1, PACK)
-        w1_steps = [
-            [(on_vector, w1_raw[0], 0, slice(0, 84), all_tiles), (on_scalar, w1_raw[0], 0, slice(84, P), all_tiles),
-             slice(0, 2), slice(2, PACK)],
-            [(on_vector, w1_raw[1], 0, slice(0, 84), slice(0, 1)), (on_scalar, w1_raw[1], 0, slice(84, P), slice(0, 1)),
-             slice(0, 1),
-             (on_vector, w1_raw[1], 0, slice(0, 36), rest), (on_vector, w1_raw[1], 0, slice(36, 72), rest),
-             (on_scalar, w1_raw[1], 0, slice(72, P), rest), slice(1, 2), slice(2, 3), slice(3, 4)],
-        ]
-
-        h_parts = [(0, slice(0, HALF), "upper0"), (0, slice(HALF, T), "lower0")]
-        h_parts.extend((t, slice(0, T), "upper%d" % t) for t in range(1, PACK))
-        h_acc = [psum.tile([P, edges.stop - edges.start], F32, name="h_acc%d" % n, tag=bank)
-                 for n, (t, edges, bank) in enumerate(h_parts)]
+        h_parts = [(0, slice(0, HALF), 4), (0, slice(HALF, T), 0)]
+        h_parts.extend((t, slice(0, T), 4 + t) for t in range(1, PACK))
+        h_acc = [bank(number, "h_acc%d" % n, [P, edges.stop - edges.start]) for n, (t, edges, number) in enumerate(h_parts)]
         h = [keep.tile([P, WINDOW], F32, name="h%d" % t) for t in range(PACK)]
         for t in (0, 2, 3):
             nc.vector.memset(h[t][:, T:], 0.0)
         nc.scalar.activation(out=h[1][:, T:], in_=h[0][:, T:], func=SILU)
         for g in range(PASSES):
-            codes, scales = deal("w1%d" % g, w1_steps[g])
-            for acc, (t, edges, bank) in zip(h_acc, h_parts):
+            codes, scales = quantize_w1(g)
+            for acc, (t, edges, number) in zip(h_acc, h_parts):
                 cols = slice(t * P, (t + 1) * P)
                 nc.tensor.matmul_mx(out=acc[:], lhsT=codes[:, cols].bitcast(FP8X4), lhsT_scale=scales[:, cols],
-                                    rhs=x_codes[g][:, edges].bitcast(FP8X4), rhs_scale=x_sc[:, g * T + edges.start : g * T + edges.stop],
+                                    rhs=x_codes[g][:, edges].bitcast(FP8X4),
+                                    rhs_scale=x_sc[:, g * T + edges.start : g * T + edges.stop],
                                     start=(g == 0), stop=(g == PASSES - 1))
-        for acc, (t, edges, bank) in zip(h_acc, h_parts):
+        for acc, (t, edges, number) in zip(h_acc, h_parts):
             nc.scalar.activation(out=h[t][:, edges], in_=acc[:], func=SILU)
 
-        terms = {}
-
-        def term_tile(d, hf, tag):
-            terms[d, hf] = keep.tile([P, PACK, HALF], F32, name="terms%d%d" % (d, hf), tag=tag, align_bytes=64)
-
-        def gather_first_list(t, tag):
+        def gather_list_0(t, tag):
             columns = keep.tile([P, T], F32, name="picked%d" % t, tag=tag, align_bytes=64)
             nc.vector.tensor_copy(columns[:], h[t][:].indirect(lists[0][:]))
             return columns
 
         def quantize_a(hf, d):
-            name = "a_bf%d%d" % (hf, d)
-            grouped = keep.tile([P, HALF, PACK], BF16, name=name, align_bytes=64)
-            on_scalar(out=four_by_four(grouped[:], "p (c i) j"), in_=four_by_four(a_raw[hf, d], "p j (c i)"))
+            grouped = keep.tile([P, HALF, PACK], BF16, name="a_bf%d%d" % (hf, d), align_bytes=64)
+            on_scalar(out=four_by_four(grouped[:], "p (c i) j"), in_=four_by_four(a_raw[hf, d][:], "p j (c i)"))
             codes = keep.tile([P, HALF], U32, name="a_codes%d%d" % (hf, d), align_bytes=64)
             scales = keep.tile([P, HALF], U8, name="a_sc%d%d" % (hf, d), align_bytes=64)
             quantize(nc, codes[:], scales[:], grouped[:].rearrange("p n j -> p (n j)"))
@@ -158,111 +165,104 @@ def tile_picked_wdime_silu_l_kernel(tc, x_words, x_scales, aT, w1, w3, w2_words,
             nc.tensor.matmul_mx(out=f, lhsT=w3_codes[:, cols].bitcast(FP8X4), lhsT_scale=w3_sc[:, cols],
                                 rhs=codes[:].bitcast(FP8X4), rhs_scale=scales[:], start=True, stop=True)
 
-        def first_term(f, t, hf):
-            nc.vector.tensor_tensor(out=terms[0, hf][:, t], in0=picked[t][:, hf * HALF : (hf + 1) * HALF], in1=f, op=MULT)
+        def term_0(dst, f, t, hf):
+            nc.vector.tensor_tensor(out=dst, in0=picked[t][:, hf * HALF : (hf + 1) * HALF], in1=f, op=MULT)
 
-        def second_filters(pair, hf, bank):
-            f = psum.tile([P, 2, HALF], F32, name="f1_%d%d" % (pair, hf), tag=bank)
+        def filters_1(pair, hf, number, tag):
+            f = bank(number, "f1_%d%d" % (pair, hf), [P, 2, HALF])
             for e in range(2):
                 filters(f[:, e], 2 * pair + e, hf, 1)
-            f_sb = keep.tile([P, 2, HALF], F32, name="f_sb%d%d" % (pair, hf), align_bytes=64,
-                             tag=("a_raw11", "a_bf11")[pair] if hf == 0 else "f_sb%d%d" % (pair, hf))
+            f_sb = keep.tile([P, 2, HALF], F32, name="f_sb%d%d" % (pair, hf), tag=tag, align_bytes=64)
             on_scalar(out=f_sb[:], in_=f[:])
             return f_sb
 
-        def second_term(dst, t, hf, first, width):
-            cols = slice(first, first + width)
+        def term_1(dst, t, hf, first, width):
             at = (hf * HALF + first) // PER_COLUMN
             offsets = lists[1][:, at : at + width // PER_COLUMN]
             nc.vector.tensor_tensor(out=dst, in0=h[t][:].indirect(offsets),
-                                    in1=f1[hf][t // 2][:, t % 2, cols], op=MULT)
+                                    in1=f1[hf][t // 2][:, t % 2, first : first + width], op=MULT)
 
-        def turn(acc, src, t, d):
-            nc.tensor.matmul(acc[:, t], lhsT=src, rhs=identity[:], is_transpose=True,
-                             start=(t == 0 and d == 0), stop=(t == last and d == LISTS - 1))
+        def turn_and_add(sums, term, t, d):
+            nc.tensor.matmul(sums[:, t], lhsT=term, rhs=identity[:], is_transpose=True,
+                             start=(t == 0 and d == 0), stop=(t == LAST and d == LISTS - 1))
 
-        def turn_back(key, sums, bank):
-            blocks = len(sums)
-            back = psum.tile([P, blocks, 2, P], F32, name="back" + key, tag=bank)
-            for b, acc in enumerate(sums):
-                rounded = keep.tile([P, 2, P, 2], BF16, name="zt_bf%s%d" % (key, b))
-                on_scalar(out=rounded[:], in_=acc[:].rearrange("v (u e) p -> v u p e", e=2))
-                words = rounded[:].rearrange("v u p e -> v (u p e)").bitcast(F32)
-                for u in range(2):
-                    nc.tensor.transpose(back[:, b, u], words[:, u * P : (u + 1) * P], identity[:])
-            grouped = keep.tile([P, blocks * P * PACK], BF16, name="z_bf" + key, align_bytes=64)
-            on_scalar(out=grouped[:].bitcast(F32).rearrange("p (b v u) -> p b v u", b=blocks, u=2),
-                      in_=back[:].rearrange("p b u v -> p b v u"))
+        def turn_back(b, sums, number):
+            back = bank(number, "back%d" % b, [P, 2, P])
+            rounded = keep.tile([P, 2, P, 2], BF16, name="zt_bf%d" % b)
+            on_scalar(out=rounded[:], in_=sums[:].rearrange("v (u e) p -> v u p e", e=2))
+            words = rounded[:].rearrange("v u p e -> v (u p e)").bitcast(F32)
+            for u in range(2):
+                nc.tensor.transpose(back[:, u], words[:, u * P : (u + 1) * P], identity[:])
+            grouped = keep.tile([P, P * PACK], BF16, name="z_bf%d" % b, align_bytes=64)
+            on_scalar(out=grouped[:].bitcast(F32).rearrange("p (v u) -> p v u", u=2),
+                      in_=back[:].rearrange("p u v -> p v u"))
             return grouped[:]
 
-        def add_on_vector(key, hf, first, width, tag):
-            cols = slice(first, first + width)
-            grouped = keep.tile([P, width, PACK], BF16, name="z_bf" + key, tag=tag, align_bytes=64)
-            nc.vector.tensor_tensor(out=four_by_four(grouped[:], "p (c i) j"),
-                                    in0=four_by_four(terms[0, hf][:, :, cols], "p j (c i)"),
-                                    in1=four_by_four(fourth[:], "p j (c i)"), op=ADD)
-            return grouped[:].rearrange("p v t -> p (v t)")
-
-        def finish(key, grouped, at, width, bank):
-            codes = keep.tile([P, width], U32, name="z_codes" + key, align_bytes=64)
-            scales = keep.tile([P, width], U8, name="z_sc" + key, align_bytes=64)
+        def finish(b, grouped, number):
+            codes = keep.tile([P, P], U32, name="z_codes%d" % b, align_bytes=64)
+            scales = keep.tile([P, P], U8, name="z_sc%d" % b, align_bytes=64)
             quantize(nc, codes[:], scales[:], grouped)
-            acc = psum.tile([P, N // P, width], F32, name="out_acc" + key, tag=bank)
+            acc = bank(number, "out_acc%d" % b, [P, N // P, P])
             for m in range(N // P):
                 nc.tensor.matmul_mx(out=acc[:, m], lhsT=w2_codes[:, 2 * m * P : 2 * (m + 1) * P].bitcast(FP4X4),
                                     lhsT_scale=w2_sc[:, m * P : (m + 1) * P],
                                     rhs=codes[:].bitcast(FP8X4), rhs_scale=scales[:], start=True, stop=True)
-            res = keep.tile([P, N // P, width], F32, name="res" + key)
+            res = keep.tile([P, N // P, P], F32, name="res%d" % b)
             nc.scalar.activation(out=res[:], in_=acc[:], func=SILU)
-            nc.sync.dma_start(out=out[:, at : at + width].rearrange("(m p) v -> p m v", p=P), in_=res[:])
+            nc.sync.dma_start(out=out[:, b * P : (b + 1) * P].rearrange("(m p) v -> p m v", p=P), in_=res[:])
 
-        w3_codes, w3_sc = deal("w3", [(on_vector, w3_raw[0], 0, slice(0, HALF_WORDS), all_tiles),
-                                       (on_scalar, w3_raw[1], HALF_WORDS, slice(HALF_WORDS, P), all_tiles), all_tiles])
+        deal_w3, codes_of_w3, w3_codes, w3_sc = dealer("w3")
+        deal_w3(on_vector, w3_raw[0], 0, slice(0, P // 2), all_tiles)
+        deal_w3(on_scalar, w3_raw[1], P // 2, slice(P // 2, P), all_tiles)
+        codes_of_w3(all_tiles)
 
-        last = PACK - 1
-        picked = [gather_first_list(t, "picked%d" % t) for t in range(last)]
+        picked = [gather_list_0(t, "picked%d" % t) for t in range(LAST)]
         a_q = {(0, 0): quantize_a(0, 0)}
-        picked.append(gather_first_list(last, "a_bf00"))
+        picked.append(gather_list_0(LAST, "a_bf00"))
         for hf, d in ((0, 1), (1, 0), (1, 1)):
             a_q[hf, d] = quantize_a(hf, d)
 
-        term_tile(0, 0, "a_bf01")
-        early = [keep.tile([P, HALF], F32, name="early%d" % t, align_bytes=64)
-                 for t in range(PACK)]
-        f0_early = [psum.tile([P, HALF], F32, name="f0_early%d" % t, tag="lower%d" % t) for t in range(PACK)]
-        f0_late = [psum.tile([P, 2, HALF], F32, name="f0_late%d" % pair, tag="upper%d" % pair) for pair in range(2)]
+        terms_0 = [keep.tile([P, PACK, HALF], F32, name="terms_00", tag="a_bf01", align_bytes=64)]
+        terms_1_half_0 = [keep.tile([P, HALF], F32, name="terms_10%d" % t, align_bytes=64) for t in range(PACK)]
+        f0_half_0 = [bank(t, "f0_%d0" % t, [P, HALF]) for t in range(PACK)]
+        f0_half_1 = [bank(4 + pair, "f0_%d1" % pair, [P, 2, HALF]) for pair in range(2)]
         for t in range(PACK):
-            filters(f0_early[t][:], t, 0, 0)
-        f1 = [[second_filters(pair, 0, "upper%d" % (2 + pair)) for pair in range(2)]]
+            filters(f0_half_0[t][:], t, 0, 0)
+        f1 = [[filters_1(pair, 0, 6 + pair, tag) for pair, tag in enumerate(("a_raw11", "a_bf11"))]]
         for t in range(PACK):
-            filters(f0_late[t // 2][:, t % 2], t, 1, 0)
+            filters(f0_half_1[t // 2][:, t % 2], t, 1, 0)
         for t in range(PACK):
-            first_term(f0_early[t][:], t, 0)
-        f1.append([second_filters(pair, 1, "lower%d" % (2 + pair)) for pair in range(2)])
-        sums = [psum.tile([P, PACK, P], F32, name="zt%d" % b, tag="lower%d" % b) for b in range(2)]
+            term_0(terms_0[0][:, t], f0_half_0[t][:], t, 0)
+        f1.append([filters_1(pair, 1, 2 + pair, "f_sb%d1" % pair) for pair in range(2)])
+        sums = [bank(b, "sums%d" % b, [P, PACK, P]) for b in range(2)]
         for t in range(PACK):
             for b in range(2):
-                turn(sums[b], terms[0, 0][:, t, b * P : (b + 1) * P], t, 0)
+                turn_and_add(sums[b], terms_0[0][:, t, b * P : (b + 1) * P], t, 0)
         for t in range(PACK):
-            second_term(early[t][:], t, 0, 0, HALF)
+            term_1(terms_1_half_0[t][:], t, 0, 0, HALF)
             for b in range(2):
-                turn(sums[b], early[t][:, b * P : (b + 1) * P], t, 1)
-        z = [turn_back("%d" % b, [sums[b]], "upper%d" % (2 + b)) for b in range(2)]
-        term_tile(0, 1, "a_raw11")
-        sums.append(psum.tile([P, PACK, P], F32, name="zt2", tag="lower1"))
+                turn_and_add(sums[b], terms_1_half_0[t][:, b * P : (b + 1) * P], t, 1)
+        z = [turn_back(b, sums[b], 6 + b) for b in range(2)]
+
+        terms_0.append(keep.tile([P, PACK, HALF], F32, name="terms_01", tag="a_raw11", align_bytes=64))
+        sums.append(bank(1, "sums2", [P, PACK, P]))
         for t in range(PACK):
-            first_term(f0_late[t // 2][:, t % 2], t, 1)
-            turn(sums[2], terms[0, 1][:, t, :P], t, 0)
-        third = keep.tile([P, PACK, P], F32)
+            term_0(terms_0[1][:, t], f0_half_1[t // 2][:, t % 2], t, 1)
+            turn_and_add(sums[2], terms_0[1][:, t, :P], t, 0)
+        terms_1_quarter_2 = keep.tile([P, PACK, P], F32)
         for t in range(PACK):
-            second_term(third[:, t], t, 1, 0, P)
-            turn(sums[2], third[:, t], t, 1)
-        z.append(turn_back("2", [sums[2]], "upper0"))
-        finish("0", z[0], 0, P, "lower0")
-        fourth = keep.tile([P, PACK, P], F32, tag="z_bf0", align_bytes=64)
+            term_1(terms_1_quarter_2[:, t], t, 1, 0, P)
+            turn_and_add(sums[2], terms_1_quarter_2[:, t], t, 1)
+        z.append(turn_back(2, sums[2], 4))
+
+        finish(0, z[0], 0)
+        terms_1_quarter_3 = keep.tile([P, PACK, P], F32, tag="z_bf0", align_bytes=64)
         for t in range(PACK):
-            second_term(fourth[:, t], t, 1, P, P)
-        finish("1", z[1], P, P, "lower1")
-        z.append(add_on_vector("3", 1, P, P, "z_bf1"))
-        finish("2", z[2], HALF, P, "lower2")
-        finish("3", z[3], HALF + P, P, "lower3")
+            term_1(terms_1_quarter_3[:, t], t, 1, P, P)
+        finish(1, z[1], 1)
+        z_last = keep.tile([P, P, PACK], BF16, tag="z_bf1", align_bytes=64)
+        nc.vector.tensor_tensor(out=four_by_four(z_last[:], "p (c i) j"),
+                                in0=four_by_four(terms_0[1][:, :, P:], "p j (c i)"),
+                                in1=four_by_four(terms_1_quarter_3[:], "p j (c i)"), op=ADD)
+        finish(2, z[2], 2)
+        finish(3, z_last[:].rearrange("p v t -> p (v t)"), 3)

@@ -84,10 +84,16 @@ def tile_picked_wdime_silu_l_kernel(tc, x_words, x_scales, aT, w1, w3, w2_words,
         load_scales(x_sc[:, T:], x_scales[1])
         w3_raw = [load_cols("w3_raw0", w3, 0, HALF)]
         nc.sync.dma_start(lists[0][:], pos1)
+        a_raw = {}
+
+        def load_a(hf, d):
+            a_raw[hf, d] = load_cols("a_raw%d%d" % (hf, d), aT, d * T + hf * HALF, HALF)
+
+        load_a(0, 0)
         w3_raw.append(load_cols("w3_raw1", w3, HALF, HALF))
         nc.sync.dma_start(lists[1][:], pos2)
-        a_raw = {(hf, d): load_cols("a_raw%d%d" % (hf, d), aT, d * T + hf * HALF, HALF)
-                 for hf in range(2) for d in range(LISTS)}
+        for hf, d in ((0, 1), (1, 0), (1, 1)):
+            load_a(hf, d)
         nc.sync.dma_start(out=w2_codes[:].bitcast(I32), in_=w2_words[0].bitcast(I32))
         load_scales(w2_sc[:], w2_scales[0])
 
@@ -146,14 +152,19 @@ def tile_picked_wdime_silu_l_kernel(tc, x_words, x_scales, aT, w1, w3, w2_words,
         for acc, (t, edges, number) in zip(h_acc, h_parts):
             nc.scalar.activation(out=h[t][:, edges], in_=acc[:], func=SILU)
 
-        def gather_list_0(t, tag):
-            columns = keep.tile([P, T], F32, name="picked%d" % t, tag=tag, align_bytes=64)
-            nc.vector.tensor_copy(columns[:], h[t][:].indirect(lists[0][:]))
-            return columns
+        def gather_list_0(dst, t, width):
+            nc.vector.tensor_copy(dst, h[t][:].indirect(lists[0][:, : width // PER_COLUMN]))
 
-        def quantize_a(hf, d):
-            grouped = keep.tile([P, HALF, PACK], BF16, name="a_bf%d%d" % (hf, d), align_bytes=64)
-            on_scalar(out=four_by_four(grouped[:], "p (c i) j"), in_=four_by_four(a_raw[hf, d][:], "p j (c i)"))
+        def round_on_scalar(grouped, raw):
+            on_scalar(out=four_by_four(grouped, "p (c i) j"), in_=four_by_four(raw, "p j (c i)"))
+
+        def round_on_gpsimd(grouped, raw):
+            nc.gpsimd.tensor_scalar(out=grouped, in0=raw.rearrange("p j n -> p n j"), scalar1=1.0, scalar2=0.0,
+                                    op0=MULT, op1=ADD)
+
+        def quantize_a(hf, d, rounder, tag):
+            grouped = keep.tile([P, HALF, PACK], BF16, name="a_bf%d%d" % (hf, d), tag=tag, align_bytes=64)
+            rounder(grouped[:], a_raw[hf, d][:])
             codes = keep.tile([P, HALF], U32, name="a_codes%d%d" % (hf, d), align_bytes=64)
             scales = keep.tile([P, HALF], U8, name="a_sc%d%d" % (hf, d), align_bytes=64)
             quantize(nc, codes[:], scales[:], grouped[:].rearrange("p n j -> p (n j)"))
@@ -165,22 +176,24 @@ def tile_picked_wdime_silu_l_kernel(tc, x_words, x_scales, aT, w1, w3, w2_words,
             nc.tensor.matmul_mx(out=f, lhsT=w3_codes[:, cols].bitcast(FP8X4), lhsT_scale=w3_sc[:, cols],
                                 rhs=codes[:].bitcast(FP8X4), rhs_scale=scales[:], start=True, stop=True)
 
-        def term_0(dst, f, t, hf):
-            nc.vector.tensor_tensor(out=dst, in0=picked[t][:, hf * HALF : (hf + 1) * HALF], in1=f, op=MULT)
-
-        def filters_1(pair, hf, number, tag):
-            f = bank(number, "f1_%d%d" % (pair, hf), [P, 2, HALF])
+        def pair_of_filters(pair, hf, d, number):
+            f = bank(number, "f%d%d%d" % (pair, hf, d), [P, 2, HALF])
             for e in range(2):
-                filters(f[:, e], 2 * pair + e, hf, 1)
-            f_sb = keep.tile([P, 2, HALF], F32, name="f_sb%d%d" % (pair, hf), tag=tag, align_bytes=64)
+                filters(f[:, e], 2 * pair + e, hf, d)
+            return f
+
+        def to_sbuf(f, name, tag):
+            f_sb = keep.tile([P, 2, HALF], F32, name=name, tag=tag, align_bytes=64)
             on_scalar(out=f_sb[:], in_=f[:])
             return f_sb
 
-        def term_1(dst, t, hf, first, width):
-            at = (hf * HALF + first) // PER_COLUMN
-            offsets = lists[1][:, at : at + width // PER_COLUMN]
-            nc.vector.tensor_tensor(out=dst, in0=h[t][:].indirect(offsets),
-                                    in1=f1[hf][t // 2][:, t % 2, first : first + width], op=MULT)
+        def product(dst, picked, f):
+            nc.vector.tensor_tensor(out=dst, in0=picked, in1=f, op=MULT)
+
+        def fused(dst, t, d, first, width, f_sb):
+            at = first // PER_COLUMN
+            offsets = lists[d][:, at : at + width // PER_COLUMN]
+            nc.vector.tensor_tensor(out=dst, in0=h[t][:].indirect(offsets), in1=f_sb, op=MULT)
 
         def turn_and_add(sums, term, t, d):
             nc.tensor.matmul(sums[:, t], lhsT=term, rhs=identity[:], is_transpose=True,
@@ -213,56 +226,66 @@ def tile_picked_wdime_silu_l_kernel(tc, x_words, x_scales, aT, w1, w3, w2_words,
 
         deal_w3, codes_of_w3, w3_codes, w3_sc = dealer("w3")
         deal_w3(on_vector, w3_raw[0], 0, slice(0, P // 2), all_tiles)
-        deal_w3(on_scalar, w3_raw[1], P // 2, slice(P // 2, P), all_tiles)
-        codes_of_w3(all_tiles)
+        picked = keep.tile([P, 2, T], F32, align_bytes=64)
+        for t in range(2):
+            gather_list_0(picked[:, t], t, T)
+        a_q = {(0, 0): quantize_a(0, 0, round_on_gpsimd, "a_bf00")}
+        for pair in range(2):
+            tiles = slice(2 * pair, 2 * pair + 2)
+            deal_w3(on_scalar, w3_raw[1], P // 2, slice(P // 2, P), tiles)
+            codes_of_w3(tiles)
+        picked_2 = keep.tile([P, HALF], F32, tag="w3_raw1", align_bytes=64)
+        gather_list_0(picked_2[:], 2, HALF)
+        a_q[0, 1] = quantize_a(0, 1, round_on_scalar, "a_bf01")
+        picked_3 = keep.tile([P, HALF], F32, tag="a_raw01", align_bytes=64)
+        gather_list_0(picked_3[:], 3, HALF)
 
-        picked = [gather_list_0(t, "picked%d" % t) for t in range(LAST)]
-        a_q = {(0, 0): quantize_a(0, 0)}
-        picked.append(gather_list_0(LAST, "a_bf00"))
-        for hf, d in ((0, 1), (1, 0), (1, 1)):
-            a_q[hf, d] = quantize_a(hf, d)
+        terms = {(hf, d): keep.tile([P, PACK, HALF], F32, name="terms%d%d" % (hf, d), tag=tag, align_bytes=64)
+                 for hf, d, tag in ((0, 0, "a_bf01"), (0, 1, "terms01"))}
+        f0_half_0 = [pair_of_filters(pair, 0, 0, 1 + pair) for pair in range(2)]
+        f1_banks = [pair_of_filters(pair, 0, 1, number) for pair, number in enumerate((3, 0))]
+        product(terms[0, 0][:, :2], picked[:, :, :HALF], f0_half_0[0][:])
+        for e, columns in enumerate((picked_2, picked_3)):
+            product(terms[0, 0][:, 2 + e], columns[:], f0_half_0[1][:, e])
+        a_q[1, 0] = quantize_a(1, 0, round_on_scalar, "a_bf10")
+        a_q[1, 1] = quantize_a(1, 1, round_on_scalar, "a_bf11")
+        f1_half_0 = [to_sbuf(f1_banks[pair], "f1_sb%d0" % pair, "f1_sb%d0" % pair) for pair in range(2)]
+        f0_half_1 = [pair_of_filters(pair, 1, 0, 4 + pair) for pair in range(2)]
+        f1_banks = [pair_of_filters(pair, 1, 1, 6 + pair) for pair in range(2)]
+        f0_sb = to_sbuf(f0_half_1[1], "f0_sb1", "f0_sb1")
+        f1_half_1 = [to_sbuf(f1_banks[pair], "f1_sb%d1" % pair, "f1_sb%d1" % pair) for pair in range(2)]
 
-        terms_0 = [keep.tile([P, PACK, HALF], F32, name="terms_00", tag="a_bf01", align_bytes=64)]
-        terms_1_half_0 = [keep.tile([P, HALF], F32, name="terms_10%d" % t, align_bytes=64) for t in range(PACK)]
-        f0_half_0 = [bank(t, "f0_%d0" % t, [P, HALF]) for t in range(PACK)]
-        f0_half_1 = [bank(4 + pair, "f0_%d1" % pair, [P, 2, HALF]) for pair in range(2)]
-        for t in range(PACK):
-            filters(f0_half_0[t][:], t, 0, 0)
-        f1 = [[filters_1(pair, 0, 6 + pair, tag) for pair, tag in enumerate(("a_raw11", "a_bf11"))]]
-        for t in range(PACK):
-            filters(f0_half_1[t // 2][:, t % 2], t, 1, 0)
-        for t in range(PACK):
-            term_0(terms_0[0][:, t], f0_half_0[t][:], t, 0)
-        f1.append([filters_1(pair, 1, 2 + pair, "f_sb%d1" % pair) for pair in range(2)])
-        sums = [bank(b, "sums%d" % b, [P, PACK, P]) for b in range(2)]
+        sums = [bank(1 + b, "sums%d" % b, [P, PACK, P]) for b in range(2)]
         for t in range(PACK):
             for b in range(2):
-                turn_and_add(sums[b], terms_0[0][:, t, b * P : (b + 1) * P], t, 0)
+                turn_and_add(sums[b], terms[0, 0][:, t, b * P : (b + 1) * P], t, 0)
         for t in range(PACK):
-            term_1(terms_1_half_0[t][:], t, 0, 0, HALF)
+            fused(terms[0, 1][:, t], t, 1, 0, HALF, f1_half_0[t // 2][:, t % 2])
             for b in range(2):
-                turn_and_add(sums[b], terms_1_half_0[t][:, b * P : (b + 1) * P], t, 1)
-        z = [turn_back(b, sums[b], 6 + b) for b in range(2)]
+                turn_and_add(sums[b], terms[0, 1][:, t, b * P : (b + 1) * P], t, 1)
+        z = [turn_back(b, sums[b], number) for b, number in enumerate((3, 0))]
 
-        terms_0.append(keep.tile([P, PACK, HALF], F32, name="terms_01", tag="a_raw11", align_bytes=64))
-        sums.append(bank(1, "sums2", [P, PACK, P]))
+        terms_10 = keep.tile([P, PACK, HALF], F32, tag="f1_sb00", align_bytes=64)
+        product(terms_10[:, :2], picked[:, :, HALF:], f0_half_1[0][:])
+        for e in range(2):
+            fused(terms_10[:, 2 + e], 2 + e, 0, HALF, HALF, f0_sb[:, e])
+        sums.append(bank(2, "sums2", [P, PACK, P]))
         for t in range(PACK):
-            term_0(terms_0[1][:, t], f0_half_1[t // 2][:, t % 2], t, 1)
-            turn_and_add(sums[2], terms_0[1][:, t, :P], t, 0)
+            turn_and_add(sums[2], terms_10[:, t, :P], t, 0)
         terms_1_quarter_2 = keep.tile([P, PACK, P], F32)
         for t in range(PACK):
-            term_1(terms_1_quarter_2[:, t], t, 1, 0, P)
+            fused(terms_1_quarter_2[:, t], t, 1, HALF, P, f1_half_1[t // 2][:, t % 2, :P])
             turn_and_add(sums[2], terms_1_quarter_2[:, t], t, 1)
         z.append(turn_back(2, sums[2], 4))
 
-        finish(0, z[0], 0)
+        finish(0, z[0], 1)
         terms_1_quarter_3 = keep.tile([P, PACK, P], F32, tag="z_bf0", align_bytes=64)
         for t in range(PACK):
-            term_1(terms_1_quarter_3[:, t], t, 1, P, P)
-        finish(1, z[1], 1)
+            fused(terms_1_quarter_3[:, t], t, 1, HALF + P, P, f1_half_1[t // 2][:, t % 2, P:])
+        finish(1, z[1], 2)
         z_last = keep.tile([P, P, PACK], BF16, tag="z_bf1", align_bytes=64)
         nc.vector.tensor_tensor(out=four_by_four(z_last[:], "p (c i) j"),
-                                in0=four_by_four(terms_0[1][:, :, P:], "p j (c i)"),
+                                in0=four_by_four(terms_10[:, :, P:], "p j (c i)"),
                                 in1=four_by_four(terms_1_quarter_3[:], "p j (c i)"), op=ADD)
-        finish(2, z[2], 2)
-        finish(3, z_last[:].rearrange("p v t -> p (v t)"), 3)
+        finish(2, z[2], 6)
+        finish(3, z_last[:].rearrange("p v t -> p (v t)"), 7)

@@ -29,7 +29,7 @@ HALF = T // 2
 PER_COLUMN = 16
 WINDOW = 704
 VECTOR_COLUMNS = 84
-VECTOR_COLUMNS_LATE = 72
+VECTOR_COLUMNS_LATE = 56
 
 
 def four_by_four(ap, pattern):
@@ -124,8 +124,7 @@ def tile_picked_wdime_silu_l_kernel(tc, x_words, x_scales, aT, w1, w3, w2_words,
                 codes_of(slice(0, 2))
                 codes_of(slice(2, PACK))
             else:
-                deal(on_vector, raw, 0, slice(0, VECTOR_COLUMNS), tile_0)
-                deal(on_scalar, raw, 0, slice(VECTOR_COLUMNS, P), tile_0)
+                deal(on_vector, raw, 0, slice(0, P), tile_0)
                 codes_of(tile_0)
                 deal(on_vector, raw, 0, slice(0, VECTOR_COLUMNS_LATE // 2), tiles_1_to_3)
                 deal(on_vector, raw, 0, slice(VECTOR_COLUMNS_LATE // 2, VECTOR_COLUMNS_LATE), tiles_1_to_3)
@@ -152,8 +151,8 @@ def tile_picked_wdime_silu_l_kernel(tc, x_words, x_scales, aT, w1, w3, w2_words,
         for acc, (t, edges, number) in zip(h_acc, h_parts):
             nc.scalar.activation(out=h[t][:, edges], in_=acc[:], func=SILU)
 
-        def gather_list_0(dst, t, width):
-            nc.vector.tensor_copy(dst, h[t][:].indirect(lists[0][:, : width // PER_COLUMN]))
+        def gather(dst, t, d):
+            nc.vector.tensor_copy(dst, h[t][:].indirect(lists[d][:, : HALF // PER_COLUMN]))
 
         def round_on_scalar(grouped, raw):
             on_scalar(out=four_by_four(grouped, "p (c i) j"), in_=four_by_four(raw, "p j (c i)"))
@@ -199,9 +198,9 @@ def tile_picked_wdime_silu_l_kernel(tc, x_words, x_scales, aT, w1, w3, w2_words,
             nc.tensor.matmul(sums[:, t], lhsT=term, rhs=identity[:], is_transpose=True,
                              start=(t == 0 and d == 0), stop=(t == LAST and d == LISTS - 1))
 
-        def turn_back(b, sums, number):
+        def turn_back(b, sums, number, tag):
             back = bank(number, "back%d" % b, [P, 2, P])
-            rounded = keep.tile([P, 2, P, 2], BF16, name="zt_bf%d" % b)
+            rounded = keep.tile([P, 2, P, 2], BF16, name="zt_bf%d" % b, tag=tag, align_bytes=64)
             on_scalar(out=rounded[:], in_=sums[:].rearrange("v (u e) p -> v u p e", e=2))
             words = rounded[:].rearrange("v u p e -> v (u p e)").bitcast(F32)
             for u in range(2):
@@ -226,49 +225,48 @@ def tile_picked_wdime_silu_l_kernel(tc, x_words, x_scales, aT, w1, w3, w2_words,
 
         deal_w3, codes_of_w3, w3_codes, w3_sc = dealer("w3")
         deal_w3(on_vector, w3_raw[0], 0, slice(0, P // 2), all_tiles)
-        picked = keep.tile([P, 2, T], F32, align_bytes=64)
-        for t in range(2):
-            gather_list_0(picked[:, t], t, T)
+        picked_0 = keep.tile([P, PACK, HALF], F32, align_bytes=64)
+        for t in range(PACK):
+            gather(picked_0[:, t], t, 0)
         a_q = {(0, 0): quantize_a(0, 0, round_on_gpsimd, "a_bf00")}
         for pair in range(2):
             tiles = slice(2 * pair, 2 * pair + 2)
             deal_w3(on_scalar, w3_raw[1], P // 2, slice(P // 2, P), tiles)
             codes_of_w3(tiles)
-        picked_2 = keep.tile([P, HALF], F32, tag="w3_raw1", align_bytes=64)
-        gather_list_0(picked_2[:], 2, HALF)
+        picked_1 = [keep.tile([P, HALF], F32, name="picked_1%d" % t, tag=tag, align_bytes=64)
+                    for t, tag in enumerate(("w3_raw1", "a_raw01"))]
+        gather(picked_1[0][:], 0, 1)
         a_q[0, 1] = quantize_a(0, 1, round_on_scalar, "a_bf01")
-        picked_3 = keep.tile([P, HALF], F32, tag="a_raw01", align_bytes=64)
-        gather_list_0(picked_3[:], 3, HALF)
+        gather(picked_1[1][:], 1, 1)
 
-        terms = {(hf, d): keep.tile([P, PACK, HALF], F32, name="terms%d%d" % (hf, d), tag=tag, align_bytes=64)
-                 for hf, d, tag in ((0, 0, "a_bf01"), (0, 1, "terms01"))}
+        terms_00 = keep.tile([P, PACK, HALF], F32, tag="a_bf01", align_bytes=64)
+        terms_01 = keep.tile([P, PACK, HALF], F32, align_bytes=64)
         f0_half_0 = [pair_of_filters(pair, 0, 0, 1 + pair) for pair in range(2)]
-        f1_banks = [pair_of_filters(pair, 0, 1, number) for pair, number in enumerate((3, 0))]
-        product(terms[0, 0][:, :2], picked[:, :, :HALF], f0_half_0[0][:])
-        for e, columns in enumerate((picked_2, picked_3)):
-            product(terms[0, 0][:, 2 + e], columns[:], f0_half_0[1][:, e])
+        f1_half_0 = [pair_of_filters(pair, 0, 1, number) for pair, number in enumerate((3, 0))]
+        for pair in range(2):
+            tiles = slice(2 * pair, 2 * pair + 2)
+            product(terms_00[:, tiles], picked_0[:, tiles], f0_half_0[pair][:])
         a_q[1, 0] = quantize_a(1, 0, round_on_scalar, "a_bf10")
+        for t in range(2):
+            product(terms_01[:, t], picked_1[t][:], f1_half_0[0][:, t])
         a_q[1, 1] = quantize_a(1, 1, round_on_scalar, "a_bf11")
-        f1_half_0 = [to_sbuf(f1_banks[pair], "f1_sb%d0" % pair, "f1_sb%d0" % pair) for pair in range(2)]
-        f0_half_1 = [pair_of_filters(pair, 1, 0, 4 + pair) for pair in range(2)]
-        f1_banks = [pair_of_filters(pair, 1, 1, 6 + pair) for pair in range(2)]
-        f0_sb = to_sbuf(f0_half_1[1], "f0_sb1", "f0_sb1")
-        f1_half_1 = [to_sbuf(f1_banks[pair], "f1_sb%d1" % pair, "f1_sb%d1" % pair) for pair in range(2)]
+        f1_sb = to_sbuf(f1_half_0[1], "f1_sb10", "f1_sb10")
+        banks_half_1 = [[pair_of_filters(pair, 1, d, 4 + 2 * d + pair) for pair in range(2)] for d in range(LISTS)]
+        f0_half_1, f1_half_1 = [[to_sbuf(banks_half_1[d][pair], "f%d_sb%d1" % (d, pair), "f%d_sb%d1" % (d, pair))
+                                 for pair in range(2)] for d in range(LISTS)]
+        for e in range(2):
+            fused(terms_01[:, 2 + e], 2 + e, 1, 0, HALF, f1_sb[:, e])
 
         sums = [bank(1 + b, "sums%d" % b, [P, PACK, P]) for b in range(2)]
-        for t in range(PACK):
-            for b in range(2):
-                turn_and_add(sums[b], terms[0, 0][:, t, b * P : (b + 1) * P], t, 0)
-        for t in range(PACK):
-            fused(terms[0, 1][:, t], t, 1, 0, HALF, f1_half_0[t // 2][:, t % 2])
-            for b in range(2):
-                turn_and_add(sums[b], terms[0, 1][:, t, b * P : (b + 1) * P], t, 1)
-        z = [turn_back(b, sums[b], number) for b, number in enumerate((3, 0))]
+        for d, terms in enumerate((terms_00, terms_01)):
+            for t in range(PACK):
+                for b in range(2):
+                    turn_and_add(sums[b], terms[:, t, b * P : (b + 1) * P], t, d)
+        z = [turn_back(0, sums[0], 3, "a_codes11"), turn_back(1, sums[1], 0, "a_sc11")]
 
-        terms_10 = keep.tile([P, PACK, HALF], F32, tag="f1_sb00", align_bytes=64)
-        product(terms_10[:, :2], picked[:, :, HALF:], f0_half_1[0][:])
-        for e in range(2):
-            fused(terms_10[:, 2 + e], 2 + e, 0, HALF, HALF, f0_sb[:, e])
+        terms_10 = keep.tile([P, PACK, HALF], F32, align_bytes=64)
+        for t in range(PACK):
+            fused(terms_10[:, t], t, 0, HALF, HALF, f0_half_1[t // 2][:, t % 2])
         sums.append(bank(2, "sums2", [P, PACK, P]))
         for t in range(PACK):
             turn_and_add(sums[2], terms_10[:, t, :P], t, 0)
@@ -276,7 +274,7 @@ def tile_picked_wdime_silu_l_kernel(tc, x_words, x_scales, aT, w1, w3, w2_words,
         for t in range(PACK):
             fused(terms_1_quarter_2[:, t], t, 1, HALF, P, f1_half_1[t // 2][:, t % 2, :P])
             turn_and_add(sums[2], terms_1_quarter_2[:, t], t, 1)
-        z.append(turn_back(2, sums[2], 4))
+        z.append(turn_back(2, sums[2], 4, "zt_bf2"))
 
         finish(0, z[0], 1)
         terms_1_quarter_3 = keep.tile([P, PACK, P], F32, tag="z_bf0", align_bytes=64)

@@ -119,10 +119,11 @@ def tile_picked_wdime_silu_l_kernel(tc, x_words, x_scales, aT, w1, w3, w2_words,
             deal, codes_of, codes, scales = dealer("w1%d" % g)
             raw = w1_raw[g]
             if g == 0:
-                deal(on_vector, raw, 0, slice(0, VECTOR_COLUMNS), all_tiles)
-                deal(on_scalar, raw, 0, slice(VECTOR_COLUMNS, P), all_tiles)
-                codes_of(slice(0, 2))
-                codes_of(slice(2, PACK))
+                for tiles in (slice(0, 2), slice(2, PACK)):
+                    deal(on_vector, raw, 0, slice(0, VECTOR_COLUMNS), tiles)
+                    deal(on_scalar, raw, 0, slice(VECTOR_COLUMNS, P), tiles)
+                for t in range(PACK):
+                    codes_of(slice(t, t + 1))
             else:
                 deal(on_vector, raw, 0, slice(0, P), tile_0)
                 codes_of(tile_0)
@@ -210,17 +211,20 @@ def tile_picked_wdime_silu_l_kernel(tc, x_words, x_scales, aT, w1, w3, w2_words,
                       in_=back[:].rearrange("p u v -> p v u"))
             return grouped[:]
 
-        def finish(b, grouped, number):
+        def finish(b, grouped, numbers):
             codes = keep.tile([P, P], U32, name="z_codes%d" % b, align_bytes=64)
             scales = keep.tile([P, P], U8, name="z_sc%d" % b, align_bytes=64)
             quantize(nc, codes[:], scales[:], grouped)
-            acc = bank(number, "out_acc%d" % b, [P, N // P, P])
-            for m in range(N // P):
-                nc.tensor.matmul_mx(out=acc[:, m], lhsT=w2_codes[:, 2 * m * P : 2 * (m + 1) * P].bitcast(FP4X4),
-                                    lhsT_scale=w2_sc[:, m * P : (m + 1) * P],
-                                    rhs=codes[:].bitcast(FP8X4), rhs_scale=scales[:], start=True, stop=True)
             res = keep.tile([P, N // P, P], F32, name="res%d" % b)
-            nc.scalar.activation(out=res[:], in_=acc[:], func=SILU)
+            tiles_a_bank = N // P // len(numbers)
+            for n, number in enumerate(numbers):
+                acc = bank(number, "out_acc%d%d" % (b, n), [P, tiles_a_bank, P])
+                for e in range(tiles_a_bank):
+                    m = n * tiles_a_bank + e
+                    nc.tensor.matmul_mx(out=acc[:, e], lhsT=w2_codes[:, 2 * m * P : 2 * (m + 1) * P].bitcast(FP4X4),
+                                        lhsT_scale=w2_sc[:, m * P : (m + 1) * P],
+                                        rhs=codes[:].bitcast(FP8X4), rhs_scale=scales[:], start=True, stop=True)
+                nc.scalar.activation(out=res[:, n * tiles_a_bank : (n + 1) * tiles_a_bank], in_=acc[:], func=SILU)
             nc.sync.dma_start(out=out[:, b * P : (b + 1) * P].rearrange("(m p) v -> p m v", p=P), in_=res[:])
 
         deal_w3, codes_of_w3, w3_codes, w3_sc = dealer("w3")
@@ -233,11 +237,10 @@ def tile_picked_wdime_silu_l_kernel(tc, x_words, x_scales, aT, w1, w3, w2_words,
             tiles = slice(2 * pair, 2 * pair + 2)
             deal_w3(on_scalar, w3_raw[1], P // 2, slice(P // 2, P), tiles)
             codes_of_w3(tiles)
-        picked_1 = [keep.tile([P, HALF], F32, name="picked_1%d" % t, tag=tag, align_bytes=64)
-                    for t, tag in enumerate(("w3_raw1", "a_raw01"))]
-        gather(picked_1[0][:], 0, 1)
+        picked_1 = keep.tile([P, 2, HALF], F32, tag="w3_raw1", align_bytes=64)
+        for t in range(2):
+            gather(picked_1[:, t], t, 1)
         a_q[0, 1] = quantize_a(0, 1, round_on_scalar, "a_bf01")
-        gather(picked_1[1][:], 1, 1)
 
         terms_00 = keep.tile([P, PACK, HALF], F32, tag="a_bf01", align_bytes=64)
         terms_01 = keep.tile([P, PACK, HALF], F32, align_bytes=64)
@@ -247,8 +250,7 @@ def tile_picked_wdime_silu_l_kernel(tc, x_words, x_scales, aT, w1, w3, w2_words,
             tiles = slice(2 * pair, 2 * pair + 2)
             product(terms_00[:, tiles], picked_0[:, tiles], f0_half_0[pair][:])
         a_q[1, 0] = quantize_a(1, 0, round_on_scalar, "a_bf10")
-        for t in range(2):
-            product(terms_01[:, t], picked_1[t][:], f1_half_0[0][:, t])
+        product(terms_01[:, :2], picked_1[:], f1_half_0[0][:])
         a_q[1, 1] = quantize_a(1, 1, round_on_scalar, "a_bf11")
         f1_sb = to_sbuf(f1_half_0[1], "f1_sb10", "f1_sb10")
         banks_half_1 = [[pair_of_filters(pair, 1, d, 4 + 2 * d + pair) for pair in range(2)] for d in range(LISTS)]
@@ -276,14 +278,14 @@ def tile_picked_wdime_silu_l_kernel(tc, x_words, x_scales, aT, w1, w3, w2_words,
             turn_and_add(sums[2], terms_1_quarter_2[:, t], t, 1)
         z.append(turn_back(2, sums[2], 4, "zt_bf2"))
 
-        finish(0, z[0], 1)
+        finish(0, z[0], (1,))
         terms_1_quarter_3 = keep.tile([P, PACK, P], F32, tag="z_bf0", align_bytes=64)
         for t in range(PACK):
             fused(terms_1_quarter_3[:, t], t, 1, HALF + P, P, f1_half_1[t // 2][:, t % 2, P:])
-        finish(1, z[1], 2)
+        finish(1, z[1], (2,))
         z_last = keep.tile([P, P, PACK], BF16, tag="z_bf1", align_bytes=64)
         nc.vector.tensor_tensor(out=four_by_four(z_last[:], "p (c i) j"),
                                 in0=four_by_four(terms_10[:, :, P:], "p j (c i)"),
                                 in1=four_by_four(terms_1_quarter_3[:], "p j (c i)"), op=ADD)
-        finish(2, z[2], 6)
-        finish(3, z_last[:].rearrange("p v t -> p (v t)"), 7)
+        finish(2, z[2], (6,))
+        finish(3, z_last[:].rearrange("p v t -> p (v t)"), (7, 5))

@@ -27,7 +27,6 @@ QUADRANTS = 4
 LISTS = 2
 HALF = T // 2
 PER_COLUMN = 16
-WINDOW = 704
 VECTOR_COLUMNS = 84
 VECTOR_COLUMNS_LATE = 56
 
@@ -60,6 +59,8 @@ def tile_picked_wdime_silu_l_kernel(tc, x_words, x_scales, aT, w1, w3, w2_words,
 
         identity = keep.tile([P, P], F32)
         make_identity(nc, identity[:])
+        unread = keep.tile([P, 1], F32)
+        nc.scalar.activation(out=unread[:], in_=w2_sc[:, :4].bitcast(F32), func=SILU)
 
         def load_cols(name, src, first, width):
             raw = keep.tile([P, PACK, width], F32, name=name, align_bytes=64)
@@ -137,10 +138,7 @@ def tile_picked_wdime_silu_l_kernel(tc, x_words, x_scales, aT, w1, w3, w2_words,
         h_parts = [(0, slice(0, HALF), 4), (0, slice(HALF, T), 0)]
         h_parts.extend((t, slice(0, T), 4 + t) for t in range(1, PACK))
         h_acc = [bank(number, "h_acc%d" % n, [P, edges.stop - edges.start]) for n, (t, edges, number) in enumerate(h_parts)]
-        h = [keep.tile([P, WINDOW], F32, name="h%d" % t) for t in range(PACK)]
-        for t in (0, 2, 3):
-            nc.vector.memset(h[t][:, T:], 0.0)
-        nc.scalar.activation(out=h[1][:, T:], in_=h[0][:, T:], func=SILU)
+        h = [keep.tile([P, T], F32, name="h%d" % t) for t in range(PACK)]
         for g in range(PASSES):
             codes, scales = quantize_w1(g)
             for acc, (t, edges, number) in zip(h_acc, h_parts):
@@ -259,17 +257,17 @@ def tile_picked_wdime_silu_l_kernel(tc, x_words, x_scales, aT, w1, w3, w2_words,
         for e in range(2):
             fused(terms_01[:, 2 + e], 2 + e, 1, 0, HALF, f1_sb[:, e])
 
-        sums = [bank(1 + b, "sums%d" % b, [P, PACK, P]) for b in range(2)]
+        sums = [bank(number, "sums%d" % b, [P, PACK, P]) for b, number in enumerate((3, 0))]
         for d, terms in enumerate((terms_00, terms_01)):
             for t in range(PACK):
                 for b in range(2):
                     turn_and_add(sums[b], terms[:, t, b * P : (b + 1) * P], t, d)
-        z = [turn_back(0, sums[0], 3, "a_codes11"), turn_back(1, sums[1], 0, "a_sc11")]
+        z = [turn_back(0, sums[0], 1, "a_codes11"), turn_back(1, sums[1], 2, "a_sc11")]
 
         terms_10 = keep.tile([P, PACK, HALF], F32, align_bytes=64)
         for t in range(PACK):
             fused(terms_10[:, t], t, 0, HALF, HALF, f0_half_1[t // 2][:, t % 2])
-        sums.append(bank(2, "sums2", [P, PACK, P]))
+        sums.append(bank(0, "sums2", [P, PACK, P]))
         for t in range(PACK):
             turn_and_add(sums[2], terms_10[:, t, :P], t, 0)
         terms_1_quarter_2 = keep.tile([P, PACK, P], F32)
@@ -282,7 +280,7 @@ def tile_picked_wdime_silu_l_kernel(tc, x_words, x_scales, aT, w1, w3, w2_words,
         terms_1_quarter_3 = keep.tile([P, PACK, P], F32, tag="z_bf0", align_bytes=64)
         for t in range(PACK):
             fused(terms_1_quarter_3[:, t], t, 1, HALF + P, P, f1_half_1[t // 2][:, t % 2, P:])
-        finish(1, z[1], (2,))
+        finish(1, z[1], (0,))
         z_last = keep.tile([P, P, PACK], BF16, tag="z_bf1", align_bytes=64)
         nc.vector.tensor_tensor(out=four_by_four(z_last[:], "p (c i) j"),
                                 in0=four_by_four(terms_10[:, :, P:], "p j (c i)"),

@@ -1,7 +1,6 @@
 from contextlib import ExitStack
 
 import concourse.mybir as mybir
-from concourse.masks import make_identity
 
 K, T, H, N, J = 1024, 512, 512, 256, 512
 FLOPS = 2 * (K * H * T + J * H * 2 * T + H * N * T)
@@ -15,12 +14,12 @@ U8 = mybir.dt.uint8
 FP8X4 = mybir.dt.float8_e4m3fn_x4
 FP4X4 = mybir.dt.float4_e2m1fn_x4
 SILU = mybir.ActivationFunctionType.Silu
+COPY = mybir.ActivationFunctionType.Copy
 ADD = mybir.AluOpType.add
 MULT = mybir.AluOpType.mult
 
 P = 128
 PACK = 4
-LAST = PACK - 1
 K_PASS = P * PACK
 PASSES = K // K_PASS
 QUADRANTS = 4
@@ -57,8 +56,6 @@ def tile_picked_wdime_silu_l_kernel(tc, x_words, x_scales, aT, w1, w3, w2_words,
         nc.vector.memset(x_sc[:].bitcast(I32), 0)
         nc.vector.memset(w2_sc[:].bitcast(I32), 0)
 
-        identity = keep.tile([P, P], F32)
-        make_identity(nc, identity[:])
         unread = keep.tile([P, 1], F32)
         nc.scalar.activation(out=unread[:], in_=w2_sc[:, :4].bitcast(F32), func=SILU)
 
@@ -83,8 +80,8 @@ def tile_picked_wdime_silu_l_kernel(tc, x_words, x_scales, aT, w1, w3, w2_words,
         w1_raw.append(load_w1(1))
         load_x(1)
         load_scales(x_sc[:, T:], x_scales[1])
-        w3_raw = [load_cols("w3_raw0", w3, 0, HALF)]
         nc.sync.dma_start(lists[0][:], pos1)
+        w3_raw = [load_cols("w3_raw0", w3, 0, HALF)]
         a_raw = {}
 
         def load_a(hf, d):
@@ -147,72 +144,75 @@ def tile_picked_wdime_silu_l_kernel(tc, x_words, x_scales, aT, w1, w3, w2_words,
                                     rhs=x_codes[g][:, edges].bitcast(FP8X4),
                                     rhs_scale=x_sc[:, g * T + edges.start : g * T + edges.stop],
                                     start=(g == 0), stop=(g == PASSES - 1))
-        for acc, (t, edges, number) in zip(h_acc, h_parts):
-            nc.scalar.activation(out=h[t][:, edges], in_=acc[:], func=SILU)
 
-        def gather(dst, t, d):
-            nc.vector.tensor_copy(dst, h[t][:].indirect(lists[d][:, : HALF // PER_COLUMN]))
+        def gather(dst, t, d, first, width):
+            at = first // PER_COLUMN
+            nc.scalar.activation(out=dst, in_=h[t][:].indirect(lists[d][:, at : at + width // PER_COLUMN]), func=COPY)
 
-        def round_on_scalar(grouped, raw):
-            on_scalar(out=four_by_four(grouped, "p (c i) j"), in_=four_by_four(raw, "p j (c i)"))
+        picked = {(hf, d): keep.tile([P, PACK, HALF], F32, name="picked%d%d" % (hf, d), align_bytes=64)
+                  for hf, d in ((0, 0), (0, 1), (1, 0))}
+        picked_last = [keep.tile([P, PACK, P], F32, name="picked_last%d" % b, align_bytes=64) for b in range(2)]
+        for t in range(PACK):
+            for acc, (part_of, edges, number) in zip(h_acc, h_parts):
+                if part_of == t:
+                    nc.scalar.activation(out=h[t][:, edges], in_=acc[:], func=SILU)
+            gather(picked[0, 0][:, t], t, 0, 0, HALF)
+        for hf, d in ((0, 1), (1, 0)):
+            for t in range(PACK):
+                gather(picked[hf, d][:, t], t, d, hf * HALF, HALF)
+        for b in range(2):
+            for t in range(PACK):
+                gather(picked_last[b][:, t], t, 1, HALF + b * P, P)
 
-        def round_on_gpsimd(grouped, raw):
-            nc.gpsimd.tensor_scalar(out=grouped, in0=raw.rearrange("p j n -> p n j"), scalar1=1.0, scalar2=0.0,
-                                    op0=MULT, op1=ADD)
-
-        def quantize_a(hf, d, rounder, tag):
-            grouped = keep.tile([P, HALF, PACK], BF16, name="a_bf%d%d" % (hf, d), tag=tag, align_bytes=64)
-            rounder(grouped[:], a_raw[hf, d][:])
+        def quantize_a(hf, d):
+            grouped = keep.tile([P, HALF, PACK], BF16, name="a_bf%d%d" % (hf, d), align_bytes=64)
+            on_vector(out=four_by_four(grouped[:], "p (c i) j"), in_=four_by_four(a_raw[hf, d][:], "p j (c i)"))
             codes = keep.tile([P, HALF], U32, name="a_codes%d%d" % (hf, d), align_bytes=64)
             scales = keep.tile([P, HALF], U8, name="a_sc%d%d" % (hf, d), align_bytes=64)
             quantize(nc, codes[:], scales[:], grouped[:].rearrange("p n j -> p (n j)"))
             return codes, scales
 
-        def filters(f, t, hf, d):
+        deal_w3, codes_of_w3, w3_codes, w3_sc = dealer("w3")
+        deal_w3(on_vector, w3_raw[0], 0, slice(0, P // 2), all_tiles)
+        a_q = {(0, 0): quantize_a(0, 0)}
+        deal_w3(on_vector, w3_raw[1], P // 2, slice(P // 2, P), all_tiles)
+        for pair in range(2):
+            codes_of_w3(slice(2 * pair, 2 * pair + 2))
+        for hf, d in ((0, 1), (1, 0), (1, 1)):
+            a_q[hf, d] = quantize_a(hf, d)
+
+        def filters(f, t, hf, d, first, width):
             cols = slice(t * P, (t + 1) * P)
             codes, scales = a_q[hf, d]
             nc.tensor.matmul_mx(out=f, lhsT=w3_codes[:, cols].bitcast(FP8X4), lhsT_scale=w3_sc[:, cols],
-                                rhs=codes[:].bitcast(FP8X4), rhs_scale=scales[:], start=True, stop=True)
+                                rhs=codes[:, first : first + width].bitcast(FP8X4),
+                                rhs_scale=scales[:, first : first + width], start=True, stop=True)
 
-        def pair_of_filters(pair, hf, d, number):
-            f = bank(number, "f%d%d%d" % (pair, hf, d), [P, 2, HALF])
-            for e in range(2):
-                filters(f[:, e], 2 * pair + e, hf, d)
-            return f
+        def terms_of_half(hf, d, numbers):
+            terms = keep.tile([P, PACK, HALF], F32, name="terms%d%d" % (hf, d), align_bytes=64)
+            for pair, number in enumerate(numbers):
+                f = bank(number, "f%d%d%d" % (pair, hf, d), [P, 2, HALF])
+                for e in range(2):
+                    filters(f[:, e], 2 * pair + e, hf, d, 0, HALF)
+                tiles = slice(2 * pair, 2 * pair + 2)
+                nc.vector.tensor_tensor(out=terms[:, tiles], in0=picked[hf, d][:, tiles], in1=f[:], op=MULT)
+            return terms
 
-        def to_sbuf(f, name, tag):
-            f_sb = keep.tile([P, 2, HALF], F32, name=name, tag=tag, align_bytes=64)
-            on_scalar(out=f_sb[:], in_=f[:])
-            return f_sb
+        def terms_of_quarter(b, number):
+            terms = keep.tile([P, PACK, P], F32, name="terms_last%d" % b, align_bytes=64)
+            f = bank(number, "f_last%d" % b, [P, PACK, P])
+            for t in range(PACK):
+                filters(f[:, t], t, 1, 1, b * P, P)
+            nc.vector.tensor_tensor(out=terms[:], in0=picked_last[b][:], in1=f[:], op=MULT)
+            return terms
 
-        def product(dst, picked, f):
-            nc.vector.tensor_tensor(out=dst, in0=picked, in1=f, op=MULT)
-
-        def fused(dst, t, d, first, width, f_sb):
-            at = first // PER_COLUMN
-            offsets = lists[d][:, at : at + width // PER_COLUMN]
-            nc.vector.tensor_tensor(out=dst, in0=h[t][:].indirect(offsets), in1=f_sb, op=MULT)
-
-        def turn_and_add(sums, term, t, d):
-            nc.tensor.matmul(sums[:, t], lhsT=term, rhs=identity[:], is_transpose=True,
-                             start=(t == 0 and d == 0), stop=(t == LAST and d == LISTS - 1))
-
-        def turn_back(b, sums, number, tag):
-            back = bank(number, "back%d" % b, [P, 2, P])
-            rounded = keep.tile([P, 2, P, 2], BF16, name="zt_bf%d" % b, tag=tag, align_bytes=64)
-            on_scalar(out=rounded[:], in_=sums[:].rearrange("v (u e) p -> v u p e", e=2))
-            words = rounded[:].rearrange("v u p e -> v (u p e)").bitcast(F32)
-            for u in range(2):
-                nc.tensor.transpose(back[:, u], words[:, u * P : (u + 1) * P], identity[:])
-            grouped = keep.tile([P, P * PACK], BF16, name="z_bf%d" % b, align_bytes=64)
-            on_scalar(out=grouped[:].bitcast(F32).rearrange("p (v u) -> p v u", u=2),
-                      in_=back[:].rearrange("p u v -> p v u"))
-            return grouped[:]
-
-        def finish(b, grouped, numbers):
+        def finish(b, first_terms, second_terms, numbers):
+            z = keep.tile([P, P, PACK], BF16, name="z_bf%d" % b, align_bytes=64)
+            nc.vector.tensor_tensor(out=four_by_four(z[:], "p (c i) j"), in0=four_by_four(first_terms, "p j (c i)"),
+                                    in1=four_by_four(second_terms, "p j (c i)"), op=ADD)
             codes = keep.tile([P, P], U32, name="z_codes%d" % b, align_bytes=64)
             scales = keep.tile([P, P], U8, name="z_sc%d" % b, align_bytes=64)
-            quantize(nc, codes[:], scales[:], grouped)
+            quantize(nc, codes[:], scales[:], z[:].rearrange("p v t -> p (v t)"))
             res = keep.tile([P, N // P, P], F32, name="res%d" % b)
             tiles_a_bank = N // P // len(numbers)
             for n, number in enumerate(numbers):
@@ -225,65 +225,10 @@ def tile_picked_wdime_silu_l_kernel(tc, x_words, x_scales, aT, w1, w3, w2_words,
                 nc.scalar.activation(out=res[:, n * tiles_a_bank : (n + 1) * tiles_a_bank], in_=acc[:], func=SILU)
             nc.sync.dma_start(out=out[:, b * P : (b + 1) * P].rearrange("(m p) v -> p m v", p=P), in_=res[:])
 
-        deal_w3, codes_of_w3, w3_codes, w3_sc = dealer("w3")
-        deal_w3(on_vector, w3_raw[0], 0, slice(0, P // 2), all_tiles)
-        picked_0 = keep.tile([P, PACK, HALF], F32, align_bytes=64)
-        for t in range(PACK):
-            gather(picked_0[:, t], t, 0)
-        a_q = {(0, 0): quantize_a(0, 0, round_on_gpsimd, "a_bf00")}
-        for pair in range(2):
-            tiles = slice(2 * pair, 2 * pair + 2)
-            deal_w3(on_scalar, w3_raw[1], P // 2, slice(P // 2, P), tiles)
-            codes_of_w3(tiles)
-        picked_1 = keep.tile([P, 2, HALF], F32, tag="w3_raw1", align_bytes=64)
-        for t in range(2):
-            gather(picked_1[:, t], t, 1)
-        a_q[0, 1] = quantize_a(0, 1, round_on_scalar, "a_bf01")
-
-        terms_00 = keep.tile([P, PACK, HALF], F32, tag="a_bf01", align_bytes=64)
-        terms_01 = keep.tile([P, PACK, HALF], F32, align_bytes=64)
-        f0_half_0 = [pair_of_filters(pair, 0, 0, 1 + pair) for pair in range(2)]
-        f1_half_0 = [pair_of_filters(pair, 0, 1, number) for pair, number in enumerate((3, 0))]
-        for pair in range(2):
-            tiles = slice(2 * pair, 2 * pair + 2)
-            product(terms_00[:, tiles], picked_0[:, tiles], f0_half_0[pair][:])
-        a_q[1, 0] = quantize_a(1, 0, round_on_scalar, "a_bf10")
-        product(terms_01[:, :2], picked_1[:], f1_half_0[0][:])
-        a_q[1, 1] = quantize_a(1, 1, round_on_scalar, "a_bf11")
-        f1_sb = to_sbuf(f1_half_0[1], "f1_sb10", "f1_sb10")
-        banks_half_1 = [[pair_of_filters(pair, 1, d, 4 + 2 * d + pair) for pair in range(2)] for d in range(LISTS)]
-        f0_half_1, f1_half_1 = [[to_sbuf(banks_half_1[d][pair], "f%d_sb%d1" % (d, pair), "f%d_sb%d1" % (d, pair))
-                                 for pair in range(2)] for d in range(LISTS)]
-        for e in range(2):
-            fused(terms_01[:, 2 + e], 2 + e, 1, 0, HALF, f1_sb[:, e])
-
-        sums = [bank(number, "sums%d" % b, [P, PACK, P]) for b, number in enumerate((3, 0))]
-        for d, terms in enumerate((terms_00, terms_01)):
-            for t in range(PACK):
-                for b in range(2):
-                    turn_and_add(sums[b], terms[:, t, b * P : (b + 1) * P], t, d)
-        z = [turn_back(0, sums[0], 1, "a_codes11"), turn_back(1, sums[1], 2, "a_sc11")]
-
-        terms_10 = keep.tile([P, PACK, HALF], F32, align_bytes=64)
-        for t in range(PACK):
-            fused(terms_10[:, t], t, 0, HALF, HALF, f0_half_1[t // 2][:, t % 2])
-        sums.append(bank(0, "sums2", [P, PACK, P]))
-        for t in range(PACK):
-            turn_and_add(sums[2], terms_10[:, t, :P], t, 0)
-        terms_1_quarter_2 = keep.tile([P, PACK, P], F32)
-        for t in range(PACK):
-            fused(terms_1_quarter_2[:, t], t, 1, HALF, P, f1_half_1[t // 2][:, t % 2, :P])
-            turn_and_add(sums[2], terms_1_quarter_2[:, t], t, 1)
-        z.append(turn_back(2, sums[2], 4, "zt_bf2"))
-
-        finish(0, z[0], (1,))
-        terms_1_quarter_3 = keep.tile([P, PACK, P], F32, tag="z_bf0", align_bytes=64)
-        for t in range(PACK):
-            fused(terms_1_quarter_3[:, t], t, 1, HALF + P, P, f1_half_1[t // 2][:, t % 2, P:])
-        finish(1, z[1], (0,))
-        z_last = keep.tile([P, P, PACK], BF16, tag="z_bf1", align_bytes=64)
-        nc.vector.tensor_tensor(out=four_by_four(z_last[:], "p (c i) j"),
-                                in0=four_by_four(terms_10[:, :, P:], "p j (c i)"),
-                                in1=four_by_four(terms_1_quarter_3[:], "p j (c i)"), op=ADD)
-        finish(2, z[2], (6,))
-        finish(3, z_last[:].rearrange("p v t -> p (v t)"), (7, 5))
+        terms_00 = terms_of_half(0, 0, (1, 2))
+        terms_01 = terms_of_half(0, 1, (3, 0))
+        for b in range(2):
+            finish(b, terms_00[:, :, b * P : (b + 1) * P], terms_01[:, :, b * P : (b + 1) * P], (1 + b,))
+        terms_10 = terms_of_half(1, 0, (4, 5))
+        finish(2, terms_10[:, :, :P], terms_of_quarter(0, 6)[:], (3,))
+        finish(3, terms_10[:, :, P:], terms_of_quarter(1, 7)[:], (0, 4))

@@ -72,28 +72,27 @@ def tile_picked_wdime_silu_l_kernel(tc, x_words, x_scales, aT, w1, w3, w2_words,
 
         def load_scales(dst, rows):
             for q in range(QUADRANTS):
-                nc.sync.dma_start(out=dst[32 * q : 32 * q + 4].bitcast(I32), in_=rows[4 * q : 4 * q + 4, :].bitcast(I32))
+                nc.sync.dma_start(out=dst[32 * q : 32 * q + 4].bitcast(I32).rearrange("r (g c) -> r g c", g=rows.shape[0]),
+                                  in_=rows[:, 4 * q : 4 * q + 4, :].bitcast(I32).rearrange("g r c -> r g c"))
 
         w1_raw = [load_w1(0)]
-        load_scales(x_sc[:, :T], x_scales[0])
+        load_scales(x_sc[:], x_scales)
         load_x(0)
         w1_raw.append(load_w1(1))
         load_x(1)
-        load_scales(x_sc[:, T:], x_scales[1])
         nc.sync.dma_start(lists[0][:], pos1)
+        nc.sync.dma_start(lists[1][:], pos2)
         w3_raw = [load_cols("w3_raw0", w3, 0, HALF)]
         a_raw = {}
 
         def load_a(hf, d):
             a_raw[hf, d] = load_cols("a_raw%d%d" % (hf, d), aT, d * T + hf * HALF, HALF)
 
-        load_a(0, 0)
         w3_raw.append(load_cols("w3_raw1", w3, HALF, HALF))
-        nc.sync.dma_start(lists[1][:], pos2)
-        for hf, d in ((0, 1), (1, 0), (1, 1)):
+        for hf, d in ((0, 0), (0, 1), (1, 0), (1, 1)):
             load_a(hf, d)
         nc.sync.dma_start(out=w2_codes[:].bitcast(I32), in_=w2_words[0].bitcast(I32))
-        load_scales(w2_sc[:], w2_scales[0])
+        load_scales(w2_sc[:], w2_scales)
 
         def dealer(name):
             grouped = keep.tile([P, PACK, P, PACK], BF16, name=name + "_bf", align_bytes=64)
@@ -111,7 +110,7 @@ def tile_picked_wdime_silu_l_kernel(tc, x_words, x_scales, aT, w1, w3, w2_words,
 
             return deal, codes_of, codes, scales
 
-        all_tiles, tile_0, tiles_1_to_3 = slice(0, PACK), slice(0, 1), slice(1, PACK)
+        all_tiles = slice(0, PACK)
 
         def quantize_w1(g):
             deal, codes_of, codes, scales = dealer("w1%d" % g)
@@ -123,13 +122,13 @@ def tile_picked_wdime_silu_l_kernel(tc, x_words, x_scales, aT, w1, w3, w2_words,
                 for t in range(PACK):
                     codes_of(slice(t, t + 1))
             else:
-                deal(on_vector, raw, 0, slice(0, P), tile_0)
-                codes_of(tile_0)
-                deal(on_vector, raw, 0, slice(0, VECTOR_COLUMNS_LATE // 2), tiles_1_to_3)
-                deal(on_vector, raw, 0, slice(VECTOR_COLUMNS_LATE // 2, VECTOR_COLUMNS_LATE), tiles_1_to_3)
-                deal(on_scalar, raw, 0, slice(VECTOR_COLUMNS_LATE, P), tiles_1_to_3)
-                for t in range(1, PACK):
-                    codes_of(slice(t, t + 1))
+                deal(on_vector, raw, 0, slice(0, VECTOR_COLUMNS), slice(0, 2))
+                deal(on_scalar, raw, 0, slice(VECTOR_COLUMNS, P), slice(0, 2))
+                codes_of(slice(0, 1))
+                codes_of(slice(1, 2))
+                deal(on_vector, raw, 0, slice(0, VECTOR_COLUMNS_LATE), slice(2, PACK))
+                deal(on_scalar, raw, 0, slice(VECTOR_COLUMNS_LATE, P), slice(2, PACK))
+                codes_of(slice(2, PACK))
             return codes, scales
 
         h_parts = [(0, slice(0, HALF), 4), (0, slice(HALF, T), 0)]
@@ -145,9 +144,15 @@ def tile_picked_wdime_silu_l_kernel(tc, x_words, x_scales, aT, w1, w3, w2_words,
                                     rhs_scale=x_sc[:, g * T + edges.start : g * T + edges.stop],
                                     start=(g == 0), stop=(g == PASSES - 1))
 
-        def gather(dst, t, d, first, width):
+        def offsets(d, first, width):
             at = first // PER_COLUMN
-            nc.scalar.activation(out=dst, in_=h[t][:].indirect(lists[d][:, at : at + width // PER_COLUMN]), func=COPY)
+            return lists[d][:, at : at + width // PER_COLUMN]
+
+        def gather(dst, t, d, first, width):
+            nc.scalar.activation(out=dst, in_=h[t][:].indirect(offsets(d, first, width)), func=COPY)
+
+        def gather_on_vector(dst, t, d, first, width):
+            nc.vector.tensor_copy(dst, h[t][:].indirect(offsets(d, first, width)))
 
         picked = {(hf, d): keep.tile([P, PACK, HALF], F32, name="picked%d%d" % (hf, d), align_bytes=64)
                   for hf, d in ((0, 0), (0, 1), (1, 0))}
@@ -157,29 +162,25 @@ def tile_picked_wdime_silu_l_kernel(tc, x_words, x_scales, aT, w1, w3, w2_words,
                 if part_of == t:
                     nc.scalar.activation(out=h[t][:, edges], in_=acc[:], func=SILU)
             gather(picked[0, 0][:, t], t, 0, 0, HALF)
-        for hf, d in ((0, 1), (1, 0)):
-            for t in range(PACK):
-                gather(picked[hf, d][:, t], t, d, hf * HALF, HALF)
+        for t in range(1, PACK):
+            gather(picked[0, 1][:, t], t, 1, 0, HALF)
+        for t in range(PACK):
+            gather(picked[1, 0][:, t], t, 0, HALF, HALF)
         for b in range(2):
             for t in range(PACK):
                 gather(picked_last[b][:, t], t, 1, HALF + b * P, P)
 
+        a_bf, a_q = {}, {}
+
+        def round_a(hf, d):
+            a_bf[hf, d] = keep.tile([P, HALF, PACK], BF16, name="a_bf%d%d" % (hf, d), align_bytes=64)
+            on_vector(out=four_by_four(a_bf[hf, d][:], "p (c i) j"), in_=four_by_four(a_raw[hf, d][:], "p j (c i)"))
+
         def quantize_a(hf, d):
-            grouped = keep.tile([P, HALF, PACK], BF16, name="a_bf%d%d" % (hf, d), align_bytes=64)
-            on_vector(out=four_by_four(grouped[:], "p (c i) j"), in_=four_by_four(a_raw[hf, d][:], "p j (c i)"))
             codes = keep.tile([P, HALF], U32, name="a_codes%d%d" % (hf, d), align_bytes=64)
             scales = keep.tile([P, HALF], U8, name="a_sc%d%d" % (hf, d), align_bytes=64)
-            quantize(nc, codes[:], scales[:], grouped[:].rearrange("p n j -> p (n j)"))
-            return codes, scales
-
-        deal_w3, codes_of_w3, w3_codes, w3_sc = dealer("w3")
-        deal_w3(on_vector, w3_raw[0], 0, slice(0, P // 2), all_tiles)
-        a_q = {(0, 0): quantize_a(0, 0)}
-        deal_w3(on_vector, w3_raw[1], P // 2, slice(P // 2, P), all_tiles)
-        for pair in range(2):
-            codes_of_w3(slice(2 * pair, 2 * pair + 2))
-        for hf, d in ((0, 1), (1, 0), (1, 1)):
-            a_q[hf, d] = quantize_a(hf, d)
+            quantize(nc, codes[:], scales[:], a_bf[hf, d][:].rearrange("p n j -> p (n j)"))
+            a_q[hf, d] = codes, scales
 
         def filters(f, t, hf, d, first, width):
             cols = slice(t * P, (t + 1) * P)
@@ -188,31 +189,37 @@ def tile_picked_wdime_silu_l_kernel(tc, x_words, x_scales, aT, w1, w3, w2_words,
                                 rhs=codes[:, first : first + width].bitcast(FP8X4),
                                 rhs_scale=scales[:, first : first + width], start=True, stop=True)
 
-        def terms_of_half(hf, d, numbers):
-            terms = keep.tile([P, PACK, HALF], F32, name="terms%d%d" % (hf, d), align_bytes=64)
-            for pair, number in enumerate(numbers):
-                f = bank(number, "f%d%d%d" % (pair, hf, d), [P, 2, HALF])
-                for e in range(2):
-                    filters(f[:, e], 2 * pair + e, hf, d, 0, HALF)
-                tiles = slice(2 * pair, 2 * pair + 2)
-                nc.vector.tensor_tensor(out=terms[:, tiles], in0=picked[hf, d][:, tiles], in1=f[:], op=MULT)
-            return terms
+        terms = {(hf, d): keep.tile([P, PACK, HALF], F32, name="terms%d%d" % (hf, d), align_bytes=64)
+                 for hf, d in ((0, 0), (0, 1), (1, 0))}
+        terms_last = [keep.tile([P, PACK, P], F32, name="terms_last%d" % b, align_bytes=64) for b in range(2)]
 
-        def terms_of_quarter(b, number):
-            terms = keep.tile([P, PACK, P], F32, name="terms_last%d" % b, align_bytes=64)
+        def product(dst, picked_values, f):
+            nc.vector.tensor_tensor(out=dst, in0=picked_values, in1=f, op=MULT)
+
+        def terms_of_pair(hf, d, pair, number):
+            f = bank(number, "f%d%d%d" % (pair, hf, d), [P, 2, HALF])
+            for e in range(2):
+                filters(f[:, e], 2 * pair + e, hf, d, 0, HALF)
+            tiles = slice(2 * pair, 2 * pair + 2)
+            product(terms[hf, d][:, tiles], picked[hf, d][:, tiles], f[:])
+
+        def filters_of_quarter(b, number):
             f = bank(number, "f_last%d" % b, [P, PACK, P])
             for t in range(PACK):
                 filters(f[:, t], t, 1, 1, b * P, P)
-            nc.vector.tensor_tensor(out=terms[:], in0=picked_last[b][:], in1=f[:], op=MULT)
-            return terms
+            return f
 
-        def finish(b, first_terms, second_terms, numbers):
-            z = keep.tile([P, P, PACK], BF16, name="z_bf%d" % b, align_bytes=64)
-            nc.vector.tensor_tensor(out=four_by_four(z[:], "p (c i) j"), in0=four_by_four(first_terms, "p j (c i)"),
+        z = {}
+
+        def add(b, first_terms, second_terms):
+            z[b] = keep.tile([P, P, PACK], BF16, name="z_bf%d" % b, align_bytes=64)
+            nc.vector.tensor_tensor(out=four_by_four(z[b][:], "p (c i) j"), in0=four_by_four(first_terms, "p j (c i)"),
                                     in1=four_by_four(second_terms, "p j (c i)"), op=ADD)
+
+        def finish(b, numbers):
             codes = keep.tile([P, P], U32, name="z_codes%d" % b, align_bytes=64)
             scales = keep.tile([P, P], U8, name="z_sc%d" % b, align_bytes=64)
-            quantize(nc, codes[:], scales[:], z[:].rearrange("p v t -> p (v t)"))
+            quantize(nc, codes[:], scales[:], z[b][:].rearrange("p v t -> p (v t)"))
             res = keep.tile([P, N // P, P], F32, name="res%d" % b)
             tiles_a_bank = N // P // len(numbers)
             for n, number in enumerate(numbers):
@@ -225,10 +232,36 @@ def tile_picked_wdime_silu_l_kernel(tc, x_words, x_scales, aT, w1, w3, w2_words,
                 nc.scalar.activation(out=res[:, n * tiles_a_bank : (n + 1) * tiles_a_bank], in_=acc[:], func=SILU)
             nc.sync.dma_start(out=out[:, b * P : (b + 1) * P].rearrange("(m p) v -> p m v", p=P), in_=res[:])
 
-        terms_00 = terms_of_half(0, 0, (1, 2))
-        terms_01 = terms_of_half(0, 1, (3, 0))
-        for b in range(2):
-            finish(b, terms_00[:, :, b * P : (b + 1) * P], terms_01[:, :, b * P : (b + 1) * P], (1 + b,))
-        terms_10 = terms_of_half(1, 0, (4, 5))
-        finish(2, terms_10[:, :, :P], terms_of_quarter(0, 6)[:], (3,))
-        finish(3, terms_10[:, :, P:], terms_of_quarter(1, 7)[:], (0, 4))
+        deal_w3, codes_of_w3, w3_codes, w3_sc = dealer("w3")
+        deal_w3(on_vector, w3_raw[0], 0, slice(0, P // 2), all_tiles)
+        gather_on_vector(picked[0, 1][:, 0], 0, 1, 0, HALF)
+        for pair in range(2):
+            deal_w3(on_vector, w3_raw[1], P // 2, slice(P // 2, P), slice(2 * pair, 2 * pair + 2))
+        codes_of_w3(slice(0, 2))
+        round_a(0, 0)
+        codes_of_w3(slice(2, PACK))
+        quantize_a(0, 0)
+        round_a(0, 1)
+        terms_of_pair(0, 0, 0, 1)
+        quantize_a(0, 1)
+        terms_of_pair(0, 0, 1, 2)
+        round_a(1, 0)
+        terms_of_pair(0, 1, 0, 3)
+        quantize_a(1, 0)
+        terms_of_pair(0, 1, 1, 0)
+        round_a(1, 1)
+        add(0, terms[0, 0][:, :, :P], terms[0, 1][:, :, :P])
+        quantize_a(1, 1)
+        add(1, terms[0, 0][:, :, P:], terms[0, 1][:, :, P:])
+        finish(0, (1,))
+        terms_of_pair(1, 0, 0, 4)
+        finish(1, (2,))
+        terms_of_pair(1, 0, 1, 5)
+        product(terms_last[0][:], picked_last[0][:], filters_of_quarter(0, 6)[:])
+        add(2, terms[1, 0][:, :, :P], terms_last[0][:])
+        f_last = filters_of_quarter(1, 7)
+        product(terms_last[1][:, :2], picked_last[1][:, :2], f_last[:, :2])
+        finish(2, (3,))
+        product(terms_last[1][:, 2:], picked_last[1][:, 2:], f_last[:, 2:])
+        add(3, terms[1, 0][:, :, P:], terms_last[1][:])
+        finish(3, (0, 4))

@@ -30,8 +30,8 @@ VECTOR_COLUMNS = 84
 VECTOR_COLUMNS_LATE = 56
 
 
-def four_by_four(ap, pattern):
-    return ap.rearrange(pattern + " -> p c j i", i=PACK)
+def line_by_line(ap, pattern):
+    return ap.rearrange(pattern + " -> p c j i", i=2)
 
 
 def quantize(nc, codes, scales, grouped):
@@ -174,7 +174,7 @@ def tile_picked_wdime_silu_l_kernel(tc, x_words, x_scales, aT, w1, w3, w2_words,
 
         def round_a(hf, d):
             a_bf[hf, d] = keep.tile([P, HALF, PACK], BF16, name="a_bf%d%d" % (hf, d), align_bytes=64)
-            on_vector(out=four_by_four(a_bf[hf, d][:], "p (c i) j"), in_=four_by_four(a_raw[hf, d][:], "p j (c i)"))
+            on_vector(out=line_by_line(a_bf[hf, d][:], "p (c i) j"), in_=line_by_line(a_raw[hf, d][:], "p j (c i)"))
 
         def quantize_a(hf, d):
             codes = keep.tile([P, HALF], U32, name="a_codes%d%d" % (hf, d), align_bytes=64)
@@ -213,8 +213,8 @@ def tile_picked_wdime_silu_l_kernel(tc, x_words, x_scales, aT, w1, w3, w2_words,
 
         def add(b, first_terms, second_terms):
             z[b] = keep.tile([P, P, PACK], BF16, name="z_bf%d" % b, align_bytes=64)
-            nc.vector.tensor_tensor(out=four_by_four(z[b][:], "p (c i) j"), in0=four_by_four(first_terms, "p j (c i)"),
-                                    in1=four_by_four(second_terms, "p j (c i)"), op=ADD)
+            nc.vector.tensor_tensor(out=line_by_line(z[b][:], "p (c i) j"), in0=line_by_line(first_terms, "p j (c i)"),
+                                    in1=line_by_line(second_terms, "p j (c i)"), op=ADD)
 
         def finish(b, numbers):
             codes = keep.tile([P, P], U32, name="z_codes%d" % b, align_bytes=64)

@@ -26,8 +26,6 @@ QUADRANTS = 4
 LISTS = 2
 HALF = T // 2
 PER_COLUMN = 16
-VECTOR_COLUMNS = 84
-VECTOR_COLUMNS_LATE = 56
 
 
 def line_by_line(ap, pattern):
@@ -40,7 +38,7 @@ def quantize(nc, codes, scales, grouped):
 
 def tile_picked_wdime_silu_l_kernel(tc, x_words, x_scales, aT, w1, w3, w2_words, w2_scales, pos1, pos2, out):
     nc = tc.nc
-    on_vector, on_scalar = nc.vector.tensor_copy, nc.scalar.copy
+    on_vector = nc.vector.tensor_copy
     with ExitStack() as ctx:
         keep = ctx.enter_context(tc.tile_pool(name="keep", bufs=1))
         psum = ctx.enter_context(tc.psum_pool(name="psum", bufs=1))
@@ -55,9 +53,6 @@ def tile_picked_wdime_silu_l_kernel(tc, x_words, x_scales, aT, w1, w3, w2_words,
         w2_sc = keep.tile([P, N], U8, align_bytes=64)
         nc.vector.memset(x_sc[:].bitcast(I32), 0)
         nc.vector.memset(w2_sc[:].bitcast(I32), 0)
-
-        unread = keep.tile([P, 1], F32)
-        nc.scalar.activation(out=unread[:], in_=w2_sc[:, :4].bitcast(F32), func=SILU)
 
         def load_cols(name, src, first, width):
             raw = keep.tile([P, PACK, width], F32, name=name, align_bytes=64)
@@ -77,8 +72,8 @@ def tile_picked_wdime_silu_l_kernel(tc, x_words, x_scales, aT, w1, w3, w2_words,
 
         w1_raw = [load_w1(0)]
         load_scales(x_sc[:], x_scales)
-        load_x(0)
         w1_raw.append(load_w1(1))
+        load_x(0)
         load_x(1)
         nc.sync.dma_start(lists[0][:], pos1)
         nc.sync.dma_start(lists[1][:], pos2)
@@ -115,34 +110,26 @@ def tile_picked_wdime_silu_l_kernel(tc, x_words, x_scales, aT, w1, w3, w2_words,
         def quantize_w1(g):
             deal, codes_of, codes, scales = dealer("w1%d" % g)
             raw = w1_raw[g]
-            if g == 0:
-                for tiles in (slice(0, 2), slice(2, PACK)):
-                    deal(on_vector, raw, 0, slice(0, VECTOR_COLUMNS), tiles)
-                    deal(on_scalar, raw, 0, slice(VECTOR_COLUMNS, P), tiles)
-                for t in range(PACK):
+            for pair in range(2):
+                deal(on_vector, raw, 0, slice(0, P), slice(2 * pair, 2 * pair + 2))
+                for t in (2 * pair, 2 * pair + 1):
                     codes_of(slice(t, t + 1))
-            else:
-                deal(on_vector, raw, 0, slice(0, VECTOR_COLUMNS), slice(0, 2))
-                deal(on_scalar, raw, 0, slice(VECTOR_COLUMNS, P), slice(0, 2))
-                codes_of(slice(0, 1))
-                codes_of(slice(1, 2))
-                deal(on_vector, raw, 0, slice(0, VECTOR_COLUMNS_LATE), slice(2, PACK))
-                deal(on_scalar, raw, 0, slice(VECTOR_COLUMNS_LATE, P), slice(2, PACK))
-                codes_of(slice(2, PACK))
             return codes, scales
 
-        h_parts = [(0, slice(0, HALF), 4), (0, slice(HALF, T), 0)]
-        h_parts.extend((t, slice(0, T), 4 + t) for t in range(1, PACK))
-        h_acc = [bank(number, "h_acc%d" % n, [P, edges.stop - edges.start]) for n, (t, edges, number) in enumerate(h_parts)]
+        h_parts = [(0, slice(0, P), 4), (0, slice(P, HALF), 0), (0, slice(HALF, T), 7)]
+        h_parts.extend((t, slice(0, T), (4, 0, 7)[t - 1]) for t in range(1, PACK))
         h = [keep.tile([P, T], F32, name="h%d" % t) for t in range(PACK)]
-        for g in range(PASSES):
-            codes, scales = quantize_w1(g)
-            for acc, (t, edges, number) in zip(h_acc, h_parts):
-                cols = slice(t * P, (t + 1) * P)
+        w1_q = [quantize_w1(g) for g in range(PASSES)]
+
+        def make_h(n, t, edges, number):
+            acc = bank(number, "h_acc%d" % n, [P, edges.stop - edges.start])
+            cols = slice(t * P, (t + 1) * P)
+            for g, (codes, scales) in enumerate(w1_q):
                 nc.tensor.matmul_mx(out=acc[:], lhsT=codes[:, cols].bitcast(FP8X4), lhsT_scale=scales[:, cols],
                                     rhs=x_codes[g][:, edges].bitcast(FP8X4),
                                     rhs_scale=x_sc[:, g * T + edges.start : g * T + edges.stop],
                                     start=(g == 0), stop=(g == PASSES - 1))
+            nc.scalar.activation(out=h[t][:, edges], in_=acc[:], func=SILU)
 
         def offsets(d, first, width):
             at = first // PER_COLUMN
@@ -158,13 +145,15 @@ def tile_picked_wdime_silu_l_kernel(tc, x_words, x_scales, aT, w1, w3, w2_words,
                   for hf, d in ((0, 0), (0, 1), (1, 0))}
         picked_last = [keep.tile([P, PACK, P], F32, name="picked_last%d" % b, align_bytes=64) for b in range(2)]
         for t in range(PACK):
-            for acc, (part_of, edges, number) in zip(h_acc, h_parts):
+            for n, (part_of, edges, number) in enumerate(h_parts):
                 if part_of == t:
-                    nc.scalar.activation(out=h[t][:, edges], in_=acc[:], func=SILU)
+                    make_h(n, t, edges, number)
             gather(picked[0, 0][:, t], t, 0, 0, HALF)
+            if t == 0:
+                gather(picked[1, 0][:, 0], 0, 0, HALF, HALF)
         for t in range(1, PACK):
             gather(picked[0, 1][:, t], t, 1, 0, HALF)
-        for t in range(PACK):
+        for t in range(1, PACK):
             gather(picked[1, 0][:, t], t, 0, HALF, HALF)
         for b in range(2):
             for t in range(PACK):
@@ -244,24 +233,24 @@ def tile_picked_wdime_silu_l_kernel(tc, x_words, x_scales, aT, w1, w3, w2_words,
         round_a(0, 1)
         terms_of_pair(0, 0, 0, 1)
         quantize_a(0, 1)
-        terms_of_pair(0, 0, 1, 2)
         round_a(1, 0)
-        terms_of_pair(0, 1, 0, 3)
+        terms_of_pair(0, 0, 1, 2)
         quantize_a(1, 0)
-        terms_of_pair(0, 1, 1, 0)
         round_a(1, 1)
-        add(0, terms[0, 0][:, :, :P], terms[0, 1][:, :, :P])
+        terms_of_pair(0, 1, 0, 3)
         quantize_a(1, 1)
+        terms_of_pair(0, 1, 1, 5)
+        terms_of_pair(1, 0, 0, 6)
+        add(0, terms[0, 0][:, :, :P], terms[0, 1][:, :, :P])
         add(1, terms[0, 0][:, :, P:], terms[0, 1][:, :, P:])
         finish(0, (1,))
-        terms_of_pair(1, 0, 0, 4)
         finish(1, (2,))
-        terms_of_pair(1, 0, 1, 5)
-        product(terms_last[0][:], picked_last[0][:], filters_of_quarter(0, 6)[:])
-        add(2, terms[1, 0][:, :, :P], terms_last[0][:])
-        f_last = filters_of_quarter(1, 7)
+        terms_of_pair(1, 0, 1, 7)
+        product(terms_last[0][:], picked_last[0][:], filters_of_quarter(0, 0)[:])
+        f_last = filters_of_quarter(1, 4)
         product(terms_last[1][:, :2], picked_last[1][:, :2], f_last[:, :2])
-        finish(2, (3,))
+        add(2, terms[1, 0][:, :, :P], terms_last[0][:])
         product(terms_last[1][:, 2:], picked_last[1][:, 2:], f_last[:, 2:])
+        finish(2, (3,))
         add(3, terms[1, 0][:, :, P:], terms_last[1][:])
-        finish(3, (0, 4))
+        finish(3, (5, 6))

@@ -99,9 +99,9 @@ def tile_picked_wdime_silu_l_kernel(tc, x_words, x_scales, aT, w1, w3, w2_words,
                 copy(out=grouped[:, tiles, columns].rearrange("p t m j -> p m j t"),
                      in_=src[:, columns.start - first : columns.stop - first, :, tiles])
 
-            def codes_of(tiles):
-                cols = slice(tiles.start * P, tiles.stop * P)
-                quantize(nc, codes[:, cols], scales[:, cols], grouped[:, tiles].rearrange("p t m j -> p (t m j)"))
+            def codes_of(t, columns):
+                cols = slice(t * P + columns.start, t * P + columns.stop)
+                quantize(nc, codes[:, cols], scales[:, cols], grouped[:, t, columns].rearrange("p m j -> p (m j)"))
 
             return deal, codes_of, codes, scales
 
@@ -113,7 +113,7 @@ def tile_picked_wdime_silu_l_kernel(tc, x_words, x_scales, aT, w1, w3, w2_words,
             for pair in range(2):
                 deal(on_vector, raw, 0, slice(0, P), slice(2 * pair, 2 * pair + 2))
                 for t in (2 * pair, 2 * pair + 1):
-                    codes_of(slice(t, t + 1))
+                    codes_of(t, slice(0, P))
             return codes, scales
 
         h_parts = [(0, slice(0, P), 4), (0, slice(P, HALF), 0), (0, slice(HALF, T), 7)]
@@ -198,37 +198,40 @@ def tile_picked_wdime_silu_l_kernel(tc, x_words, x_scales, aT, w1, w3, w2_words,
                 filters(f[:, t], t, 1, 1, b * P, P)
             return f
 
-        z = {}
-
-        def add(b, first_terms, second_terms):
-            z[b] = keep.tile([P, P, PACK], BF16, name="z_bf%d" % b, align_bytes=64)
-            nc.vector.tensor_tensor(out=line_by_line(z[b][:], "p (c i) j"), in0=line_by_line(first_terms, "p j (c i)"),
+        def add(name, width, first_terms, second_terms):
+            z = keep.tile([P, width, PACK], BF16, name="z_bf" + name, align_bytes=64)
+            nc.vector.tensor_tensor(out=line_by_line(z[:], "p (c i) j"), in0=line_by_line(first_terms, "p j (c i)"),
                                     in1=line_by_line(second_terms, "p j (c i)"), op=ADD)
+            return z
 
-        def finish(b, numbers):
-            codes = keep.tile([P, P], U32, name="z_codes%d" % b, align_bytes=64)
-            scales = keep.tile([P, P], U8, name="z_sc%d" % b, align_bytes=64)
-            quantize(nc, codes[:], scales[:], z[b][:].rearrange("p v t -> p (v t)"))
-            res = keep.tile([P, N // P, P], F32, name="res%d" % b)
+        def finish(name, z, first, width, numbers):
+            codes = keep.tile([P, width], U32, name="z_codes" + name, align_bytes=64)
+            scales = keep.tile([P, width], U8, name="z_sc" + name, align_bytes=64)
+            quantize(nc, codes[:], scales[:], z[:].rearrange("p v t -> p (v t)"))
+            res = keep.tile([P, N // P, width], F32, name="res" + name)
             tiles_a_bank = N // P // len(numbers)
             for n, number in enumerate(numbers):
-                acc = bank(number, "out_acc%d%d" % (b, n), [P, tiles_a_bank, P])
+                acc = bank(number, "out_acc%s%d" % (name, n), [P, tiles_a_bank, width])
                 for e in range(tiles_a_bank):
                     m = n * tiles_a_bank + e
                     nc.tensor.matmul_mx(out=acc[:, e], lhsT=w2_codes[:, 2 * m * P : 2 * (m + 1) * P].bitcast(FP4X4),
                                         lhsT_scale=w2_sc[:, m * P : (m + 1) * P],
                                         rhs=codes[:].bitcast(FP8X4), rhs_scale=scales[:], start=True, stop=True)
                 nc.scalar.activation(out=res[:, n * tiles_a_bank : (n + 1) * tiles_a_bank], in_=acc[:], func=SILU)
-            nc.sync.dma_start(out=out[:, b * P : (b + 1) * P].rearrange("(m p) v -> p m v", p=P), in_=res[:])
+            nc.sync.dma_start(out=out[:, first : first + width].rearrange("(m p) v -> p m v", p=P), in_=res[:])
 
         deal_w3, codes_of_w3, w3_codes, w3_sc = dealer("w3")
         deal_w3(on_vector, w3_raw[0], 0, slice(0, P // 2), all_tiles)
         gather_on_vector(picked[0, 1][:, 0], 0, 1, 0, HALF)
+        for t in range(PACK):
+            codes_of_w3(t, slice(0, P // 2))
         for pair in range(2):
             deal_w3(on_vector, w3_raw[1], P // 2, slice(P // 2, P), slice(2 * pair, 2 * pair + 2))
-        codes_of_w3(slice(0, 2))
+        for t in range(2):
+            codes_of_w3(t, slice(P // 2, P))
         round_a(0, 0)
-        codes_of_w3(slice(2, PACK))
+        for t in range(2, PACK):
+            codes_of_w3(t, slice(P // 2, P))
         quantize_a(0, 0)
         round_a(0, 1)
         terms_of_pair(0, 0, 0, 1)
@@ -241,16 +244,13 @@ def tile_picked_wdime_silu_l_kernel(tc, x_words, x_scales, aT, w1, w3, w2_words,
         quantize_a(1, 1)
         terms_of_pair(0, 1, 1, 5)
         terms_of_pair(1, 0, 0, 6)
-        add(0, terms[0, 0][:, :, :P], terms[0, 1][:, :, :P])
-        add(1, terms[0, 0][:, :, P:], terms[0, 1][:, :, P:])
-        finish(0, (1,))
-        finish(1, (2,))
+        z_half = add("half", HALF, terms[0, 0][:], terms[0, 1][:])
         terms_of_pair(1, 0, 1, 7)
+        finish("half", z_half, 0, HALF, (1,))
         product(terms_last[0][:], picked_last[0][:], filters_of_quarter(0, 0)[:])
         f_last = filters_of_quarter(1, 4)
         product(terms_last[1][:, :2], picked_last[1][:, :2], f_last[:, :2])
-        add(2, terms[1, 0][:, :, :P], terms_last[0][:])
+        z_2 = add("2", P, terms[1, 0][:, :, :P], terms_last[0][:])
         product(terms_last[1][:, 2:], picked_last[1][:, 2:], f_last[:, 2:])
-        finish(2, (3,))
-        add(3, terms[1, 0][:, :, P:], terms_last[1][:])
-        finish(3, (5, 6))
+        finish("2", z_2, HALF, P, (3,))
+        finish("3", add("3", P, terms[1, 0][:, :, P:], terms_last[1][:]), HALF + P, P, (5, 6))

@@ -26,6 +26,7 @@ QUADRANTS = 4
 LISTS = 2
 HALF = T // 2
 PER_COLUMN = 16
+OWN = 64
 
 
 def line_by_line(ap, pattern):
@@ -161,14 +162,19 @@ def tile_picked_wdime_silu_l_kernel(tc, x_words, x_scales, aT, w1, w3, w2_words,
 
         a_bf, a_q = {}, {}
 
-        def round_a(hf, d):
-            a_bf[hf, d] = keep.tile([P, HALF, PACK], BF16, name="a_bf%d%d" % (hf, d), align_bytes=64)
-            on_vector(out=line_by_line(a_bf[hf, d][:], "p (c i) j"), in_=line_by_line(a_raw[hf, d][:], "p j (c i)"))
+        for d in range(LISTS):
+            a_bf[0, d] = keep.tile([P, HALF, PACK], BF16, name="a_bf0%d" % d, align_bytes=64)[:]
+        a_bf_late = keep.tile([P, OWN + HALF, PACK], BF16, align_bytes=64)
+        a_bf[1, 0], a_bf[1, 1] = a_bf_late[:, OWN:], a_bf_late[:, :HALF]
+
+        def round_a(hf, d, width):
+            on_vector(out=line_by_line(a_bf[hf, d][:, :width], "p (c i) j"),
+                      in_=line_by_line(a_raw[hf, d][:, :, :width], "p j (c i)"))
 
         def quantize_a(hf, d):
             codes = keep.tile([P, HALF], U32, name="a_codes%d%d" % (hf, d), align_bytes=64)
             scales = keep.tile([P, HALF], U8, name="a_sc%d%d" % (hf, d), align_bytes=64)
-            quantize(nc, codes[:], scales[:], a_bf[hf, d][:].rearrange("p n j -> p (n j)"))
+            quantize(nc, codes[:], scales[:], a_bf[hf, d].rearrange("p n j -> p (n j)"))
             a_q[hf, d] = codes, scales
 
         def filters(f, t, hf, d, first, width):
@@ -204,11 +210,17 @@ def tile_picked_wdime_silu_l_kernel(tc, x_words, x_scales, aT, w1, w3, w2_words,
                                     in1=line_by_line(second_terms, "p j (c i)"), op=ADD)
             return z
 
-        def finish(name, z, first, width, numbers):
+        res_first = keep.tile([P, N // P, HALF + P], F32)
+        res_last = keep.tile([P, N // P, P], F32)
+
+        def store(res, tiles, first, width):
+            rows = out[:, first : first + width].rearrange("(m p) v -> p m v", p=P)
+            nc.sync.dma_start(out=rows[:, tiles], in_=res[:, tiles])
+
+        def finish(name, z, res, width, numbers):
             codes = keep.tile([P, width], U32, name="z_codes" + name, align_bytes=64)
             scales = keep.tile([P, width], U8, name="z_sc" + name, align_bytes=64)
             quantize(nc, codes[:], scales[:], z[:].rearrange("p v t -> p (v t)"))
-            res = keep.tile([P, N // P, width], F32, name="res" + name)
             tiles_a_bank = N // P // len(numbers)
             for n, number in enumerate(numbers):
                 acc = bank(number, "out_acc%s%d" % (name, n), [P, tiles_a_bank, width])
@@ -218,7 +230,6 @@ def tile_picked_wdime_silu_l_kernel(tc, x_words, x_scales, aT, w1, w3, w2_words,
                                         lhsT_scale=w2_sc[:, m * P : (m + 1) * P],
                                         rhs=codes[:].bitcast(FP8X4), rhs_scale=scales[:], start=True, stop=True)
                 nc.scalar.activation(out=res[:, n * tiles_a_bank : (n + 1) * tiles_a_bank], in_=acc[:], func=SILU)
-            nc.sync.dma_start(out=out[:, first : first + width].rearrange("(m p) v -> p m v", p=P), in_=res[:])
 
         deal_w3, codes_of_w3, w3_codes, w3_sc = dealer("w3")
         deal_w3(on_vector, w3_raw[0], 0, slice(0, P // 2), all_tiles)
@@ -229,28 +240,33 @@ def tile_picked_wdime_silu_l_kernel(tc, x_words, x_scales, aT, w1, w3, w2_words,
             deal_w3(on_vector, w3_raw[1], P // 2, slice(P // 2, P), slice(2 * pair, 2 * pair + 2))
         for t in range(2):
             codes_of_w3(t, slice(P // 2, P))
-        round_a(0, 0)
+        round_a(0, 0, HALF)
         for t in range(2, PACK):
             codes_of_w3(t, slice(P // 2, P))
         quantize_a(0, 0)
-        round_a(0, 1)
+        round_a(0, 1, HALF)
         terms_of_pair(0, 0, 0, 1)
         quantize_a(0, 1)
-        round_a(1, 0)
+        round_a(1, 0, HALF)
         terms_of_pair(0, 0, 1, 2)
+        round_a(1, 1, OWN)
         quantize_a(1, 0)
-        round_a(1, 1)
+        nc.gpsimd.tensor_scalar(out=a_bf[1, 1][:, OWN:], in0=a_raw[1, 1][:, :, OWN:].rearrange("p j n -> p n j"),
+                                scalar1=1.0, scalar2=0.0, op0=MULT, op1=ADD)
         terms_of_pair(0, 1, 0, 3)
-        quantize_a(1, 1)
         terms_of_pair(0, 1, 1, 5)
         terms_of_pair(1, 0, 0, 6)
+        quantize_a(1, 1)
         z_half = add("half", HALF, terms[0, 0][:], terms[0, 1][:])
         terms_of_pair(1, 0, 1, 7)
-        finish("half", z_half, 0, HALF, (1,))
+        finish("half", z_half, res_first[:, :, :HALF], HALF, (1,))
         product(terms_last[0][:], picked_last[0][:], filters_of_quarter(0, 0)[:])
         f_last = filters_of_quarter(1, 4)
         product(terms_last[1][:, :2], picked_last[1][:, :2], f_last[:, :2])
         z_2 = add("2", P, terms[1, 0][:, :, :P], terms_last[0][:])
         product(terms_last[1][:, 2:], picked_last[1][:, 2:], f_last[:, 2:])
-        finish("2", z_2, HALF, P, (3,))
-        finish("3", add("3", P, terms[1, 0][:, :, P:], terms_last[1][:]), HALF + P, P, (5, 6))
+        finish("2", z_2, res_first[:, :, HALF:], P, (3,))
+        store(res_first, slice(0, 2), 0, HALF + P)
+        finish("3", add("3", P, terms[1, 0][:, :, P:], terms_last[1][:]), res_last[:], P, (5, 6))
+        for m in range(N // P):
+            store(res_last, slice(m, m + 1), HALF + P, P)

@@ -72,13 +72,13 @@ def tile_picked_wdime_silu_l_kernel(tc, x_words, x_scales, aT, w1, w3, w2_words,
                                   in_=rows[:, 4 * q : 4 * q + 4, :].bitcast(I32).rearrange("g r c -> r g c"))
 
         w1_raw = [load_w1(0)]
-        load_scales(x_sc[:], x_scales)
         w1_raw.append(load_w1(1))
+        load_scales(x_sc[:], x_scales)
         load_x(0)
         load_x(1)
+        w3_raw = [load_cols("w3_raw0", w3, 0, HALF)]
         nc.sync.dma_start(lists[0][:], pos1)
         nc.sync.dma_start(lists[1][:], pos2)
-        w3_raw = [load_cols("w3_raw0", w3, 0, HALF)]
         a_raw = {}
 
         def load_a(hf, d):

from contextlib import ExitStack

import concourse.mybir as mybir

K, T, H, N, J = 1024, 512, 512, 256, 512
FLOPS = 2 * (K * H * T + J * H * 2 * T + H * N * T)

F32 = mybir.dt.float32
BF16 = mybir.dt.bfloat16
I32 = mybir.dt.int32
U32 = mybir.dt.uint32
U16 = mybir.dt.uint16
U8 = mybir.dt.uint8
FP8X4 = mybir.dt.float8_e4m3fn_x4
FP4X4 = mybir.dt.float4_e2m1fn_x4
SILU = mybir.ActivationFunctionType.Silu
COPY = mybir.ActivationFunctionType.Copy
ADD = mybir.AluOpType.add
MULT = mybir.AluOpType.mult

P = 128
PACK = 4
K_PASS = P * PACK
PASSES = K // K_PASS
QUADRANTS = 4
LISTS = 2
HALF = T // 2
PER_COLUMN = 16
OWN = 64


def line_by_line(ap, pattern):
    return ap.rearrange(pattern + " -> p c j i", i=2)


def quantize(nc, codes, scales, grouped):
    nc.vector.quantize_mx(out=codes.bitcast(FP8X4), scales=scales, in_=grouped)


def tile_picked_wdime_silu_l_kernel(tc, x_words, x_scales, aT, w1, w3, w2_words, w2_scales, pos1, pos2, out):
    nc = tc.nc
    on_vector = nc.vector.tensor_copy
    with ExitStack() as ctx:
        keep = ctx.enter_context(tc.tile_pool(name="keep", bufs=1))
        psum = ctx.enter_context(tc.psum_pool(name="psum", bufs=1))

        def bank(number, name, shape):
            return psum.tile(shape, F32, name=name, tag="bank%d" % number)

        lists = [keep.tile([P, T // PER_COLUMN], U16, name="pos%d" % d) for d in range(LISTS)]
        x_codes = [keep.tile([P, T], U32, name="x_codes%d" % g, align_bytes=64) for g in range(PASSES)]
        x_sc = keep.tile([P, PASSES * T], U8, align_bytes=64)
        w2_codes = keep.tile([P, 2 * N], U8, align_bytes=64)
        w2_sc = keep.tile([P, N], U8, align_bytes=64)
        nc.vector.memset(x_sc[:].bitcast(I32), 0)
        nc.vector.memset(w2_sc[:].bitcast(I32), 0)

        def load_cols(name, src, first, width):
            raw = keep.tile([P, PACK, width], F32, name=name, align_bytes=64)
            nc.sync.dma_start(out=raw[:], in_=src[:, first : first + width].rearrange("(p j) n -> p j n", j=PACK))
            return raw

        def load_w1(g):
            return load_cols("w1_raw%d" % g, w1[g * K_PASS : (g + 1) * K_PASS], 0, H)

        def load_x(g):
            nc.sync.dma_start(out=x_codes[g][:].bitcast(I32), in_=x_words[g].rearrange("p n j -> p (n j)").bitcast(I32))

        def load_scales(dst, rows):
            for q in range(QUADRANTS):
                nc.sync.dma_start(out=dst[32 * q : 32 * q + 4].bitcast(I32).rearrange("r (g c) -> r g c", g=rows.shape[0]),
                                  in_=rows[:, 4 * q : 4 * q + 4, :].bitcast(I32).rearrange("g r c -> r g c"))

        w1_raw = [load_w1(0)]
        w1_raw.append(load_w1(1))
        load_scales(x_sc[:], x_scales)
        load_x(0)
        load_x(1)
        w3_raw = [load_cols("w3_raw0", w3, 0, HALF)]
        nc.sync.dma_start(lists[0][:], pos1)
        nc.sync.dma_start(lists[1][:], pos2)
        a_raw = {}

        def load_a(hf, d):
            a_raw[hf, d] = load_cols("a_raw%d%d" % (hf, d), aT, d * T + hf * HALF, HALF)

        w3_raw.append(load_cols("w3_raw1", w3, HALF, HALF))
        for hf, d in ((0, 0), (0, 1), (1, 0), (1, 1)):
            load_a(hf, d)
        nc.sync.dma_start(out=w2_codes[:].bitcast(I32), in_=w2_words[0].bitcast(I32))
        load_scales(w2_sc[:], w2_scales)

        def dealer(name):
            grouped = keep.tile([P, PACK, P, PACK], BF16, name=name + "_bf", align_bytes=64)
            codes = keep.tile([P, H], U32, name=name + "_codes", align_bytes=64)
            scales = keep.tile([P, H], U8, name=name + "_sc", align_bytes=64)

            def deal(copy, raw, first, columns, tiles):
                src = raw[:].rearrange("p j (m t) -> p m j t", t=PACK)
                copy(out=grouped[:, tiles, columns].rearrange("p t m j -> p m j t"),
                     in_=src[:, columns.start - first : columns.stop - first, :, tiles])

            def codes_of(t, columns):
                cols = slice(t * P + columns.start, t * P + columns.stop)
                quantize(nc, codes[:, cols], scales[:, cols], grouped[:, t, columns].rearrange("p m j -> p (m j)"))

            return deal, codes_of, codes, scales

        all_tiles = slice(0, PACK)

        def quantize_w1(g):
            deal, codes_of, codes, scales = dealer("w1%d" % g)
            raw = w1_raw[g]
            for pair in range(2):
                deal(on_vector, raw, 0, slice(0, P), slice(2 * pair, 2 * pair + 2))
                for t in (2 * pair, 2 * pair + 1):
                    codes_of(t, slice(0, P))
            return codes, scales

        h_parts = [(0, slice(0, P), 4), (0, slice(P, HALF), 0), (0, slice(HALF, T), 7)]
        h_parts.extend((t, slice(0, T), (4, 0, 7)[t - 1]) for t in range(1, PACK))
        h = [keep.tile([P, T], F32, name="h%d" % t) for t in range(PACK)]
        w1_q = [quantize_w1(g) for g in range(PASSES)]

        def make_h(n, t, edges, number):
            acc = bank(number, "h_acc%d" % n, [P, edges.stop - edges.start])
            cols = slice(t * P, (t + 1) * P)
            for g, (codes, scales) in enumerate(w1_q):
                nc.tensor.matmul_mx(out=acc[:], lhsT=codes[:, cols].bitcast(FP8X4), lhsT_scale=scales[:, cols],
                                    rhs=x_codes[g][:, edges].bitcast(FP8X4),
                                    rhs_scale=x_sc[:, g * T + edges.start : g * T + edges.stop],
                                    start=(g == 0), stop=(g == PASSES - 1))
            nc.scalar.activation(out=h[t][:, edges], in_=acc[:], func=SILU)

        def offsets(d, first, width):
            at = first // PER_COLUMN
            return lists[d][:, at : at + width // PER_COLUMN]

        def gather(dst, t, d, first, width):
            nc.scalar.activation(out=dst, in_=h[t][:].indirect(offsets(d, first, width)), func=COPY)

        def gather_on_vector(dst, t, d, first, width):
            nc.vector.tensor_copy(dst, h[t][:].indirect(offsets(d, first, width)))

        picked = {(hf, d): keep.tile([P, PACK, HALF], F32, name="picked%d%d" % (hf, d), align_bytes=64)
                  for hf, d in ((0, 0), (0, 1), (1, 0))}
        picked_last = [keep.tile([P, PACK, P], F32, name="picked_last%d" % b, align_bytes=64) for b in range(2)]
        for t in range(PACK):
            for n, (part_of, edges, number) in enumerate(h_parts):
                if part_of == t:
                    make_h(n, t, edges, number)
            gather(picked[0, 0][:, t], t, 0, 0, HALF)
            if t == 0:
                gather(picked[1, 0][:, 0], 0, 0, HALF, HALF)
        for t in range(1, PACK):
            gather(picked[0, 1][:, t], t, 1, 0, HALF)
        for t in range(1, PACK):
            gather(picked[1, 0][:, t], t, 0, HALF, HALF)
        for b in range(2):
            for t in range(PACK):
                gather(picked_last[b][:, t], t, 1, HALF + b * P, P)

        a_bf, a_q = {}, {}

        for d in range(LISTS):
            a_bf[0, d] = keep.tile([P, HALF, PACK], BF16, name="a_bf0%d" % d, align_bytes=64)[:]
        a_bf_late = keep.tile([P, OWN + HALF, PACK], BF16, align_bytes=64)
        a_bf[1, 0], a_bf[1, 1] = a_bf_late[:, OWN:], a_bf_late[:, :HALF]

        def round_a(hf, d, width):
            on_vector(out=line_by_line(a_bf[hf, d][:, :width], "p (c i) j"),
                      in_=line_by_line(a_raw[hf, d][:, :, :width], "p j (c i)"))

        def quantize_a(hf, d):
            codes = keep.tile([P, HALF], U32, name="a_codes%d%d" % (hf, d), align_bytes=64)
            scales = keep.tile([P, HALF], U8, name="a_sc%d%d" % (hf, d), align_bytes=64)
            quantize(nc, codes[:], scales[:], a_bf[hf, d].rearrange("p n j -> p (n j)"))
            a_q[hf, d] = codes, scales

        def filters(f, t, hf, d, first, width):
            cols = slice(t * P, (t + 1) * P)
            codes, scales = a_q[hf, d]
            nc.tensor.matmul_mx(out=f, lhsT=w3_codes[:, cols].bitcast(FP8X4), lhsT_scale=w3_sc[:, cols],
                                rhs=codes[:, first : first + width].bitcast(FP8X4),
                                rhs_scale=scales[:, first : first + width], start=True, stop=True)

        terms = {(hf, d): keep.tile([P, PACK, HALF], F32, name="terms%d%d" % (hf, d), align_bytes=64)
                 for hf, d in ((0, 0), (0, 1), (1, 0))}
        terms_last = [keep.tile([P, PACK, P], F32, name="terms_last%d" % b, align_bytes=64) for b in range(2)]

        def product(dst, picked_values, f):
            nc.vector.tensor_tensor(out=dst, in0=picked_values, in1=f, op=MULT)

        def terms_of_pair(hf, d, pair, number):
            f = bank(number, "f%d%d%d" % (pair, hf, d), [P, 2, HALF])
            for e in range(2):
                filters(f[:, e], 2 * pair + e, hf, d, 0, HALF)
            tiles = slice(2 * pair, 2 * pair + 2)
            product(terms[hf, d][:, tiles], picked[hf, d][:, tiles], f[:])

        def filters_of_quarter(b, number):
            f = bank(number, "f_last%d" % b, [P, PACK, P])
            for t in range(PACK):
                filters(f[:, t], t, 1, 1, b * P, P)
            return f

        def add(name, width, first_terms, second_terms):
            z = keep.tile([P, width, PACK], BF16, name="z_bf" + name, align_bytes=64)
            nc.vector.tensor_tensor(out=line_by_line(z[:], "p (c i) j"), in0=line_by_line(first_terms, "p j (c i)"),
                                    in1=line_by_line(second_terms, "p j (c i)"), op=ADD)
            return z

        res_first = keep.tile([P, N // P, HALF + P], F32)
        res_last = keep.tile([P, N // P, P], F32)

        def store(res, tiles, first, width):
            rows = out[:, first : first + width].rearrange("(m p) v -> p m v", p=P)
            nc.sync.dma_start(out=rows[:, tiles], in_=res[:, tiles])

        def finish(name, z, res, width, numbers):
            codes = keep.tile([P, width], U32, name="z_codes" + name, align_bytes=64)
            scales = keep.tile([P, width], U8, name="z_sc" + name, align_bytes=64)
            quantize(nc, codes[:], scales[:], z[:].rearrange("p v t -> p (v t)"))
            tiles_a_bank = N // P // len(numbers)
            for n, number in enumerate(numbers):
                acc = bank(number, "out_acc%s%d" % (name, n), [P, tiles_a_bank, width])
                for e in range(tiles_a_bank):
                    m = n * tiles_a_bank + e
                    nc.tensor.matmul_mx(out=acc[:, e], lhsT=w2_codes[:, 2 * m * P : 2 * (m + 1) * P].bitcast(FP4X4),
                                        lhsT_scale=w2_sc[:, m * P : (m + 1) * P],
                                        rhs=codes[:].bitcast(FP8X4), rhs_scale=scales[:], start=True, stop=True)
                nc.scalar.activation(out=res[:, n * tiles_a_bank : (n + 1) * tiles_a_bank], in_=acc[:], func=SILU)

        deal_w3, codes_of_w3, w3_codes, w3_sc = dealer("w3")
        deal_w3(on_vector, w3_raw[0], 0, slice(0, P // 2), all_tiles)
        gather_on_vector(picked[0, 1][:, 0], 0, 1, 0, HALF)
        for t in range(PACK):
            codes_of_w3(t, slice(0, P // 2))
        for pair in range(2):
            deal_w3(on_vector, w3_raw[1], P // 2, slice(P // 2, P), slice(2 * pair, 2 * pair + 2))
        for t in range(2):
            codes_of_w3(t, slice(P // 2, P))
        round_a(0, 0, HALF)
        for t in range(2, PACK):
            codes_of_w3(t, slice(P // 2, P))
        quantize_a(0, 0)
        round_a(0, 1, HALF)
        terms_of_pair(0, 0, 0, 1)
        quantize_a(0, 1)
        round_a(1, 0, HALF)
        terms_of_pair(0, 0, 1, 2)
        round_a(1, 1, OWN)
        quantize_a(1, 0)
        nc.gpsimd.tensor_scalar(out=a_bf[1, 1][:, OWN:], in0=a_raw[1, 1][:, :, OWN:].rearrange("p j n -> p n j"),
                                scalar1=1.0, scalar2=0.0, op0=MULT, op1=ADD)
        terms_of_pair(0, 1, 0, 3)
        terms_of_pair(0, 1, 1, 5)
        terms_of_pair(1, 0, 0, 6)
        quantize_a(1, 1)
        z_half = add("half", HALF, terms[0, 0][:], terms[0, 1][:])
        terms_of_pair(1, 0, 1, 7)
        finish("half", z_half, res_first[:, :, :HALF], HALF, (1,))
        product(terms_last[0][:], picked_last[0][:], filters_of_quarter(0, 0)[:])
        f_last = filters_of_quarter(1, 4)
        product(terms_last[1][:, :2], picked_last[1][:, :2], f_last[:, :2])
        z_2 = add("2", P, terms[1, 0][:, :, :P], terms_last[0][:])
        product(terms_last[1][:, 2:], picked_last[1][:, 2:], f_last[:, 2:])
        finish("2", z_2, res_first[:, :, HALF:], P, (3,))
        store(res_first, slice(0, 2), 0, HALF + P)
        finish("3", add("3", P, terms[1, 0][:, :, P:], terms_last[1][:]), res_last[:], P, (5, 6))
        for m in range(N // P):
            store(res_last, slice(m, m + 1), HALF + P, P)
